import numpy as np, ml_dtypes
CORES = [23,119,17,113]
N = 4
BF = ml_dtypes.bfloat16
V, L, RO, HP, S, ST = 3712, 256, 3, 2, 1, 97
def parts(rng):
    cen = rng.integers(0, 255, (1, 8, 16, 24)); k = rng.integers(0, 24, (N, 8, 1, V)); size = rng.choice(np.array([3, 12, 40, 90]), (N, 8, 1, V))
    x = np.take_along_axis(cen, k, 3) + np.floor((2 * size + 1) * rng.random((N, 8, 16, V))).astype(np.int64) - size
    x = np.minimum(np.maximum(x, 0), 254)
    hub = np.argsort(rng.random((N, 8, 1, V)), axis=3); u = rng.random((N, 8, 16, V))
    c = np.take_along_axis(hub, np.minimum((V * u * u).astype(np.int64), V - 1), 3)
    c = np.where(rng.random((N, 8, 1, V)) < 0.06, c[:, :, :1], c)
    w = rng.integers(0, V, (N, 8, 16, L)); u = rng.random((N, 8, L)); n = 2 * np.minimum((8 * u * u).astype(np.int64), 7) + 1
    t = rng.integers(0, 1600, (N, 8, L))
    return x, c, w, n, t
def trap(rng, d, T, f):
    x, c, w, n, t = d
    o = np.argsort(rng.random((N, 8, V)), axis=2); z = np.argsort(rng.random((N, 8, L)), axis=2)
    if len(f):
        for r in range(N):
            for g in range(8):
                u = o[r, g].copy(); o[r, g] = np.concatenate([np.array(f), u[~np.isin(u, np.array(f))]])
    for r in range(N):
        q = (r + S) % N; b = (r - S) % N
        for g in range(8):
            tv = o[r, g, :T]; tw = o[q, g, T:2 * T]; h = o[b, g, 2 * T:3 * T]; la = z[r, g, :T]; lb = z[b, g, T:2 * T]
            c[r, g][:, tv] = tw; c[q, g][:, tw] = tv
            w[r, g][0, la] = tv; n[r, g][la] = 1
            x[b, g][:, h] = x[r, g][:, tv]
            w[b, g][0, lb] = h; w[b, g][1, lb] = tv; n[b, g][lb] = 3; t[b, g][lb] = np.maximum(t[b, g][lb], 1)
def pack(d):
    x, c, w, n, t = d
    return {"pts": np.ascontiguousarray(x.reshape(N, 128, V)).astype(np.float32).astype(BF), "cand": np.ascontiguousarray(c.reshape(N, 128, V)).astype(np.int32),
            "way": np.ascontiguousarray(w.reshape(N, 128, L)).astype(np.int32), "cnt": np.ascontiguousarray(n).astype(np.int32), "th": np.ascontiguousarray(t).astype(np.int32)}
def setup_inputs(rng):
    d = parts(rng); trap(rng, d, 12, [])
    return pack(d)
def setup_inputs_spread(rng):
    x, c, w, n, t = parts(rng)
    x = np.minimum((np.exp2(8 * rng.random((N, 8, 1, V))) * rng.random((N, 8, 16, V))).astype(np.int64), 254)
    hub = np.argsort(rng.random((N, 8, 1, V)), axis=3)
    c = np.take_along_axis(hub, np.minimum((V * rng.random((N, 8, 16, V)) ** 6).astype(np.int64), V - 1), 3)
    hub = np.argsort(rng.random((N, 8, 1, V)), axis=3)
    w = np.take_along_axis(hub, np.minimum((V * rng.random((N, 8, 16, L)) ** 3).astype(np.int64), V - 1), 3)
    n = 2 * rng.integers(0, 8, (N, 8, L)) + 1; t = np.minimum(np.exp2(12 * rng.random((N, 8, L))).astype(np.int64) - 1, 4095)
    d = (x, c, w, n, t); trap(rng, d, 12, [])
    return pack(d)
def setup_inputs_ends(rng):
    cls = rng.integers(0, 5, (N, 8, 1, V)); cls[..., 0] = 0; cls[..., V - 1] = 1
    x = 254 * np.where(cls == 0, 0, np.where(cls == 1, 1, rng.integers(0, 2, (N, 8, 16, V))))
    c = np.where(rng.random((N, 8, 16, V)) < 0.7, (V - 1) * rng.integers(0, 2, (N, 8, 16, V)), rng.integers(0, V, (N, 8, 16, V)))
    w = np.where(rng.random((N, 8, 1, L)) < 0.25, rng.integers(0, V, (N, 8, 16, L)), (V - 1) * rng.integers(0, 2, (N, 8, 16, L)))
    n = 1 + 14 * rng.integers(0, 2, (N, 8, L)); t = 4095 * rng.integers(0, 2, (N, 8, L))
    for r in range(N):
        q = (r + S) % N
        for g in range(8):
            lo = rng.permutation(np.flatnonzero(cls[r, g, 0, 1:] == 0) + 1); up = rng.permutation(np.flatnonzero(cls[q, g, 0, :V - 1] == 1)); lq = rng.permutation(np.flatnonzero(cls[q, g, 0, 1:] == 0) + 1)
            uh = rng.permutation(np.flatnonzero(cls[r, g, 0, :V - 1] == 1))
            for m, l in enumerate((3, 8, L - 2, L - 1)):
                w[r, g][0::2, l] = lo[8 * m:8 * m + 8]; w[r, g][1::2, l] = up[8 * m:8 * m + 8]; n[r, g, l] = 15; t[r, g, l] = 4095
            for m, l in enumerate((5, L - 4, L - 3)):
                e = lo[32 + m]; col = np.concatenate([up[32:40], up[32:40]])
                if m > 0: col[15] = lq[0]
                if m > 1: col[6] = lq[1]
                c[r, g][:, e] = col; w[r, g][0, l] = e; n[r, g, l] = 1; t[r, g, l] = 4095
            for m, l in enumerate((6, L - 6, 11, L - 5)):
                e = lo[36 + m]; h = lo[40 + m]; f = up[44 + m]; z = lq[24 + m]
                w[r, g][0, l] = uh[m]; w[r, g][1, l] = z; w[r, g][2, l] = e; n[r, g, l] = 3; t[r, g, l] = 0
                if m < 2:
                    c[r, g][:15, e] = z; c[r, g][15, e] = f; c[q, g][:, f] = h
                else:
                    c[r, g][:, e] = f; c[q, g][:15, f] = uh[m]; c[q, g][15, f] = h
            if g % 2 == 0: c[r, g][:, V - 1] = lq[4:20]
            else:
                c[r, g][:15, V - 1] = V - 1; c[r, g][15, V - 1] = lq[4]
    return pack((x, c, w, n, t))
def setup_inputs_corners(rng):
    d = parts(rng); x, c, w, n, t = d
    for r in range(N):
        for g in range(8):
            k = (g + r) % 8
            if k == 0: w[r, g] = w[r, g][:1].copy(); n[r, g] = 15
            if k == 1: w[r, g] = (V - 1) * rng.integers(0, 2, (16, L)); n[r, g] = 1
            if k == 2: n[r, g] = 13 + 2 * rng.integers(0, 2, L)
            if k == 3: c[r, g] = np.arange(V)[None, :]
            if k == 4: c[r, g] = c[r, g][:1].copy()
            if k == 5: w[r, g] = rng.choice(np.array([0, V // 2, V - 1]), (16, L))
            if k == 6: n[r, g] = 1 + 14 * rng.integers(0, 2, L); t[r, g] = 0
            if k < 6: t[r, g] = 4095 * rng.integers(0, 2, L)
    trap(rng, d, 12, [V - 1, V - ST, V - ST - 1, 0])
    o = np.argsort(rng.random((N, 8, V)), axis=2)
    for r in (0, 1):
        q = (r + S) % N
        for g in range(8):
            w[r, g][0] = o[r, g, :L]; w[r, g][1] = o[q, g, L:2 * L]; w[r, g][2] = o[r, g, 2 * L:3 * L]; n[r, g] = 3; t[r, g] = 4095
    q = S % N
    for g in range(8):
        x[0, g][:, o[0, g, :L]] = x[q, g][:, o[q, g, L:2 * L]]
        e = o[0, g, 2 * L:3 * L:2]; f = o[q, g, 2 * L:3 * L:2]; v = x[q, g][:, f].copy(); s = rng.integers(6, 41, len(e))
        v[0] = np.where(v[0] < 200, v[0] + s, v[0] - s)
        x[0, g][:, e] = v; c[0, g][:, e] = f[None, :]
    t[0] = rng.choice(np.array([1, 2, 5, 4095]), (8, L))
    M = int(rng.choice(np.array([31, 63, 95]))); pk = rng.permutation(8 * L)[:M]; pick = np.zeros(8 * L, np.int64); pick[pk] = 4095
    t[1] = pick.reshape(8, L); q = (1 + S) % N
    for u in pk[:16]:
        g = int(u) // L; l = int(u) % L
        c[1, g][:, o[1, g, 2 * L + l]] = o[q, g, L + l]
    return pack(d)
def setup_inputs_crowd(rng):
    d = parts(rng); x, c, w, n, t = d
    n[...] = np.maximum(n, 3); t[...] = np.maximum(t, 1); o = np.argsort(rng.random((N, 8, V)), axis=2)
    far = rng.permutation(V); rest = far[(RO + 1) * L:]; z = int(rng.integers(0, N))
    c[:, 7] = rest[c[:, 7] % len(rest)]; w[:, 7] = rest[w[:, 7] % len(rest)]
    for r in range(N): o[r, 7, :len(rest)] = rng.permutation(rest)
    for g in range(8):
        s = rng.integers(0, 255, (16, 1))
        for r in range(N):
            q = (r + S) % N; a = o[r, g, :L]; b = o[q, g, L:2 * L]
            if g == 6:
                c[r, g] = rng.permutation(V)[:16][:, None]; continue
            x[r, g][:, a] = s; x[q, g][:, b] = s
            aa = a.copy(); bb = b.copy()
            if g in (0, 1, 2, 5): aa[:] = a[0]
            if g in (0, 1, 3, 5): bb[:] = b[0]
            if g == 1:
                u = int(rng.integers(0, L)); aa[u] = a[1]; bb[u] = b[1]
            if g == 4: aa = a[rng.integers(0, 3, L)]; bb = b[rng.integers(0, 3, L)]
            if g == 5: t[r, g, 0] = 0
            if g == 7: aa[L - 1] = a[0]
            w[r, g][0] = aa; w[r, g][1] = bb
    q = (z + S) % N; hs = far[:(RO + 1) * L].reshape(RO + 1, L); bs = rng.permutation(far[:RO * L]).reshape(RO, L)
    for m in range(RO):
        x[z, 7][:, hs[m]] = x[q, 7][:, bs[m]]; w[z, 7][2 * m] = hs[m]; w[z, 7][2 * m + 1] = bs[m]
    w[z, 7][2 * RO] = hs[RO]; n[z, 7] = 2 * RO + 1
    return pack(d)
def setup_inputs_ties(rng):
    d = parts(rng); x, c, w, n, t = d
    pat = 64 * rng.integers(0, 2, (1, 8, 16, 10)); x[...] = np.take_along_axis(pat, rng.integers(0, 10, (N, 8, 1, V)), 3)
    c[:, :, 8:] = c[:, :, :8].copy()
    t[...] = np.maximum(64 * rng.integers(0, 11, (N, 8, L)) + rng.integers(-1, 2, (N, 8, L)), 0)
    K = 24; o = np.argsort(rng.random((N, 8, V)), axis=2); z = np.argsort(rng.random((N, 8, L)), axis=2)
    for r in range(N):
        q = (r + S) % N
        for g in range(8):
            la = z[r, g, :K]; a = o[r, g, :K]; e = o[r, g, K:2 * K]; b = o[q, g, 2 * K:3 * K]
            s = rng.integers(1, 64, (1, K)); near = rng.integers(1, 8, K)
            v = np.floor(s * rng.random((16, K))).astype(np.int64); hi = 254 - np.floor(s * rng.random((16, K))).astype(np.int64)
            u = v.copy(); u[3] = u[3] + near
            x[r, g][:, a] = v; x[r, g][:, e] = u; x[q, g][:, b] = hi
            turn = rng.random(K) < 0.5
            w[r, g][0, la] = np.where(turn, e, a); w[r, g][1, la] = b; w[r, g][2, la] = np.where(turn, a, e); n[r, g][la] = 3
            t[r, g][la] = np.add.reduce(hi - v, axis=0) - near + rng.integers(-1, 2, K)
    trap(rng, d, 12, [])
    return pack(d)
def check_inputs(d):
    bad = []
    for k, lo, hi in (("pts", 0, 254), ("cand", 0, V - 1), ("way", 0, V - 1), ("cnt", 1, 15), ("th", 0, 4095)):
        a = np.asarray(d[k]).astype(np.float64)
        if not (np.min(a) >= lo and np.max(a) <= hi): bad.append("range of " + k)
    a = np.asarray(d["pts"]).astype(np.float64)
    if not np.all(a == np.floor(a)): bad.append("pts not whole")
    if np.any((np.asarray(d["cnt"]).astype(np.int64) & 1) != 1): bad.append("cnt not odd")
    return bad
def hop(e, xa, ca, xb, old, use):
    c = np.take_along_axis(ca, e[:, None, :], 2); xe = np.take_along_axis(xa, e[:, None, :], 2)
    xc = np.take_along_axis(xb, c.reshape(8, 1, 16 * L), 2).reshape(8, 16, 16, L)
    s = np.add.reduce(np.abs(xc - xe[:, :, None, :]), axis=1)
    on = np.any((c[:, :, None, :] == old[:, None]) & use[:, None], axis=2)
    ok = (xc[:, 0] != 255) & ~on
    i = np.argmin(np.where(ok, s, 9999), axis=1)
    return np.any(ok, axis=1), np.take_along_axis(c, i[:, None, :], 1)[:, 0]
def reference(pts, cand, way, cnt, th):
    x = pts.astype(np.float32).astype(np.int32).reshape(N, 8, 16, V); c = cand.astype(np.int64).reshape(N, 8, 16, V)
    w = way.astype(np.int64).reshape(N, 8, 16, L); n = cnt.astype(np.int64); t = th.astype(np.int64)
    rows = np.arange(16)[None, :, None]; low = np.arange(L)[:, None] > np.arange(L)[None, :]; A = [0] * N
    for rnd in range(RO):
        wins = []
        for r in range(N):
            q = (r + S) % N; p = w[r]; k = n[r]
            v = np.zeros((8, 16, 16, L), np.int32)
            v[:, :, 0::2] = np.take_along_axis(x[r], p[:, 0::2].reshape(8, 1, 8 * L), 2).reshape(8, 16, 8, L)
            v[:, :, 1::2] = np.take_along_axis(x[q], p[:, 1::2].reshape(8, 1, 8 * L), 2).reshape(8, 16, 8, L)
            dead = (v[:, 0] == 255) & (rows < k[:, None, :]); cut = np.any(dead, axis=1); j = np.argmax(dead, axis=1)
            pre = np.where((j & 1) == 1, j, np.maximum(j - 1, 0)); s = j + 2 - (j & 1); post = np.maximum(k - s, 0); first = pre >= post
            start = np.where(cut & ~first, s, 0); m = np.where(cut, np.where(first, pre, post), k); none = m == 0
            ix = np.minimum(rows + start[:, None, :], 15)
            p2 = np.take_along_axis(p, ix, 1); v = np.take_along_axis(v, ix[:, None], 2)
            new = p[:, 0] + ST; new = np.where(new >= V, new - V, new)
            p2[:, 0] = np.where(none, new, p2[:, 0]); m = np.where(none, 1, m)
            live = (v[:, 0] != 255) & (rows < m[:, None, :])
            d = np.add.reduce(np.abs(v[:, :, :15] - v[:, :, 1:]), axis=1)
            d = np.where(live[:, :15] & live[:, 1:], d, 9999)
            i = np.argmin(d, axis=1); least = np.min(d, axis=1); prop = least < t[r] + 8 * (A[r] & 31)
            a = np.take_along_axis(p2, (i + (i & 1))[:, None, :], 1)[:, 0]; b = np.take_along_axis(p2, (i + 1 - (i & 1))[:, None, :], 1)[:, 0]
            same = (a[:, :, None] == a[:, None, :]) | (b[:, :, None] == b[:, None, :])
            win = prop & ~np.any(same & low[None] & prop[:, None, :], axis=2)
            mid = (np.take_along_axis(x[r], a[:, None, :], 2) + np.take_along_axis(x[q], b[:, None, :], 2)) >> 1
            wins.append((win, a, b, mid)); w[r] = p2; n[r] = m
        for r in range(N):
            win, a, b, mid = wins[r]; A[r] = int(np.count_nonzero(win))
            for g in range(8): x[r, g][:, a[g][win[g]]] = mid[g][:, win[g]]
        for r in range(N):
            win, a, b, mid = wins[r]; q = (r + S) % N
            for g in range(8): x[q, g][:, b[g][win[g]]] = 255
        for r in range(N):
            q = (r + S) % N
            for h in range(HP):
                p = w[r]; k = n[r]; use = rows < k[:, None, :]
                e = np.take_along_axis(p, k[:, None, :] - 1, 1)[:, 0]
                f1, u1 = hop(e, x[r], c[r], x[q], p[:, 1::2], use[:, 1::2])
                f2, u2 = hop(u1, x[q], c[q], x[r], p[:, 0::2], use[:, 0::2])
                go = f1 & f2 & (k <= 13)
                p = np.where(go[:, None, :] & (rows == k[:, None, :]), u1[:, None, :], p)
                p = np.where(go[:, None, :] & (rows == k[:, None, :] + 1), u2[:, None, :], p)
                w[r] = p; n[r] = np.where(go, k + 2, k)
    w = np.where(np.arange(16)[None, None, :, None] < n[:, :, None, :], w, 0)
    return {"yx": x.reshape(N, 128, V).astype(np.float32).astype(BF), "yw": w.reshape(N, 128, L).astype(np.float32), "yn": n.astype(np.float32)}

@@ -1,0 +1,727 @@
+from concourse.bass import DstId, RemoteDMATransfer
+from concourse.mybir import AluOpType as ALU, AxisListType as AX, ActivationFunctionType as AF
+
+V = 3712
+SENT = 3712.0
+DUM = 3728
+XW = DUM + 256
+DEAD_O, DEAD_P = 2048.0, -1024.0
+MAGIC = 12582912.0
+NV = (5, 6)
+BIAS = 4000.0
+LAT = 120.0
+PE = 0.55
+EQAT = 1
+VOS = ((0, 1), (1, 1))
+SEED = 10
+NOISE = 1000.0
+WIN = 30.0
+PASSES = 8
+NX, NC = 4, 2
+
+F, B, I, U = "float32", "bfloat16", "int32", "uint16"
+SCRATCH = {}
+
+
+def _sb(name, shape, dt):
+    SCRATCH[name] = ("sbuf", [128] + shape, dt)
+
+
+for _n, _s, _d in [
+    ("XO", [XW], B), ("XP", [XW], B), ("CI", [V], I), ("CO", [V], F), ("CP", [V], F), ("CU", [V], U), ("CN", [V], U),
+    ("IOT", [3840], F), ("YX", [V], B), ("WI", [256], I), ("ZI", [256], I),
+    ("PC", [16], I), ("PF", [24], F), ("XI", [144], F), ("MB", [6, 128], B), ("MF", [2, 128], F), ("BS", [144], B),
+    ("KF", [1792], F), ("KB", [512], B), ("LI", [256], I), ("LF", [256], F), ("LU", [256], U), ("TM", [64], F),
+    ("TH", [16], F), ("THR", [16], F), ("AB", [2, 16], I), ("ABU", [32], U), ("AS", [32], F), ("PRP", [16], F),
+    ("ROW", [512], U), ("EA", [16, 256], B), ("EB", [16, 256], B), ("CS", [256], F), ("LS", [48], F), ("LM", [32], F),
+    ("XA", [512], B), ("MT", [256], F), ("DK", [512], B), ("CT", [8], F), ("CTI", [8], I), ("YC", [2, 256], F),
+]:
+    _sb(_n, _s, _d)
+for _r in range(3):
+    _sb("MID%d" % _r, [256], B); _sb("MIN%d" % _r, [256], B)
+    _sb("LW%d" % _r, [32], U); _sb("LA%d" % _r, [16], U); _sb("LB%d" % _r, [16], U)
+for _h in range(2):
+    for _n, _s, _d in [
+        ("PW", [160], F), ("LP", [128], U), ("VE", [1040], B), ("VO", [1024], B), ("A", [8, 16, 16], B), ("R", [128], F),
+        ("NN", [128], F), ("W1", [256], F), ("W2", [256], F), ("W3", [256], F), ("PL", [2, 128], F), ("TI", [2, 8], I),
+        ("SM", [160], F), ("IX", [8], F), ("TS", [16], F), ("OH", [48], F), ("PR", [5, 128], F), ("FL", [256], B),
+        ("EX", [16], U), ("CR", [256], F), ("TT", [256], F), ("OF", [128], U), ("CW", [128], F), ("PP", [1920], F), ("XE", [256], B),
+        ("D", [8, 256], B), ("EQ", [896], B), ("FD", [32], F), ("IG", [16], F), ("PZ", [136], F),
+    ]:
+        _sb(_n + str(_h), _s, _d)
+    for _n in ("pD", "pA", "pB"):
+        SCRATCH[_n + str(_h)] = ("psum", [128, 512], F)
+SCRATCH["pM"] = ("psum", [128, 512], F)
+SCRATCH["pC"] = ("psum", [128, 512], F)
+
+SEMAPHORES = ["cV", "cS", "cP", "cG"] + ["d%d" % _i for _i in range(20)] + ["l%d" % _i for _i in range(16)] + ["a%d" % _i for _i in range(16)]
+
+
+def build(g, core, T, topo):
+    rank = T.rank_of(core)
+    n = len(T.cores)
+    cp, cq = T.cores[(rank - 1) % n], T.cores[(rank + 1) % n]
+    ops = []
+    cur = [0.0]
+    cnt = {"d": 0, "l": 0, "a": 0}
+
+    def R(name, *idx):
+        shp = SCRATCH[name][1][1:]
+        idx = list(idx) + [slice(None)] * (len(shp) - len(idx))
+        bits = 1
+        num = 1
+        st = 1
+        for d in range(len(shp) - 1, -1, -1):
+            x = idx[d]
+            rg = [x] if isinstance(x, int) else range(*x.indices(shp[d]))
+            if st == 1 and len(rg) > 1 and rg[1] - rg[0] == 1:
+                bits = ((1 << len(rg)) - 1) << rg[0]
+            else:
+                bits = sum(bits << (y * st) for y in rg)
+            num *= len(rg)
+            st *= shp[d]
+        return {"ap": T[name][tuple([slice(None)] + idx)], "reg": [(name, bits)], "n": num, "dt": SCRATCH[name][2],
+                "ps": SCRATCH[name][0] == "psum", "ind": False}
+
+    def C(name, a, b, s=1):
+        return R(name, slice(a, b, s))
+
+    def IN(win, off):
+        return {"ap": win["ap"].indirect(off["ap"]), "reg": win["reg"], "off": off["reg"], "n": 16 * off["n"], "dt": win["dt"],
+                "ps": False, "ind": True}
+
+    def add(eng, cost, fn, outs, ins, lat=0.0, sem=None, after=()):
+        rd, wr = [], []
+        for x in ins:
+            if isinstance(x, dict):
+                rd += x["reg"] + x.get("off", [])
+        for x in outs:
+            wr += x["reg"]; rd += x.get("off", [])
+        ops.append({"eng": eng, "cost": cost, "fn": fn, "rd": rd, "wr": wr, "lat": lat, "sem": sem, "bias": cur[0], "after": list(after),
+                    "ind": any(isinstance(x, dict) and x.get("ind") for x in list(ins) + list(outs))})
+        return len(ops) - 1
+
+    def ap(x):
+        return x["ap"] if isinstance(x, dict) else x
+
+    def vcost(out, in0, base):
+        if in0["ind"]:
+            return 60 + 1.56 * in0["n"]
+        if out["ind"]:
+            return 60 + 3.8 * out["n"]
+        return max(64, base * out["n"])
+
+    def half(out, in0):
+        return 0.5 if out["dt"] in (B, U) and in0["dt"] in (B, U) else 1.0
+
+    def cpy(out, in0):
+        return add("V", vcost(out, in0, half(out, in0)), lambda q: q.tensor_copy(out["ap"], in0["ap"]), [out], [in0])
+
+    def ts(out, in0, s1, op0, s2=None, op1=None):
+        if op1 is None:
+            fn = lambda q: q.tensor_scalar(out["ap"], in0["ap"], ap(s1), None, op0)
+        else:
+            fn = lambda q: q.tensor_scalar(out["ap"], in0["ap"], ap(s1), ap(s2), op0, op1)
+        return add("V", vcost(out, in0, half(out, in0)), fn, [out], [in0, s1, s2])
+
+    def tt(out, in0, in1, op):
+        base = 1.0 if in0["ps"] or in1["ps"] else 2.0
+        return add("V", vcost(out, in0, base), lambda q: q.tensor_tensor(out["ap"], in0["ap"], in1["ap"], op), [out], [in0, in1])
+
+    def scan(out, d0, d1, op0, op1, init=0.0):
+        return add("V", max(64, out["n"]), lambda q: q.tensor_tensor_scan(out["ap"], d0["ap"], d1["ap"], init, op0, op1), [out], [d0, d1])
+
+    def tr(out, in0):
+        return add("V", max(64, out["n"]), lambda q: q.transpose(out["ap"], in0["ap"]), [out], [in0])
+
+    def red(out, in0):
+        return add("V", max(64, in0["n"]), lambda q: q.tensor_reduce(out["ap"], in0["ap"], AX.X, ALU.add), [out], [in0])
+
+    def ms(out, val):
+        return add("V", max(64, out["n"] * (0.5 if out["dt"] == B else 1)), lambda q: q.memset(out["ap"], val), [out], [])
+
+    def act(out, in0, func=AF.Identity, bias=0.0, scale=1.0):
+        cost = 80 + 1.56 * in0["n"] if in0["ind"] else 40 + max(64, in0["n"])
+        return add("S", cost, lambda q: q.activation(out["ap"], in0["ap"], func, bias=bias, scale=scale), [out], [in0])
+
+    def mm(items):
+        def fn(q):
+            last = None
+            for k, (o, l, r) in enumerate(items):
+                last = q.matmul(o["ap"], l["ap"], r["ap"], k == 0, k == len(items) - 1)
+            return last
+        cost = sum(PE * max(64, r["n"]) * (4 if r["dt"] == F else 1) for o, l, r in items)
+        return add("P", cost, fn, [o for o, l, r in items], [x for o, l, r in items for x in (l, r)], lat=60.0)
+
+    def iota(out, pat, base=0, cm=0):
+        if out["dt"] == I:
+            fn = lambda q: q.iota(out["ap"], pat, base, cm)
+        else:
+            fn = lambda q: q.iota(out["ap"], pat, base, cm, allow_small_or_imprecise_dtypes=True)
+        return add("G", 160 + 2 * out["n"], fn, [out], [])
+
+    def dma(eng, o, i, outs, ins, lat):
+        s = "d%d" % cnt["d"]; cnt["d"] += 1
+        return add(eng, 60, lambda q: q.dma_start(o, i), outs, ins, lat=lat, sem=(s, 16, True))
+
+    def send(parts, lat):
+        sl = "l%d" % cnt["l"]; cnt["l"] += 1
+        sa = []
+        for _ in parts:
+            sa.append("a%d" % cnt["a"]); cnt["a"] += 1
+        if len(parts) == 1:
+            dst, o, i = parts[0]
+            ne = len(topo.engines(core, dst))
+            nin = [len(topo.engines(cq if dst == cp else cp, core))]
+
+            def fn(q):
+                rid, pid, _ = topo.addr(dst)
+                return q.remote_dma(o["ap"], i["ap"], T.sem[sa[0]], T.sem[sl], pid, rid, topo.mask(core, dst))
+        else:
+            def share(a, b, c, k):
+                e = [x for x in topo.engines(a, b) if x in topo.engines(a, c)]
+                return e[:len(e) // 2] if k == 0 else e[len(e) // 2:]
+            es = [share(core, cp, cq, 0), share(core, cp, cq, 1)]
+            ne = len(es[0]) + len(es[1])
+            nin = [len(share(cq, core, T.cores[(rank + 2) % n], 0)), len(share(cp, T.cores[(rank - 2) % n], core, 1))]
+
+            def fn(q):
+                trs = []
+                for k, (dst, o, i) in enumerate(parts):
+                    rid, pid, _ = topo.addr(dst)
+                    trs.append(RemoteDMATransfer(dst_ids=[DstId(rid=rid, pnc=pid)], dma_engine_mask=sum(1 << e for e in es[k]),
+                                                 remote_sem=T.sem[sa[k]], src=i["ap"], dst=o["ap"]))
+                return q.remote_dma_fused(trs, local_sem=T.sem[sl])
+        k0 = add("G", 500, fn, [], [i for d, o, i in parts], lat=1500.0, sem=(sl, ne, False))
+        for k, (d, o, i) in enumerate(parts):
+            add("X", lat, None, [o], [], lat=500.0, sem=(sa[k], nin[k], False), after=[k0])
+        return k0
+
+    w = V // NX
+    for k in range(NX):
+        c = C("XO", k * w, (k + 1) * w)
+        dma("Y", c["ap"], T.pts[:, k * w:(k + 1) * w], [c], [], 2200.0 + 1300 * k)
+    dma("S", T.WI[:], T.way[:], [R("WI")], [], 3000.0)
+    ms(R("ZI"), 0)
+    dma("S", T.ZI[0::16, :], T.cnt[:], [{"reg": [("ZI", 1 << 256)]}], [R("ZI")], 2500.0)
+    dma("S", T.ZI[1::16, :], T.th[:], [{"reg": [("ZI", 1 << 257)]}], [R("ZI")], 2500.0)
+    for k in range(NX):
+        send([(cp, C("XP", k * w, (k + 1) * w), C("XO", k * w, (k + 1) * w))], 3600.0)
+    w = V // NC
+    for k in range(NC):
+        c = C("CI", k * w, (k + 1) * w)
+        dma("Y", c["ap"], T.cand[:, k * w:(k + 1) * w], [c], [], 9000.0 + 4000 * k)
+        for a in range(k * w, (k + 1) * w, 464):
+            cpy(C("CU", a, a + 464), C("CI", a, a + 464))
+            cpy(C("CO", a, a + 464), C("CI", a, a + 464))
+        send([(cp, C("CN", k * w, (k + 1) * w), C("CU", k * w, (k + 1) * w))], 7000.0)
+    ms(C("XO", V, XW), DEAD_O); ms(C("XP", V, XW), DEAD_P)
+    ms(C("DK", 0, 256), DEAD_O); ms(C("DK", 256, 512), DEAD_P)
+
+    pc = lambda k: C("PC", k, k + 1)
+    pf = lambda k: C("PF", k, k + 1)
+    iota(pc(0), [[0, 1]], 0, 1)
+    ts(pc(1), pc(0), 15, ALU.bitwise_and)
+    ts(pc(2), pc(0), 16, ALU.bitwise_and)
+    ts(pc(3), pc(0), 4, ALU.logical_shift_right)
+    ts(pc(4), pc(0), 31, ALU.bitwise_and)
+    ts(pc(5), pc(0), 1, ALU.logical_shift_right, 7, ALU.bitwise_and)
+    ts(pc(6), pc(0), 1, ALU.bitwise_and)
+    ts(pc(7), pc(0), 3, ALU.logical_shift_right, 1, ALU.bitwise_and)
+    ts(pc(8), pc(0), 7, ALU.bitwise_and)
+    cpy(C("PF", 0, 9), C("PC", 0, 9))
+    ts(pf(9), pf(3), 16.0, ALU.mult, 15.0, ALU.add)
+    ts(pf(10), pf(5), 16.0, ALU.mult, pf(6), ALU.add)
+    ts(pf(10), pf(10), 2.0, ALU.mult, pf(2), ALU.add)
+    ts(pf(11), pf(5), pf(6), ALU.add, 7.0, ALU.min)
+    ts(pf(12), pf(6), 64.0, ALU.mult, pf(5), ALU.add)
+    ts(pf(13), pf(1), pf(2), ALU.subtract, 16.0, ALU.add)
+    iota(R("XI"), [[1, 144]])
+    x128 = C("XI", 0, 128)
+    ID, NI, PEN, SI, BO8, BOW = [R("MB", k) for k in range(6)]
+    IDF, ONE = R("MF", 0), R("MF", 1)
+    ts(ID, x128, pf(0), ALU.is_equal)
+    ts(NI, x128, pf(0), ALU.is_equal, -1.0, ALU.mult)
+    ts(PEN, x128, pf(0), ALU.is_equal, 0.0625, ALU.mult)
+    ts(SI, x128, pf(0), ALU.is_equal, SENT, ALU.mult)
+    ts(IDF, x128, pf(0), ALU.is_equal)
+    ms(ONE, 1.0)
+    ts(R("BS"), R("XI"), pf(9), ALU.is_equal, 2.0 ** -16, ALU.mult)
+    ms(C("TM", 0, 16), 0.5); ms(C("TM", 16, 32), 0.0)
+    scan(C("TM", 32, 48), C("TM", 0, 16), C("TM", 16, 32), ALU.mult, ALU.add, 2.0)
+    ts(C("TM", 48, 64), C("XI", 0, 16), pf(1), ALU.is_equal)
+    tt(C("TM", 48, 64), C("TM", 48, 64), C("TM", 32, 48), ALU.mult)
+    red(pf(14), C("TM", 48, 64))
+    ts(pf(15), pf(14), 4.0, ALU.mult)
+    K16, GC, RST, VRS, IC2, KH, KP8, CAP, COH, DUMC = (C("KF", 0, 256), C("KF", 256, 384), C("KF", 384, 512), C("KF", 512, 768), C("KF", 768, 1024),
+                                                       C("KF", 1024, 1152), C("KF", 1152, 1216), C("KF", 1216, 1472), C("KF", 1472, 1520), C("KF", 1520, 1536))
+    CTR, K8 = C("KF", 1536, 1664), C("KF", 1664, 1728)
+    iota(K16, [[0, 16], [1, 16]])
+    iota(GC, [[1, 8], [0, 16]])
+    iota(K8, [[0, 8], [1, 8]])
+    iota(COH, [[1, 6], [0, 8]])
+    k128 = C("KF", 0, 128)
+    ts(BO8, GC, pf(3), ALU.is_equal, 8.0, ALU.mult)
+    ts(BOW, GC, pf(3), ALU.is_equal, pf(14), ALU.mult)
+    ts(RST, k128, 0.0, ALU.is_equal)
+    act(IC2, K16, AF.Sign)
+    act(VRS, IC2, AF.Identity, -1.0e6, 2.0e6)
+    act(KH, k128, AF.Identity, 0.0, 0.5)
+    act(KP8, K8, AF.Sign)
+    for k, o in enumerate((4.0, 5.0, 3.0, 4.0)):
+        act(C("KF", 1216 + 64 * k, 1280 + 64 * k), K8, AF.Identity, o)
+    act(C("KF", 1536, 1600), K8, AF.Identity, -1.0); act(C("KF", 1600, 1664), K8)
+    ts(DUMC, C("XI", 0, 16), 16.0, ALU.mult, pf(1), ALU.add)
+    act(DUMC, DUMC, AF.Identity, float(DUM))
+    ICON, ICB, MASK = C("KB", 0, 128), C("KB", 128, 256), C("KB", 256, 512)
+    act(ICON, k128, AF.Identity, 0.0, 2.0 ** -20)
+    act(ICB, k128, AF.Identity, 61440.0, -4096.0)
+    ts(MASK, K16, pf(1), ALU.not_equal, -65536.0, ALU.mult)
+    for k in range(8):
+        iota(C("IOT", 480 * k, 480 * k + 480), [[1, 480]], 480 * k + 1)
+    lists = {}
+    pos = [0]
+
+    def mk(name, parts):
+        a = pos[0]
+        for pat, base, col in parts:
+            m = 1
+            for _, c in pat:
+                m *= c
+            iota(C("LI", pos[0], pos[0] + m), pat, base)
+            if col is None:
+                cpy(C("LF", pos[0], pos[0] + m), C("LI", pos[0], pos[0] + m))
+            else:
+                ts(C("LF", pos[0], pos[0] + m), C("LI", pos[0], pos[0] + m), pf(col), ALU.add)
+            pos[0] += m
+        lists[name] = a
+        return C("LF", a, pos[0])
+    mk("mi", [([[0, 2], [32, 8]], 0, 4)])
+    mk("perm", [([[1, 2], [4, 4]], 0, 10)])
+    mk("on", [([[1, 8]], 128, None), ([[1, 7], [8, 8]], 0, None), ([[1, 8]], 136, None), ([[1, 6], [8, 8]], 64, None)])
+    mk("r16", [([[1, 16]], 0, None)])
+    mk("r8", [([[8, 2], [0, 2], [2, 4]], 0, 7)])
+    mk("val", [([[8, 4], [2, 4]], 128, 7)])
+    mk("pay", [([[8, 8]], 0, 11), ([[8, 8]], 64, 5)])
+    mk("oh", [([[0, 4]], 0, 8)])
+    mk("dup", [([[16, 8], [0, 2]], 0, 1)])
+    cpy(C("LU", 0, pos[0]), C("LF", 0, pos[0]))
+    nl = pos[0]
+    L = lambda name, a, b: C("LU", lists[name] + a, lists[name] + b)
+    iota(C("W10", 0, 40), [[8, 5], [0, 2], [2, 4]])
+    ts(C("W10", 0, 40), C("W10", 0, 40), pf(7), ALU.add)
+    iota(C("W10", 40, 56), [[8, 8], [0, 2]]); iota(C("W10", 56, 72), [[1, 8], [0, 2]], 128); iota(C("W10", 72, 88), [[0, 8], [16, 2]])
+    ts(C("W10", 40, 56), C("W10", 40, 56), pf(12), ALU.add)
+    ts(C("W10", 72, 88), C("W10", 72, 88), pf(2), ALU.is_equal)
+    tt(C("W10", 40, 56), C("W10", 40, 56), C("W10", 56, 72), ALU.subtract)
+    tt(C("W10", 40, 56), C("W10", 40, 56), C("W10", 72, 88), ALU.mult)
+    tt(C("W10", 40, 56), C("W10", 40, 56), C("W10", 56, 72), ALU.add)
+    iota(C("W10", 56, 64), [[32, 8]])
+    ts(C("W10", 56, 64), C("W10", 56, 64), pf(13), ALU.add)
+    lists["out"] = nl; lists["sib"] = nl + 16
+    cpy(C("LU", nl, nl + 24), C("W10", 40, 64))
+    cpy(C("LT", 0, 40), C("W10", 0, 40))
+
+    XOw, XPw = C("XO", 0, DUM), C("XP", 0, DUM)
+
+    for h in range(2):
+        H = str(h)
+        ms(C("VE" + H, 1024, 1040), 0.0); ms(C("PW" + H, 128, 160), 0.0)
+        for src in ("ZI", "WI"):
+            win = IN(C(src, 128 * h, 128 * h + 128), L("dup", 0, 16))
+            win["reg"] = win["reg"] + [(src, 3 << 256)]
+            cpy(R("CR" + H), win)
+            tr(R("TT" + H), R("CR" + H))
+            act(C("W2" + H, 0, 128), IN(R("TT" + H), L("mi", 0, 8)))
+            if src == "ZI":
+                act(R("IX" + H), C("W2" + H, 0, 128, 16), AF.Identity, -0.5, 0.5)
+                act(C("TH", 8 * h, 8 * h + 8), C("W2" + H, 1, 128, 16), AF.Identity, 0.0, 2.0 ** -16)
+            else:
+                tt(C("W3" + H, 0, 128), IN(R("IX" + H), L("r8", 0, 8)), CTR, ALU.is_le)
+                act(C("W3" + H, 0, 128), C("W3" + H, 0, 128), AF.Identity, 0.0, SENT)
+                tt(C("PW" + H, 0, 64), C("W2" + H, 0, 128, 2), C("W3" + H, 0, 64), ALU.max)
+                tt(C("PW" + H, 64, 128), C("W2" + H, 1, 128, 2), C("W3" + H, 64, 128), ALU.max)
+    for a in range(0, V, 464):
+        cpy(C("CP", a, a + 464), C("CN", a, a + 464))
+
+    def group(parts, whole):
+        for j, part in enumerate(parts):
+            def fn(q, part=part, j=j):
+                last = None
+                for k, (o, l, x) in enumerate(part):
+                    last = q.matmul(o["ap"], l["ap"], x["ap"], j == 0 and k == 0, j == len(parts) - 1 and k == len(part) - 1)
+                return last
+            add("P", sum(PE * max(64, x["n"]) for o, l, x in part), fn, [whole], [y for o, l, x in part for y in (l, x)], lat=60.0)
+
+    def reduce_mm(H, extra, ms_, is_):
+        D = C("pD" + H, 0, 128)
+        parts = [[(C("pD" + H, 16 * a.start + b.start, 16 * a.stop, b.step), C("BS", 15 - s, 143 - s), R("A" + H, a, b, s)) for s in range(16)]
+                 for a in ms_ for b in is_]
+        parts[0] = [(D, ID, ICON)] + parts[0]
+        if extra:
+            parts.insert(EQAT, [(D, PEN, x) for x in extra])
+        group(parts, R("pD" + H))
+        return D
+
+    def edges(h, rnd):
+        H = str(h)
+        PW = "PW" + H
+        sm = lambda k: C("SM" + H, 8 * k, 8 * k + 8)
+        cpy(R("LP" + H), C(PW, 0, 128))
+        for c in range(2):
+            act(C("VE" + H, 512 * c, 512 * c + 512), IN(XOw, C("LP" + H, 32 * c, 32 * c + 32)))
+            (act if (h, c) in VOS else cpy)(C("VO" + H, 512 * c, 512 * c + 512), IN(XPw, C("LP" + H, 64 + 32 * c, 96 + 32 * c)))
+        for c in range(2):
+            for sd in range(2):
+                bk = R(("pA", "pB")[sd] + H)
+                mm([(bk, ID, C("VO" + H, 512 * c, 512 * c + 512)), (bk, NI, C("VE" + H, 512 * c + 16 * sd, 512 * c + 512 + 16 * sd))])
+                act(R("A" + H, slice(4 * c, 4 * c + 4), slice(sd, 16, 2)), bk, AF.Abs)
+        act(R("W1" + H), IN(R(PW), L("pay", 0, 16)))
+        for k in range(2):
+            o = C("pD" + H, 128 + 128 * k, 256 + 128 * k)
+            mm([(o, ID, ICB), (o, IDF, C("W1" + H, 128 * k, 128 * k + 128))])
+        D = reduce_mm(H, [], [slice(0, 4), slice(4, 8)], [slice(0, 16, 1)])
+        if rnd == 0:
+            scan(R("R" + H), RST, D, ALU.max, ALU.min)
+            tt(R("NN" + H), D, R("R" + H), ALU.not_equal)
+        else:
+            ts(C("W2" + H, 0, 128), D, 0.125, ALU.is_lt)
+            ts(sm(0), C("pD" + H, 0, 128, 16), 0.375, ALU.is_ge)
+            scan(C("W2" + H, 128, 256), RST, C("W2" + H, 0, 128), ALU.max, ALU.min)
+            scan(C("W3" + H, 0, 64), KP8, C("W2" + H, 128, 256, 2), ALU.mult, ALU.add)
+            scan(C("W3" + H, 64, 128), KP8, C("W2" + H, 129, 256, 2), ALU.mult, ALU.add)
+            Uc, Tc = C("W3" + H, 7, 64, 8), C("W3" + H, 71, 128, 8)
+            tt(sm(1), R("IX" + H), Uc, ALU.subtract)
+            tt(sm(2), sm(1), Tc, ALU.subtract)
+            tt(sm(3), sm(2), sm(0), ALU.add)
+            ts(sm(4), sm(3), 2.0, ALU.is_ge)
+            ts(sm(5), sm(3), 2.0, ALU.is_ge, 8.0, ALU.mult)
+            ts(sm(6), Uc, 1.0, ALU.add)
+            tt(C("TS" + H, 0, 8), sm(6), sm(4), ALU.mult)
+            tt(C("TS" + H, 8, 16), sm(5), Tc, ALU.max)
+            tt(C("W2" + H, 0, 128), IN(R("TS" + H), L("r16", 0, 8)), KH, ALU.is_ge)
+            tt(C("W2" + H, 128, 256), IN(R("TS" + H), L("r16", 8, 16)), KH, ALU.is_le)
+            tt(C("W3" + H, 128, 256), D, C("W2" + H, 128, 256), ALU.max)
+            scan(R("R" + H), C("W2" + H, 0, 128), C("W3" + H, 128, 256), ALU.max, ALU.min)
+            tt(R("NN" + H), C("W3" + H, 128, 256), R("R" + H), ALU.not_equal)
+        for k in range(2):
+            scan(R("PL" + H, k), R("NN" + H), C("pD" + H, 128 + 128 * k, 256 + 128 * k), ALU.mult, ALU.max)
+        cpy(R("TI" + H), R("PL" + H, slice(None), slice(15, 128, 16)))
+        ts(R("AB", slice(None), slice(8 * h, 8 * h + 8)), R("TI" + H), 4095, ALU.bitwise_and)
+        tt(C("PRP", 8 * h, 8 * h + 8), C("R" + H, 15, 128, 16), C("TH" if rnd == 0 else "THR", 8 * h, 8 * h + 8), ALU.is_lt)
+        if rnd > 0:
+            act(sm(7), sm(2), AF.Identity, -1.0)
+            tt(sm(7), sm(7), sm(4), ALU.mult)
+            tt(R("IX" + H), sm(7), Tc, ALU.add)
+            tt(sm(8), sm(0), sm(4), ALU.is_gt)
+            ts(sm(9), C(PW, 0, 64, 8), float(V - 97), ALU.is_ge, -float(V), ALU.mult)
+            act(sm(9), sm(9), AF.Identity, 97.0)
+            tt(sm(9), sm(9), sm(8), ALU.mult)
+            tt(R("OH" + H), IN(C("TS" + H, 0, 8), L("oh", 0, 3)), COH, ALU.is_equal)
+            for t in range(5):
+                tt(R("PR" + H, t), IN(R("OH" + H), C("LT", 8 * t, 8 * t + 8)), C(PW, t, t + 128), ALU.mult)
+            tt(C("FL" + H, 0, 128), IN(R("IX" + H), L("r8", 0, 8)), CTR, ALU.is_le)
+            bk = C("pA" + H, 0, 128)
+            mm([(bk, SI, C("FL" + H, 0, 128))] + [(bk, IDF, R("PR" + H, t)) for t in range(5)])
+            ts(C(PW, 0, 128), bk, SENT, ALU.min)
+            tt(C(PW, 0, 64, 8), C(PW, 0, 64, 8), sm(9), ALU.add)
+        ts(C("W2" + H, 0, 64), C(PW, 0, 64), SENT, ALU.is_lt, 8192.0, ALU.mult)
+        scan(C("W2" + H, 64, 128), C("W2" + H, 0, 64), C(PW, 0, 64), ALU.max, ALU.min)
+        for d in range(2):
+            cpy(C("EX" + H, d, 16, 2), C("W2" + H, 71, 128, 8))
+        ts(sm(10), R("IX" + H), 6.0, ALU.is_le); ts(sm(11), R("IX" + H), 5.0, ALU.is_le)
+        act(sm(12), R("IX" + H), AF.Identity, 5.0); act(sm(13), R("IX" + H), AF.Identity, 5.0)
+
+    def merge(rnd):
+        r = str(rnd)
+        cpy(R("ABU"), R("AB"))
+        act(C("XA", 0, 256), IN(XOw, C("ABU", 0, 16)))
+        act(C("XA", 256, 512), IN(XPw, C("ABU", 16, 32)))
+        bk = C("pM", 0, 256)
+        mm([(bk, ID, C("XA", 0, 256)), (bk, ID, C("XA", 256, 512))])
+        act(R("MT"), bk, AF.Identity, MAGIC, 0.5 - 2.0 ** -11)
+        act(R("MID" + r), R("MT"), AF.Identity, -MAGIC)
+        send([(cp, R("MIN" + r), R("MID" + r))], 1000.0)
+        cpy(R("ROW"), IN(R("IOT"), R("ABU")))
+        ts(R("AS"), R("AB"), 1.0, ALU.add)
+        for k in range(2):
+            tt(C("AS", 16 * k, 16 * k + 16), C("AS", 16 * k, 16 * k + 16), R("PRP"), ALU.mult)
+        act(C("LS", 0, 16), R("PRP"), AF.Identity, 1.0, -1.0)
+        for m in range(16):
+            for k, E in enumerate(("EA", "EB")):
+                ts(R(E, m, slice(0, 256 - 16 * m)), C("ROW", 256 * k + 16 * m, 256 * k + 256), C("AS", 16 * k + m, 16 * k + m + 1), ALU.is_equal)
+        items = [(C("pC", 0, 256), ID, MASK)]
+        for m in range(15):
+            for E in ("EA", "EB"):
+                items.append((C("pC", 16 * m + 16, 256), BO8, R(E, m, slice(16, 256 - 16 * m))))
+        for E in ("EA", "EB"):
+            items.append((C("pC", 0, 256), BOW, R(E, slice(None), slice(0, 16))))
+        cuts = [0, 5, 11, 19, 27, len(items)]
+        group([items[cuts[j]:cuts[j + 1]] for j in range(5)], C("pC", 0, 256))
+        scan(R("CS"), VRS, C("pC", 0, 256), ALU.min, ALU.max)
+        ts(C("LS", 16, 32), C("CS", 15, 256, 16), pf(15), ALU.is_ge)
+        tt(C("LS", 16, 32), C("LS", 16, 32), C("LS", 0, 16), ALU.max)
+        tt(C("LS", 32, 48), C("LS", 16, 32), DUMC, ALU.mult)
+        for k in range(2):
+            tt(C("LM", 16 * k, 16 * k + 16), C("LS", 32, 48), R("AB", k), ALU.max)
+        cpy(R("LW" + r), R("LM"))
+        send([(cp, R("LA" + r), C("LW" + r, 0, 16)), (cq, R("LB" + r), C("LW" + r, 16, 32))], 600.0)
+        cpy(IN(R("XO"), C("LW" + r, 0, 16)), R("MID" + r))
+        cpy(IN(R("XP"), R("LA" + r)), R("MIN" + r))
+        cpy(IN(R("XP"), C("LW" + r, 16, 32)), C("DK", 256, 512))
+        cpy(IN(R("XO"), R("LB" + r)), C("DK", 0, 256))
+        if rnd < 2:
+            red(C("CT", 0, 1), C("LS", 16, 32))
+            mm([(C("pM", 256, 257), ONE, C("CT", 0, 1))])
+            ts(C("CTI", 0, 1), C("pM", 256, 257), -1.0, ALU.mult, 2048.0, ALU.add)
+            ts(C("CTI", 1, 2), C("CTI", 0, 1), 31, ALU.bitwise_and)
+            ts(C("CT", 1, 2), C("CTI", 1, 2), 2.0 ** -13, ALU.mult)
+            ts(R("THR"), R("TH"), C("CT", 1, 2), ALU.add)
+
+    def hop(h, j, nv):
+        H = str(h)
+        cw, xe, xc = (R("CO"), XOw, XPw) if j % 2 == 0 else (R("CP"), XPw, XOw)
+        b0, nb = ((9, 6), (1, 7), (8, 6), (0, 7))[j]
+        act(R("CR" + H), IN(cw, R("EX" + H)))
+        if j == 0:
+            act(R("W1" + H), IN(xe, R("EX" + H)), AF.Relu, 255.0, -1.0)
+            act(R("XE" + H), R("W1" + H), AF.Identity, 255.0, -1.0)
+        else:
+            act(R("XE" + H), IN(xe, R("EX" + H)))
+        tr(R("TT" + H), R("CR" + H))
+        cpy(R("OF" + H), IN(R("TT" + H), L("perm", 0, 8)))
+        act(R("CW" + H), IN(R("TT" + H), L("mi", 0, 8)))
+        IC = C("pD" + H, 128, 256)
+        mm([(IC, ID, ICB), (IC, IDF, R("CW" + H))])
+        bc = ("pM", "pC")[h]
+        for k in range(2):
+            mm([(C(bc, 128 * k, 128 * k + 128), IDF, R("CW" + H))])
+        for a, b in (([(9, 12), (12, 15)], [(1, 4), (4, 8)], [(8, 9)], [(0, 1)])[j]):
+            act(C("PP" + H, 128 * a, 128 * b), IN(C("PW" + H, 0, 128 if j < 2 else 144), L("on", 8 * a, 8 * b)))
+        z = 0
+        for p in range(8):
+            src = IN(xc, C("OF" + H, 16 * p, 16 * p + 16))
+            out = R("A" + H, slice(None), slice(4 * (p % 4) + p // 4, 4 * (p % 4) + 4, 2))
+            if (p * nv) % 8 < nv:
+                tt(R("D" + H, p), src, R("XE" + H), ALU.subtract)
+                act(out, R("D" + H, p), AF.Abs)
+            else:
+                act(R("D" + H, p), src)
+                bk = C(("pA", "pB")[z % 2] + H, 0, 256)
+                z += 1
+                mm([(bk, ID, R("D" + H, p)), (bk, NI, R("XE" + H))])
+                act(out, bk, AF.Abs)
+        for k in range(0, nb, 2):
+            e = min(2, nb - k)
+            tt(C("EQ" + H, 128 * k, 128 * (k + e)), C("PP" + H, 128 * (b0 + k), 128 * (b0 + k + e)), C(bc, 0, 128 * e), ALU.is_equal)
+        D = reduce_mm(H, [C("EQ" + H, 128 * k, 128 * k + 128) for k in range(nb)], [slice(0, 8)], [slice(0, 16, 2), slice(1, 16, 2)])
+        scan(R("R" + H), RST, D, ALU.max, ALU.min)
+        tt(R("NN" + H), D, R("R" + H), ALU.not_equal)
+        scan(R("PL" + H, 0), R("NN" + H), IC, ALU.mult, ALU.max)
+        cpy(R("TI" + H, 0), R("PL" + H, 0, slice(15, 128, 16)))
+        ts(R("TI" + H, 1), R("TI" + H, 0), 4095, ALU.bitwise_and)
+        if j < 3:
+            for d in range(2):
+                cpy(C("EX" + H, d, 16, 2), R("TI" + H, 1))
+        c = (136, 128, 152, 144)[j]
+        cpy(C("PW" + H, c, c + 8), R("TI" + H, 1))
+        c = (0, 16, 8, 24)[j]
+        ts(C("FD" + H, c, c + 8), C("R" + H, 15, 128, 16), 0.0625, ALU.is_lt)
+
+    def append(h):
+        H = str(h)
+        PW = "PW" + H
+        gg = lambda a, b: C("SM" + H, 112 + a, 112 + b)
+        tt(gg(0, 16), C("FD" + H, 0, 16), C("FD" + H, 16, 32), ALU.mult)
+        tt(gg(0, 16), gg(0, 16), C("SM" + H, 80, 96), ALU.mult)
+        tt(gg(8, 16), gg(8, 16), gg(0, 8), ALU.mult)
+        tt(R("IG" + H), gg(0, 16), C("SM" + H, 96, 112), ALU.mult)
+        tt(R("FL" + H), IN(R("IG" + H), L("r8", 0, 16)), CAP, ALU.not_equal)
+        act(R("W3" + H), IN(R(PW), L("val", 0, 16)))
+        bk = C("pA" + H, 0, 256)
+        mm([(bk, IDF, R("W3" + H)), (bk, SI, R("FL" + H))])
+        for k in range(2):
+            tt(C(PW, 0, 128), C(PW, 0, 128), C("pA" + H, 128 * k, 128 * k + 128), ALU.min)
+        tt(gg(16, 24), gg(0, 8), gg(8, 16), ALU.add)
+        tt(R("IX" + H), R("IX" + H), gg(16, 24), ALU.add)
+
+    t = 0
+    for rnd in range(3):
+        for h in range(2):
+            cur[0] = BIAS * (1 - h)
+            edges(h, rnd)
+        cur[0] = 0.0
+        merge(rnd)
+        if rnd == 2:
+            for k in range(2):
+                c = C("YX", 1856 * k, 1856 * (k + 1))
+                for a in range(1856 * k, 1856 * (k + 1), 464):
+                    ts(C("YX", a, a + 464), C("XO", a, a + 464), 255.0, ALU.min)
+                dma("Y", T.yx[:, 1856 * k:1856 * (k + 1)], c["ap"], [], [c], 6000.0)
+        for h in range(2):
+            cur[0] = BIAS * (1 - h)
+            for j in range(4):
+                hop(h, j, NV[(t + h) % len(NV)])
+                t += 1
+            append(h)
+    for h in range(2):
+        cur[0] = BIAS * (1 - h)
+        H = str(h)
+        ts(C("W2" + H, 0, 128), C("PW" + H, 0, 128), SENT, ALU.is_lt)
+        tt(C("PZ" + H, 0, 128), C("PW" + H, 0, 128), C("W2" + H, 0, 128), ALU.mult)
+        ts(C("PZ" + H, 128, 136), R("IX" + H), 2.0, ALU.mult, 1.0, ALU.add)
+        cpy(R("W1" + H), IN(R("PZ" + H), L("out", 0, 16)))
+        tr(R("TT" + H), R("W1" + H))
+        act(R("YC", 0, slice(128 * h, 128 * h + 128)), IN(R("TT" + H), L("mi", 0, 8)))
+        cpy(R("YC", 1, slice(128 * h, 128 * h + 128)), IN(R("TT" + H), L("sib", 0, 8)))
+        dma("S", T.yw[:, 128 * h:128 * h + 128], T.YC[:, 0, 128 * h:128 * h + 128], [], [R("YC", 0, slice(128 * h, 128 * h + 128))], 2200.0)
+    dma("Y", T.yn[0::2, :], T.YC[16::32, 1, :], [], [R("YC", 1)], 2000.0)
+    dma("Y", T.yn[1::2, :], T.YC[0::32, 1, :], [], [R("YC", 1)], 2000.0)
+    return ops
+
+
+_sb("LT", [40], U)
+
+
+def order(ops):
+    n = len(ops)
+    hist = {}
+    bank = {}
+    pred = []
+    for k, o in enumerate(ops):
+        p = set(o["after"])
+        for w, regs in ((False, o["rd"]), (True, o["wr"])):
+            for name, bits in regs:
+                if SCRATCH[name][0] == "psum":
+                    ph = bank.setdefault(name, [o["eng"], [], []])
+                    if ph[0] != o["eng"]:
+                        ph[:] = [o["eng"], [], ph[1]]
+                        hist[name] = []
+                    p.update(ph[2])
+                    ph[1].append(k)
+                for (j, w2, b2) in hist.get(name, []):
+                    if j != k and (w or w2) and bits & b2:
+                        p.add(j)
+        for w, regs in ((False, o["rd"]), (True, o["wr"])):
+            for name, bits in regs:
+                hs = hist.setdefault(name, [])
+                if w:
+                    hs[:] = [x for x in hs if x[2] & ~bits]
+                hs.append((k, w, bits))
+        pred.append(sorted(p))
+    succ = [[] for _ in range(n)]
+    for k in range(n):
+        for j in pred[k]:
+            succ[j].append(k)
+    lev = [0.0] * n
+    for k in range(n - 1, -1, -1):
+        lev[k] = ops[k]["cost"] + ops[k]["lat"] + max([lev[j] + LAT for j in succ[k]] + [0.0])
+    x = SEED
+    for k in range(n):
+        x = (x * 1103515245 + 12345) % 2147483648
+        lev[k] += ops[k]["bias"] + NOISE * x / 2147483648.0
+    left = [len(p) for p in pred]
+    rdy = {k: 0.0 for k in range(n) if left[k] == 0}
+    free = {}
+    fin = [0.0] * n
+    seq = []
+    while rdy:
+        best = min(rdy, key=lambda k: max(rdy[k], free.get(ops[k]["eng"], 0.0)))
+        e = ops[best]["eng"]
+        t0 = max(rdy[best], free.get(e, 0.0))
+        k = max([j for j in rdy if ops[j]["eng"] == e and rdy[j] <= t0 + WIN], key=lambda j: lev[j])
+        s = max(rdy.pop(k), free.get(e, 0.0))
+        free[e] = s + ops[k]["cost"]
+        fin[k] = free[e] + ops[k]["lat"]
+        seq.append(k)
+        for j in succ[k]:
+            left[j] -= 1
+            if left[j] == 0:
+                rdy[j] = max(fin[i] + LAT for i in pred[j])
+
+    def gap(j, k):
+        return ops[j]["lat"] + (0.0 if ops[j]["eng"] == "P" and ops[k]["eng"] == "P" else LAT)
+
+    def place(lst, back):
+        busy = {}
+        end = [0.0] * n
+        for k in lst:
+            c = max(ops[k]["cost"], 1.0)
+            if back:
+                s = max([end[j] + gap(k, j) for j in succ[k]] + [ops[k]["lat"]])
+            else:
+                s = max([end[j] + gap(j, k) for j in pred[k]] + [0.0])
+            b = busy.setdefault(ops[k]["eng"], [])
+            lo, hi = 0, len(b)
+            while lo < hi:
+                mid = (lo + hi) // 2
+                if b[mid][1] <= s:
+                    lo = mid + 1
+                else:
+                    hi = mid
+            while lo < len(b) and b[lo][0] < s + c:
+                s = max(s, b[lo][1])
+                lo += 1
+            b.insert(lo, (s, s + c))
+            end[k] = s + c
+        return end
+    end = place(seq, False)
+    best = None
+    for _ in range(PASSES):
+        span = max(end[k] + ops[k]["lat"] for k in range(n))
+        if best is None or span < best[0]:
+            best = (span, end)
+        end = place(sorted(range(n), key=lambda k: (-end[k], -k)), True)
+        end = place(sorted(range(n), key=lambda k: (-end[k], k)), False)
+    end = best[1]
+    seq = sorted(range(n), key=lambda k: (end[k] - max(ops[k]["cost"], 1.0), k))
+    return pred, seq, [end[k] + ops[k]["lat"] for k in range(n)]
+
+
+def rank_program(g, core, T, topo):
+    if T.rank_of(core) is None:
+        return
+    ops = build(g, core, T, topo)
+    pred, seq, fin = order(ops)
+    Q = {"V": g.vector, "S": g.scalar, "P": g.tensor, "G": g, "Y": g.sync}
+    tok = {}
+    know = {}
+    at = {k: i for i, k in enumerate(seq)}
+    count = {}
+    seen = {e: {} for e in Q}
+    for k in seq:
+        o = ops[k]
+        e = o["eng"]
+        if e == "X":
+            tok[k] = o["sem"][:2]
+            count[tok[k][0]] = tok[k][1]
+            continue
+        need = {}
+        for j in pred[k]:
+            if e == "P" and ops[j]["eng"] == "P":
+                continue
+            s, v = tok[j]
+            if need.get(s, (0, 0))[0] < v:
+                need[s] = (v, j)
+        for s, (v, j) in sorted(need.items(), key=lambda y: -at[y[1][1]]):
+            if seen[e].get(s, 0) < v:
+                Q[e].wait_ge(T.sem[s], v)
+                seen[e][s] = v
+                for s2, v2 in know.get(j, {}).items():
+                    if seen[e].get(s2, 0) < v2:
+                        seen[e][s2] = v2
+        know[k] = dict(seen[e])
+        ins = o["fn"](Q[e])
+        if o["sem"] is None:
+            s = "c" + e
+            count[s] = count.get(s, 0) + 1
+            ins.then_inc(T.sem[s], 1)
+            tok[k] = (s, count[s])
+        else:
+            tok[k] = o["sem"][:2]
+            count[tok[k][0]] = tok[k][1]
+            if o["sem"][2]:
+                ins.then_inc(T.sem[tok[k][0]], 16)
+    for s, v in count.items():
+        if seen["G"].get(s, 0) < v:
+            g.wait_ge(T.sem[s], v)

@@ -5,21 +5,23 @@ V = 3712
 SENT = 3712.0
 DUM = 3728
 XW = DUM + 256
-DEAD_O, DEAD_P = 2048.0, -1024.0
+DEAD_O, DEAD_P = 3584.0, 1280.0
 MAGIC = 12582912.0
-NV = (5, 6)
-BIAS = 4000.0
+HB = (48, 48, 32)
+HV = ()
+EB = (64, 64)
+EV = ((1,), (), ())
+PENAT = 1
+BIAS = 2500.0
 LAT = 120.0
 PE = 0.55
-EQAT = 1
-VOS = ((0, 1), (1, 1))
-SEED = 10
-NOISE = 1000.0
+SEED = 36
+NOISE = 300.0
 WIN = 30.0
 PASSES = 8
 NX, NC = 4, 2
 
-F, B, I, U = "float32", "bfloat16", "int32", "uint16"
+F, B, I, U, H16 = "float32", "bfloat16", "int32", "uint16", "float16"
 SCRATCH = {}
 
 
@@ -28,33 +30,32 @@ def _sb(name, shape, dt):
 
 
 for _n, _s, _d in [
-    ("XO", [XW], B), ("XP", [XW], B), ("CI", [V], I), ("CO", [V], F), ("CP", [V], F), ("CU", [V], U), ("CN", [V], U),
-    ("IOT", [3840], F), ("YX", [V], B), ("WI", [256], I), ("ZI", [256], I),
-    ("PC", [16], I), ("PF", [24], F), ("XI", [144], F), ("MB", [6, 128], B), ("MF", [2, 128], F), ("BS", [144], B),
-    ("KF", [1792], F), ("KB", [512], B), ("LI", [256], I), ("LF", [256], F), ("LU", [256], U), ("TM", [64], F),
-    ("TH", [16], F), ("THR", [16], F), ("AB", [2, 16], I), ("ABU", [32], U), ("AS", [32], F), ("PRP", [16], F),
-    ("ROW", [512], U), ("EA", [16, 256], B), ("EB", [16, 256], B), ("CS", [256], F), ("LS", [48], F), ("LM", [32], F),
-    ("XA", [512], B), ("MT", [256], F), ("DK", [512], B), ("CT", [8], F), ("CTI", [8], I), ("YC", [2, 256], F),
+    ("X", [2 * XW], B), ("CI", [V], I), ("CP", [V], F), ("CU", [V], U), ("CN", [V], U),
+    ("IOT", [3840], F), ("YX", [V], B), ("WI", [256], I), ("WF", [256], F), ("ZI", [512], I), ("ZF", [512], F),
+    ("PC", [16], I), ("PF", [24], F), ("XI", [128], F), ("MB", [8, 128], B), ("MF", [2, 128], F), ("SEL", [24], B),
+    ("KF", [1792], F), ("KB", [768], B), ("EK", [13, 128], B), ("SAB", [256], B),
+    ("LI", [128], I), ("LF", [128], F), ("LU", [128], U), ("TM", [80], F),
+    ("TH", [16], F), ("THR", [16], F), ("ABU", [32], U), ("AS", [32], F), ("AB", [32], F),
+    ("ROW", [512], U), ("EA", [16, 256], B), ("EB", [16, 256], B), ("LM", [2, 2, 8], F),
+    ("DK", [256], B), ("CT", [24], F), ("CTI", [8], I), ("YC", [256], F), ("YN", [256], F), ("ZZ", [128], B),
 ]:
     _sb(_n, _s, _d)
 for _r in range(3):
     _sb("MID%d" % _r, [256], B); _sb("MIN%d" % _r, [256], B)
-    _sb("LW%d" % _r, [32], U); _sb("LA%d" % _r, [16], U); _sb("LB%d" % _r, [16], U)
+    _sb("LW%d" % _r, [32], U); _sb("LA%d" % _r, [16], U); _sb("LB%d" % _r, [16], U); _sb("AP%d" % _r, [8], U)
 for _h in range(2):
     for _n, _s, _d in [
-        ("PW", [160], F), ("LP", [128], U), ("VE", [1040], B), ("VO", [1024], B), ("A", [8, 16, 16], B), ("R", [128], F),
-        ("NN", [128], F), ("W1", [256], F), ("W2", [256], F), ("W3", [256], F), ("PL", [2, 128], F), ("TI", [2, 8], I),
-        ("SM", [160], F), ("IX", [8], F), ("TS", [16], F), ("OH", [48], F), ("PR", [5, 128], F), ("FL", [256], B),
-        ("EX", [16], U), ("CR", [256], F), ("TT", [256], F), ("OF", [128], U), ("CW", [128], F), ("PP", [1920], F), ("XE", [256], B),
-        ("D", [8, 256], B), ("EQ", [896], B), ("FD", [32], F), ("IG", [16], F), ("PZ", [136], F),
+        ("PW", [144], F), ("LP", [128], U), ("PA", [128], H16), ("PB", [128], H16), ("D", [2048], B), ("A", [2048], B),
+        ("R", [4, 128], F), ("PL", [512], F), ("NN", [128], B), ("W1", [256], F), ("W2", [256], F), ("W3", [256], F),
+        ("SM", [176], F), ("IX", [8], F), ("TS", [16], F), ("OH", [48], F), ("PR", [5, 128], F), ("FL", [256], B),
+        ("EX", [8], U), ("OF", [128], U), ("C16", [128], H16), ("CW", [128], F), ("XE", [128], B), ("WX", [256], F),
+        ("EQ", [7, 128], B), ("FD", [2, 8], F), ("XA", [256], B), ("MT", [128], F), ("CS", [128], F), ("LS", [48], F),
     ]:
         _sb(_n + str(_h), _s, _d)
-    for _n in ("pD", "pA", "pB"):
+    for _n in ("pD", "pX", "pE", "pI"):
         SCRATCH[_n + str(_h)] = ("psum", [128, 512], F)
-SCRATCH["pM"] = ("psum", [128, 512], F)
-SCRATCH["pC"] = ("psum", [128, 512], F)
 
-SEMAPHORES = ["cV", "cS", "cP", "cG"] + ["d%d" % _i for _i in range(20)] + ["l%d" % _i for _i in range(16)] + ["a%d" % _i for _i in range(16)]
+SEMAPHORES = ["cV", "cS", "cP", "cG"] + ["d%d" % _i for _i in range(20)] + ["l%d" % _i for _i in range(24)] + ["a%d" % _i for _i in range(30)]
 
 
 def build(g, core, T, topo):
@@ -65,7 +66,7 @@ def build(g, core, T, topo):
     cur = [0.0]
     cnt = {"d": 0, "l": 0, "a": 0}
 
-    def R(name, *idx):
+    def R(name, *idx, p=slice(None)):
         shp = SCRATCH[name][1][1:]
         idx = list(idx) + [slice(None)] * (len(shp) - len(idx))
         bits = 1
@@ -80,11 +81,11 @@ def build(g, core, T, topo):
                 bits = sum(bits << (y * st) for y in rg)
             num *= len(rg)
             st *= shp[d]
-        return {"ap": T[name][tuple([slice(None)] + idx)], "reg": [(name, bits)], "n": num, "dt": SCRATCH[name][2],
+        return {"ap": T[name][tuple([p] + idx)], "reg": [(name, bits)], "n": num, "dt": SCRATCH[name][2],
                 "ps": SCRATCH[name][0] == "psum", "ind": False}
 
-    def C(name, a, b, s=1):
-        return R(name, slice(a, b, s))
+    def C(name, a, b, s=1, p=slice(None)):
+        return R(name, slice(a, b, s), p=p)
 
     def IN(win, off):
         return {"ap": win["ap"].indirect(off["ap"]), "reg": win["reg"], "off": off["reg"], "n": 16 * off["n"], "dt": win["dt"],
@@ -112,7 +113,7 @@ def build(g, core, T, topo):
         return max(64, base * out["n"])
 
     def half(out, in0):
-        return 0.5 if out["dt"] in (B, U) and in0["dt"] in (B, U) else 1.0
+        return 0.5 if out["dt"] in (B, U, H16) and in0["dt"] in (B, U, H16) else 1.0
 
     def cpy(out, in0):
         return add("V", vcost(out, in0, half(out, in0)), lambda q: q.tensor_copy(out["ap"], in0["ap"]), [out], [in0])
@@ -131,9 +132,6 @@ def build(g, core, T, topo):
     def scan(out, d0, d1, op0, op1, init=0.0):
         return add("V", max(64, out["n"]), lambda q: q.tensor_tensor_scan(out["ap"], d0["ap"], d1["ap"], init, op0, op1), [out], [d0, d1])
 
-    def tr(out, in0):
-        return add("V", max(64, out["n"]), lambda q: q.transpose(out["ap"], in0["ap"]), [out], [in0])
-
     def red(out, in0):
         return add("V", max(64, in0["n"]), lambda q: q.tensor_reduce(out["ap"], in0["ap"], AX.X, ALU.add), [out], [in0])
 
@@ -144,14 +142,18 @@ def build(g, core, T, topo):
         cost = 80 + 1.56 * in0["n"] if in0["ind"] else 40 + max(64, in0["n"])
         return add("S", cost, lambda q: q.activation(out["ap"], in0["ap"], func, bias=bias, scale=scale), [out], [in0])
 
-    def mm(items):
+    def mm(items, first=True, last=True):
         def fn(q):
-            last = None
+            ins = None
             for k, (o, l, r) in enumerate(items):
-                last = q.matmul(o["ap"], l["ap"], r["ap"], k == 0, k == len(items) - 1)
-            return last
-        cost = sum(PE * max(64, r["n"]) * (4 if r["dt"] == F else 1) for o, l, r in items)
-        return add("P", cost, fn, [o for o, l, r in items], [x for o, l, r in items for x in (l, r)], lat=60.0)
+                ins = q.matmul(o["ap"], l["ap"], r["ap"], first and k == 0, last and k == len(items) - 1)
+            return ins
+        cost = sum(PE * max(min(64, l["n"]), r["n"]) * (4 if r["dt"] == F else 1) for o, l, r in items)
+        return add("P", cost, fn, [R(items[0][0]["reg"][0][0])], [x for o, l, r in items for x in (l, r)], lat=60.0)
+
+    def group(parts):
+        for j, part in enumerate(parts):
+            mm(part, j == 0, j == len(parts) - 1)
 
     def iota(out, pat, base=0, cm=0):
         if out["dt"] == I:
@@ -194,393 +196,386 @@ def build(g, core, T, topo):
                 return q.remote_dma_fused(trs, local_sem=T.sem[sl])
         k0 = add("G", 500, fn, [], [i for d, o, i in parts], lat=1500.0, sem=(sl, ne, False))
         for k, (d, o, i) in enumerate(parts):
-            add("X", lat, None, [o], [], lat=500.0, sem=(sa[k], nin[k], False), after=[k0])
+            add("X", lat, None, [o], [], lat=1000.0, sem=(sa[k], nin[k], False), after=[k0])
         return k0
 
     w = V // NX
     for k in range(NX):
-        c = C("XO", k * w, (k + 1) * w)
+        c = C("X", k * w, (k + 1) * w)
         dma("Y", c["ap"], T.pts[:, k * w:(k + 1) * w], [c], [], 2200.0 + 1300 * k)
+    lo8 = slice(0, 8)
     dma("S", T.WI[:], T.way[:], [R("WI")], [], 3000.0)
-    ms(R("ZI"), 0)
-    dma("S", T.ZI[0::16, :], T.cnt[:], [{"reg": [("ZI", 1 << 256)]}], [R("ZI")], 2500.0)
-    dma("S", T.ZI[1::16, :], T.th[:], [{"reg": [("ZI", 1 << 257)]}], [R("ZI")], 2500.0)
+    dma("S", T.ZI[0:8, 0:256], T.cnt[:], [C("ZI", 0, 256)], [], 2500.0)
+    dma("S", T.ZI[0:8, 256:512], T.th[:], [C("ZI", 256, 512)], [], 2500.0)
     for k in range(NX):
-        send([(cp, C("XP", k * w, (k + 1) * w), C("XO", k * w, (k + 1) * w))], 3600.0)
+        send([(cp, C("X", XW + k * w, XW + (k + 1) * w), C("X", k * w, (k + 1) * w))], 3600.0)
     w = V // NC
     for k in range(NC):
         c = C("CI", k * w, (k + 1) * w)
         dma("Y", c["ap"], T.cand[:, k * w:(k + 1) * w], [c], [], 9000.0 + 4000 * k)
         for a in range(k * w, (k + 1) * w, 464):
             cpy(C("CU", a, a + 464), C("CI", a, a + 464))
-            cpy(C("CO", a, a + 464), C("CI", a, a + 464))
         send([(cp, C("CN", k * w, (k + 1) * w), C("CU", k * w, (k + 1) * w))], 7000.0)
-    ms(C("XO", V, XW), DEAD_O); ms(C("XP", V, XW), DEAD_P)
-    ms(C("DK", 0, 256), DEAD_O); ms(C("DK", 256, 512), DEAD_P)
+    ms(C("X", V, XW), DEAD_O); ms(C("X", XW + V, 2 * XW), DEAD_P)
+    ms(C("DK", 0, 128), DEAD_O); ms(C("DK", 128, 256), DEAD_P)
 
     pc = lambda k: C("PC", k, k + 1)
     pf = lambda k: C("PF", k, k + 1)
     iota(pc(0), [[0, 1]], 0, 1)
     ts(pc(1), pc(0), 15, ALU.bitwise_and)
-    ts(pc(2), pc(0), 16, ALU.bitwise_and)
+    ts(pc(2), pc(0), 1, ALU.bitwise_and)
     ts(pc(3), pc(0), 4, ALU.logical_shift_right)
-    ts(pc(4), pc(0), 31, ALU.bitwise_and)
-    ts(pc(5), pc(0), 1, ALU.logical_shift_right, 7, ALU.bitwise_and)
-    ts(pc(6), pc(0), 1, ALU.bitwise_and)
-    ts(pc(7), pc(0), 3, ALU.logical_shift_right, 1, ALU.bitwise_and)
-    ts(pc(8), pc(0), 7, ALU.bitwise_and)
-    cpy(C("PF", 0, 9), C("PC", 0, 9))
-    ts(pf(9), pf(3), 16.0, ALU.mult, 15.0, ALU.add)
-    ts(pf(10), pf(5), 16.0, ALU.mult, pf(6), ALU.add)
-    ts(pf(10), pf(10), 2.0, ALU.mult, pf(2), ALU.add)
-    ts(pf(11), pf(5), pf(6), ALU.add, 7.0, ALU.min)
-    ts(pf(12), pf(6), 64.0, ALU.mult, pf(5), ALU.add)
-    ts(pf(13), pf(1), pf(2), ALU.subtract, 16.0, ALU.add)
-    iota(R("XI"), [[1, 144]])
-    x128 = C("XI", 0, 128)
-    ID, NI, PEN, SI, BO8, BOW = [R("MB", k) for k in range(6)]
+    ts(pc(4), pc(0), 7, ALU.bitwise_and)
+    cpy(C("PF", 0, 5), C("PC", 0, 5))
+    ts(pf(5), pf(2), float(XW), ALU.mult)
+    ts(pf(6), pf(1), 15.0, ALU.is_equal)
+    ts(pf(7), pf(6), 4096.0 - SENT, ALU.mult, -2048.0, ALU.add)
+    tt(pf(8), pf(7), pf(5), ALU.subtract)
+    ts(pf(9), pf(6), -1.0, ALU.mult, 1.0, ALU.add)
+    tt(pf(9), pf(9), pf(8), ALU.add)
+    ts(pf(10), pf(2), -128.0, ALU.mult)
+    ts(pf(11), pf(4), 16.0, ALU.mult)
+    iota(R("XI"), [[1, 128]])
+    x128 = R("XI")
+    ID, NI, PEN, SI, BO8, BOW, N4, GEQ = [R("MB", k) for k in range(8)]
     IDF, ONE = R("MF", 0), R("MF", 1)
-    ts(ID, x128, pf(0), ALU.is_equal)
-    ts(NI, x128, pf(0), ALU.is_equal, -1.0, ALU.mult)
-    ts(PEN, x128, pf(0), ALU.is_equal, 0.0625, ALU.mult)
-    ts(SI, x128, pf(0), ALU.is_equal, SENT, ALU.mult)
     ts(IDF, x128, pf(0), ALU.is_equal)
+    cpy(ID, IDF)
+    for o, x in ((NI, -1.0), (PEN, 0.125), (SI, SENT), (N4, -4096.0)):
+        ts(o, ID, x, ALU.mult)
     ms(ONE, 1.0)
-    ts(R("BS"), R("XI"), pf(9), ALU.is_equal, 2.0 ** -16, ALU.mult)
+    SEL1, SEL2, SELN = C("SEL", 0, 8), C("SEL", 8, 16), C("SEL", 16, 24)
+    for o, x in ((SEL1, 2.0 ** -16), (SEL2, 2.0 ** -15), (SELN, -2.0 ** -16)):
+        ts(o, C("XI", 0, 8), pf(3), ALU.is_equal, x, ALU.mult)
     ms(C("TM", 0, 16), 0.5); ms(C("TM", 16, 32), 0.0)
     scan(C("TM", 32, 48), C("TM", 0, 16), C("TM", 16, 32), ALU.mult, ALU.add, 2.0)
     ts(C("TM", 48, 64), C("XI", 0, 16), pf(1), ALU.is_equal)
     tt(C("TM", 48, 64), C("TM", 48, 64), C("TM", 32, 48), ALU.mult)
     red(pf(14), C("TM", 48, 64))
     ts(pf(15), pf(14), 4.0, ALU.mult)
-    K16, GC, RST, VRS, IC2, KH, KP8, CAP, COH, DUMC = (C("KF", 0, 256), C("KF", 256, 384), C("KF", 384, 512), C("KF", 512, 768), C("KF", 768, 1024),
-                                                       C("KF", 1024, 1152), C("KF", 1152, 1216), C("KF", 1216, 1472), C("KF", 1472, 1520), C("KF", 1520, 1536))
-    CTR, K8 = C("KF", 1536, 1664), C("KF", 1664, 1728)
+    K16, RST, VRS, MW, KH, KP8, CAP, COH, DUMC, SM8 = (C("KF", 0, 256), C("KF", 256, 384), C("KF", 384, 512), C("KF", 512, 768), C("KF", 768, 896),
+                                                       C("KF", 896, 960), C("KF", 960, 1216), C("KF", 1216, 1264), C("KF", 1264, 1296), C("KF", 1296, 1304))
+    K8, KAB, KH1 = C("KF", 1312, 1376), C("KF", 1376, 1632), C("KF", 1632, 1760)
     iota(K16, [[0, 16], [1, 16]])
-    iota(GC, [[1, 8], [0, 16]])
+    iota(C("KB", 640, 768), [[1, 8], [0, 16]])
     iota(K8, [[0, 8], [1, 8]])
     iota(COH, [[1, 6], [0, 8]])
+    for q_ in range(2):
+        iota(C("KF", 960 + 128 * q_, 1088 + 128 * q_), [[0, 8], [1, 8], [1, 2]], 4 - q_)
+        iota(C("KF", 1376 + 128 * q_, 1504 + 128 * q_), [[16, 8], [2, 8], [2 - 2 * q_, 2]], q_)
+    iota(DUMC, [[128, 2], [0, 2], [16, 8]], DUM)
+    iota(C("TM", 64, 70), [[2, 6]], 1); iota(C("TM", 70, 77), [[2, 7]])
     k128 = C("KF", 0, 128)
-    ts(BO8, GC, pf(3), ALU.is_equal, 8.0, ALU.mult)
-    ts(BOW, GC, pf(3), ALU.is_equal, pf(14), ALU.mult)
-    ts(RST, k128, 0.0, ALU.is_equal)
-    act(IC2, K16, AF.Sign)
-    act(VRS, IC2, AF.Identity, -1.0e6, 2.0e6)
+    ts(GEQ, C("KB", 640, 768), pf(3), ALU.is_equal)
+    ts(BO8, GEQ, 8.0, ALU.mult)
+    ts(BOW, GEQ, pf(14), ALU.mult)
+    ts(SM8, C("XI", 0, 8), pf(3), ALU.is_equal)
+    ts(RST, k128, 0.0, ALU.is_equal, 4.0, ALU.mult)
+    ts(MW, K16, pf(1), ALU.is_equal)
+    act(VRS, k128, AF.Sign)
+    act(VRS, VRS, AF.Identity, -1.0e6, 2.0e6)
     act(KH, k128, AF.Identity, 0.0, 0.5)
     act(KP8, K8, AF.Sign)
-    for k, o in enumerate((4.0, 5.0, 3.0, 4.0)):
-        act(C("KF", 1216 + 64 * k, 1280 + 64 * k), K8, AF.Identity, o)
-    act(C("KF", 1536, 1600), K8, AF.Identity, -1.0); act(C("KF", 1600, 1664), K8)
-    ts(DUMC, C("XI", 0, 16), 16.0, ALU.mult, pf(1), ALU.add)
-    act(DUMC, DUMC, AF.Identity, float(DUM))
-    ICON, ICB, MASK = C("KB", 0, 128), C("KB", 128, 256), C("KB", 256, 512)
+    ts(DUMC, DUMC, pf(1), ALU.add)
+    ICON, ICE, MASK, K2 = C("KB", 0, 128), C("KB", 128, 256), C("KB", 256, 384), C("KB", 384, 512)
     act(ICON, k128, AF.Identity, 0.0, 2.0 ** -20)
-    act(ICB, k128, AF.Identity, 61440.0, -4096.0)
-    ts(MASK, K16, pf(1), ALU.not_equal, -65536.0, ALU.mult)
+    act(ICE, k128, AF.Identity, 0.0, 2.0 ** -20)
+    ms(C("KB", 143, 256, 16), 0.0)
+    act(KH1, k128, AF.Identity, 1.0, 0.5)
+    ms(C("KF", 1647, 1760, 16), -1.0)
+    act(MASK, C("KF", 512, 640), AF.Identity, -65536.0, 65536.0)
+    ms(K2, 2048.0)
+    ts(C("TM", 64, 77), C("TM", 64, 77), pf(1), ALU.is_equal, pf(6), ALU.add)
+    for k in range(13):
+        ts(R("EK", k), GEQ, C("TM", 64 + k, 65 + k), ALU.mult)
+    ts(R("SAB"), KAB, pf(0), ALU.is_equal)
+    ts(C("KB", 512, 640), GEQ, pf(6), ALU.mult)
+    for k in range(2):
+        tt(C("SAB", 128 * k, 128 * k + 128), C("SAB", 128 * k, 128 * k + 128), C("KB", 512, 640), ALU.add)
+    ms(C("SAB", 15, 256, 16), 0.0)
     for k in range(8):
         iota(C("IOT", 480 * k, 480 * k + 480), [[1, 480]], 480 * k + 1)
     lists = {}
     pos = [0]
 
-    def mk(name, parts):
+    def mk(name, pat, base, col):
+        m = 1
+        for _, c in pat:
+            m *= c
         a = pos[0]
-        for pat, base, col in parts:
-            m = 1
-            for _, c in pat:
-                m *= c
-            iota(C("LI", pos[0], pos[0] + m), pat, base)
-            if col is None:
-                cpy(C("LF", pos[0], pos[0] + m), C("LI", pos[0], pos[0] + m))
-            else:
-                ts(C("LF", pos[0], pos[0] + m), C("LI", pos[0], pos[0] + m), pf(col), ALU.add)
-            pos[0] += m
+        iota(C("LI", a, a + m), pat, base)
+        if col is None:
+            cpy(C("LF", a, a + m), C("LI", a, a + m))
+        else:
+            ts(C("LF", a, a + m), C("LI", a, a + m), pf(col), ALU.add)
+        pos[0] += m
         lists[name] = a
-        return C("LF", a, pos[0])
-    mk("mi", [([[0, 2], [32, 8]], 0, 4)])
-    mk("perm", [([[1, 2], [4, 4]], 0, 10)])
-    mk("on", [([[1, 8]], 128, None), ([[1, 7], [8, 8]], 0, None), ([[1, 8]], 136, None), ([[1, 6], [8, 8]], 64, None)])
-    mk("r16", [([[1, 16]], 0, None)])
-    mk("r8", [([[8, 2], [0, 2], [2, 4]], 0, 7)])
-    mk("val", [([[8, 4], [2, 4]], 128, 7)])
-    mk("pay", [([[8, 8]], 0, 11), ([[8, 8]], 64, 5)])
-    mk("oh", [([[0, 4]], 0, 8)])
-    mk("dup", [([[16, 8], [0, 2]], 0, 1)])
+    mk("r16", [[1, 40]], 0, None)
+    mk("e16", [[16, 16]], 15, None)
+    mk("e8", [[8, 8]], 7, None)
+    mk("val", [[16, 8]], 143, 10)
+    mk("oh", [[0, 4]], 0, 4)
+    mk("c15", [[0, 2]], 15, 11)
     cpy(C("LU", 0, pos[0]), C("LF", 0, pos[0]))
-    nl = pos[0]
     L = lambda name, a, b: C("LU", lists[name] + a, lists[name] + b)
-    iota(C("W10", 0, 40), [[8, 5], [0, 2], [2, 4]])
-    ts(C("W10", 0, 40), C("W10", 0, 40), pf(7), ALU.add)
-    iota(C("W10", 40, 56), [[8, 8], [0, 2]]); iota(C("W10", 56, 72), [[1, 8], [0, 2]], 128); iota(C("W10", 72, 88), [[0, 8], [16, 2]])
-    ts(C("W10", 40, 56), C("W10", 40, 56), pf(12), ALU.add)
-    ts(C("W10", 72, 88), C("W10", 72, 88), pf(2), ALU.is_equal)
-    tt(C("W10", 40, 56), C("W10", 40, 56), C("W10", 56, 72), ALU.subtract)
-    tt(C("W10", 40, 56), C("W10", 40, 56), C("W10", 72, 88), ALU.mult)
-    tt(C("W10", 40, 56), C("W10", 40, 56), C("W10", 56, 72), ALU.add)
-    iota(C("W10", 56, 64), [[32, 8]])
-    ts(C("W10", 56, 64), C("W10", 56, 64), pf(13), ALU.add)
-    lists["out"] = nl; lists["sib"] = nl + 16
-    cpy(C("LU", nl, nl + 24), C("W10", 40, 64))
-    cpy(C("LT", 0, 40), C("W10", 0, 40))
 
-    XOw, XPw = C("XO", 0, DUM), C("XP", 0, DUM)
+    XOw, XPw, XO, XP = C("X", 0, DUM), C("X", XW, XW + DUM), C("X", 0, XW), C("X", XW, 2 * XW)
 
+    cpy(R("WF"), R("WI"))
+    cpy(R("ZF", p=lo8), R("ZI", p=lo8))
     for h in range(2):
         H = str(h)
-        ms(C("VE" + H, 1024, 1040), 0.0); ms(C("PW" + H, 128, 160), 0.0)
-        for src in ("ZI", "WI"):
-            win = IN(C(src, 128 * h, 128 * h + 128), L("dup", 0, 16))
-            win["reg"] = win["reg"] + [(src, 3 << 256)]
-            cpy(R("CR" + H), win)
-            tr(R("TT" + H), R("CR" + H))
-            act(C("W2" + H, 0, 128), IN(R("TT" + H), L("mi", 0, 8)))
-            if src == "ZI":
-                act(R("IX" + H), C("W2" + H, 0, 128, 16), AF.Identity, -0.5, 0.5)
-                act(C("TH", 8 * h, 8 * h + 8), C("W2" + H, 1, 128, 16), AF.Identity, 0.0, 2.0 ** -16)
-            else:
-                tt(C("W3" + H, 0, 128), IN(R("IX" + H), L("r8", 0, 8)), CTR, ALU.is_le)
-                act(C("W3" + H, 0, 128), C("W3" + H, 0, 128), AF.Identity, 0.0, SENT)
-                tt(C("PW" + H, 0, 64), C("W2" + H, 0, 128, 2), C("W3" + H, 0, 64), ALU.max)
-                tt(C("PW" + H, 64, 128), C("W2" + H, 1, 128, 2), C("W3" + H, 64, 128), ALU.max)
+        ms(C("PW" + H, 128, 144), 0.0)
+        mm([(C("pI" + H, 0, 128), C("WF", 128 * h, 128 * h + 128), IDF)])
+        for k in range(2):
+            mm([(C("pI" + H, 128 + 8 * k, 136 + 8 * k), C("ZF", 256 * k + 128 * h, 256 * k + 128 * h + 128, p=lo8), R("MF", 0, slice(0, 8), p=lo8))])
+        ts(R("IX" + H), C("pI" + H, 128, 136), 0.5, ALU.mult, -0.5, ALU.add)
+        ts(C("TH", 8 * h, 8 * h + 8), C("pI" + H, 136, 144), 2.0 ** -16, ALU.mult)
+        tt(C("W3" + H, 0, 128), IN(R("IX" + H), L("r16", 0, 8)), KH, ALU.is_lt)
+        ts(C("W3" + H, 0, 128), C("W3" + H, 0, 128), SENT, ALU.mult)
+        tt(C("PW" + H, 0, 128), C("W3" + H, 0, 128), C("pI" + H, 0, 128), ALU.max)
     for a in range(0, V, 464):
         cpy(C("CP", a, a + 464), C("CN", a, a + 464))
 
-    def group(parts, whole):
-        for j, part in enumerate(parts):
-            def fn(q, part=part, j=j):
-                last = None
-                for k, (o, l, x) in enumerate(part):
-                    last = q.matmul(o["ap"], l["ap"], x["ap"], j == 0 and k == 0, j == len(parts) - 1 and k == len(part) - 1)
-                return last
-            add("P", sum(PE * max(64, x["n"]) for o, l, x in part), fn, [whole], [y for o, l, x in part for y in (l, x)], lat=60.0)
+    def spread(H, bank, win, off, k):
+        tt(C("WX" + H, 0, 128 * k), IN(win, off), C("KF", 512, 512 + 128 * k), ALU.mult)
+        for j in range(k):
+            mm([(C(bank + H, 384 + 8 * j, 392 + 8 * j), C("WX" + H, 128 * j, 128 * j + 128), SM8)])
+        return C(bank + H, 384, 384 + 8 * k)
 
-    def reduce_mm(H, extra, ms_, is_):
-        D = C("pD" + H, 0, 128)
-        parts = [[(C("pD" + H, 16 * a.start + b.start, 16 * a.stop, b.step), C("BS", 15 - s, 143 - s), R("A" + H, a, b, s)) for s in range(16)]
-                 for a in ms_ for b in is_]
-        parts[0] = [(D, ID, ICON)] + parts[0]
-        if extra:
-            parts.insert(EQAT, [(D, PEN, x) for x in extra])
-        group(parts, R("pD" + H))
-        return D
+    def gathers(H, win, off, blocks, onv):
+        a = 0
+        for k, m in enumerate(blocks):
+            (cpy if k in onv else act)(C("D" + H, 16 * a, 16 * (a + m)), IN(win, C(off, a, a + m)))
+            a += m
 
     def edges(h, rnd):
         H = str(h)
         PW = "PW" + H
         sm = lambda k: C("SM" + H, 8 * k, 8 * k + 8)
-        cpy(R("LP" + H), C(PW, 0, 128))
-        for c in range(2):
-            act(C("VE" + H, 512 * c, 512 * c + 512), IN(XOw, C("LP" + H, 32 * c, 32 * c + 32)))
-            (act if (h, c) in VOS else cpy)(C("VO" + H, 512 * c, 512 * c + 512), IN(XPw, C("LP" + H, 64 + 32 * c, 96 + 32 * c)))
-        for c in range(2):
-            for sd in range(2):
-                bk = R(("pA", "pB")[sd] + H)
-                mm([(bk, ID, C("VO" + H, 512 * c, 512 * c + 512)), (bk, NI, C("VE" + H, 512 * c + 16 * sd, 512 * c + 512 + 16 * sd))])
-                act(R("A" + H, slice(4 * c, 4 * c + 4), slice(sd, 16, 2)), bk, AF.Abs)
-        act(R("W1" + H), IN(R(PW), L("pay", 0, 16)))
-        for k in range(2):
-            o = C("pD" + H, 128 + 128 * k, 256 + 128 * k)
-            mm([(o, ID, ICB), (o, IDF, C("W1" + H, 128 * k, 128 * k + 128))])
-        D = reduce_mm(H, [], [slice(0, 4), slice(4, 8)], [slice(0, 16, 1)])
+        R0 = R("R" + H, 0)
+        mm([(C("pI" + H, 0, 128), C(PW, 0, 128), IDF)])
+        ts(R("LP" + H), C("pI" + H, 0, 128), pf(5), ALU.add)
+        ts(R("PA" + H), R("LP" + H), pf(9), ALU.add)
         if rnd == 0:
-            scan(R("R" + H), RST, D, ALU.max, ALU.min)
-            tt(R("NN" + H), D, R("R" + H), ALU.not_equal)
-        else:
-            ts(C("W2" + H, 0, 128), D, 0.125, ALU.is_lt)
-            ts(sm(0), C("pD" + H, 0, 128, 16), 0.375, ALU.is_ge)
-            scan(C("W2" + H, 128, 256), RST, C("W2" + H, 0, 128), ALU.max, ALU.min)
-            scan(C("W3" + H, 0, 64), KP8, C("W2" + H, 128, 256, 2), ALU.mult, ALU.add)
-            scan(C("W3" + H, 64, 128), KP8, C("W2" + H, 129, 256, 2), ALU.mult, ALU.add)
-            Uc, Tc = C("W3" + H, 7, 64, 8), C("W3" + H, 71, 128, 8)
-            tt(sm(1), R("IX" + H), Uc, ALU.subtract)
-            tt(sm(2), sm(1), Tc, ALU.subtract)
-            tt(sm(3), sm(2), sm(0), ALU.add)
-            ts(sm(4), sm(3), 2.0, ALU.is_ge)
-            ts(sm(5), sm(3), 2.0, ALU.is_ge, 8.0, ALU.mult)
-            ts(sm(6), Uc, 1.0, ALU.add)
-            tt(C("TS" + H, 0, 8), sm(6), sm(4), ALU.mult)
-            tt(C("TS" + H, 8, 16), sm(5), Tc, ALU.max)
-            tt(C("W2" + H, 0, 128), IN(R("TS" + H), L("r16", 0, 8)), KH, ALU.is_ge)
-            tt(C("W2" + H, 128, 256), IN(R("TS" + H), L("r16", 8, 16)), KH, ALU.is_le)
-            tt(C("W3" + H, 128, 256), D, C("W2" + H, 128, 256), ALU.max)
-            scan(R("R" + H), C("W2" + H, 0, 128), C("W3" + H, 128, 256), ALU.max, ALU.min)
-            tt(R("NN" + H), C("W3" + H, 128, 256), R("R" + H), ALU.not_equal)
-        for k in range(2):
-            scan(R("PL" + H, k), R("NN" + H), C("pD" + H, 128 + 128 * k, 256 + 128 * k), ALU.mult, ALU.max)
-        cpy(R("TI" + H), R("PL" + H, slice(None), slice(15, 128, 16)))
-        ts(R("AB", slice(None), slice(8 * h, 8 * h + 8)), R("TI" + H), 4095, ALU.bitwise_and)
-        tt(C("PRP", 8 * h, 8 * h + 8), C("R" + H, 15, 128, 16), C("TH" if rnd == 0 else "THR", 8 * h, 8 * h + 8), ALU.is_lt)
+            ts(R("PB" + H), R("LP" + H), pf(8), ALU.add)
+        gathers(H, R("X"), "LP" + H, EB, EV[rnd])
+        mm([(C("pI" + H, 128, 384), R("PA" + H), R("SAB"))], True, False)
+        D = C("pD" + H, 0, 128)
+        parts = [[(D, ID, ICE), (C("pD" + H, 15, 128, 16), IDF, C("TH" if rnd == 0 else "THR", 8 * h, 8 * h + 8))]]
         if rnd > 0:
-            act(sm(7), sm(2), AF.Identity, -1.0)
-            tt(sm(7), sm(7), sm(4), ALU.mult)
-            tt(R("IX" + H), sm(7), Tc, ALU.add)
-            tt(sm(8), sm(0), sm(4), ALU.is_gt)
-            ts(sm(9), C(PW, 0, 64, 8), float(V - 97), ALU.is_ge, -float(V), ALU.mult)
+            mm([(C("pD" + H, 128, 256), ID, ICE)] + [(C("pD" + H, 128 + k, 256, 16), C("D" + H, k, 2048, 16), SEL1) for k in range(16)])
+            ts(C("W2" + H, 0, 128), C("pD" + H, 128, 256), 0.125, ALU.is_lt)
+            scan(C("W2" + H, 128, 256), RST, C("W2" + H, 0, 128), ALU.max, ALU.min)
+            scan(C("W3" + H, 0, 64), KP8, C("W2" + H, 129, 256, 2), ALU.mult, ALU.add)
+            scan(C("W3" + H, 64, 128), KP8, C("W2" + H, 128, 256, 2), ALU.mult, ALU.add)
+            No, Ne = C("W3" + H, 7, 64, 8), C("W3" + H, 71, 128, 8)
+            tt(sm(1), R("IX" + H), No, ALU.subtract)
+            ts(sm(6), No, 1.0, ALU.add)
+            tt(sm(4), sm(1), Ne, ALU.is_gt)
+            tt(sm(2), sm(1), Ne, ALU.max)
+            tt(C("TS" + H, 0, 8), sm(6), sm(4), ALU.mult)
+            tt(C("TS" + H, 8, 16), sm(2), C("TS" + H, 0, 8), ALU.add)
+            tt(R("EQ" + H, 0), IN(R("TS" + H), L("r16", 0, 8)), KH, ALU.is_gt)
+            tt(R("EQ" + H, 1), IN(R("TS" + H), L("r16", 8, 16)), KH1, ALU.is_le)
+            parts.append([(D, ID, R("EQ" + H, k)) for k in range(2)])
+        for c in range(4):
+            a = 512 * c
+            bk = C(("pX", "pE")[c % 2] + H, 0, 511)
+            mm([(bk, ID, C("D" + H, a, a + 511)), (bk, NI, C("D" + H, a + 1, a + 512))])
+            act(C("A" + H, a, a + 511), bk, AF.Abs)
+        parts.insert(min(PENAT, len(parts)), [(C("pD" + H, k, 128, 16), C("A" + H, k, 2048, 16), SEL1) for k in range(15)])
+        group(parts)
+        scan(R0, RST, D, ALU.max, ALU.min)
+        tt(R("NN" + H), D, R0, ALU.not_equal)
+        mm([(C("pI" + H, 128 + 128 * k, 256 + 128 * k), N4, R("NN" + H)) for k in range(2)], False, True)
+        for k in range(2):
+            scan(C("PL" + H, 128 * k, 128 * k + 128), R("NN" + H), C("pI" + H, 128 + 128 * k, 256 + 128 * k), ALU.mult, ALU.max)
+        o = spread(H, "pI", C("PL" + H, 0, 256), L("e16", 0, 16), 2)
+        ts(C("ABU", 16 * h, 16 * h + 16), o, -1.0, ALU.add)
+        cpy(C("AS", 16 * h, 16 * h + 16), o)
+        if rnd > 0:
+            act(R("IX" + H), sm(2), AF.Relu, -1.0)
+            ts(sm(8), sm(2), 0.5, ALU.is_lt)
+            ts(sm(9), C(PW, 0, 128, 16), float(V - 97), ALU.is_ge, -float(V), ALU.mult)
             act(sm(9), sm(9), AF.Identity, 97.0)
             tt(sm(9), sm(9), sm(8), ALU.mult)
             tt(R("OH" + H), IN(C("TS" + H, 0, 8), L("oh", 0, 3)), COH, ALU.is_equal)
             for t in range(5):
-                tt(R("PR" + H, t), IN(R("OH" + H), C("LT", 8 * t, 8 * t + 8)), C(PW, t, t + 128), ALU.mult)
-            tt(C("FL" + H, 0, 128), IN(R("IX" + H), L("r8", 0, 8)), CTR, ALU.is_le)
-            bk = C("pA" + H, 0, 128)
+                tt(R("PR" + H, t), IN(R("OH" + H), L("r16", 8 * t, 8 * t + 8)), C(PW, 2 * t, 2 * t + 128), ALU.mult)
+            tt(C("FL" + H, 0, 128), IN(R("IX" + H), L("r16", 0, 8)), KH, ALU.is_lt)
+            bk = C("pX" + H, 0, 128)
             mm([(bk, SI, C("FL" + H, 0, 128))] + [(bk, IDF, R("PR" + H, t)) for t in range(5)])
             ts(C(PW, 0, 128), bk, SENT, ALU.min)
-            tt(C(PW, 0, 64, 8), C(PW, 0, 64, 8), sm(9), ALU.add)
-        ts(C("W2" + H, 0, 64), C(PW, 0, 64), SENT, ALU.is_lt, 8192.0, ALU.mult)
-        scan(C("W2" + H, 64, 128), C("W2" + H, 0, 64), C(PW, 0, 64), ALU.max, ALU.min)
-        for d in range(2):
-            cpy(C("EX" + H, d, 16, 2), C("W2" + H, 71, 128, 8))
+            tt(C(PW, 0, 128, 16), C(PW, 0, 128, 16), sm(9), ALU.add)
+            mm([(C("pX" + H, 128, 256), C(PW, 0, 128), IDF)])
+            ts(R("PB" + H), C("pX" + H, 128, 256), pf(7), ALU.add)
+        ts(C("W2" + H, 0, 64), C(PW, 0, 128, 2), SENT, ALU.is_lt, 8192.0, ALU.mult)
+        scan(C("W2" + H, 64, 128), C("W2" + H, 0, 64), C(PW, 0, 128, 2), ALU.max, ALU.min)
+        cpy(R("EX" + H), spread(H, "pX", C("W2" + H, 64, 128), L("e8", 0, 8), 1))
         ts(sm(10), R("IX" + H), 6.0, ALU.is_le); ts(sm(11), R("IX" + H), 5.0, ALU.is_le)
-        act(sm(12), R("IX" + H), AF.Identity, 5.0); act(sm(13), R("IX" + H), AF.Identity, 5.0)
+        act(sm(12), R("IX" + H), AF.Identity, 5.0)
+
+    def clash(h, rnd):
+        H = str(h)
+        r = str(rnd)
+        hs = slice(128 * h, 128 * h + 128)
+        act(C("XA" + H, 0, 128), IN(XOw, C("ABU", 16 * h, 16 * h + 8)))
+        act(C("XA" + H, 128, 256), IN(XPw, C("ABU", 16 * h + 8, 16 * h + 16)))
+        bk = C("pE" + H, 0, 128)
+        mm([(bk, ID, C("XA" + H, 0, 128)), (bk, ID, C("XA" + H, 128, 256))])
+        act(R("MT" + H), bk, AF.Identity, MAGIC, 0.5 - 2.0 ** -11)
+        act(R("MID" + r, hs), R("MT" + H), AF.Identity, -MAGIC)
+        send([(cp, R("MIN" + r, hs), R("MID" + r, hs))], 300.0)
+        if h == 1:
+            send([(cp, R("AP" + r), C("ABU", 16, 24))], 100.0)
+        row = lambda k, a: C("ROW", 256 * h + 128 * k + a, 256 * h + 128 * k + 128)
+        cpy(C("ROW", 256 * h, 256 * h + 256), IN(R("IOT"), C("ABU", 16 * h, 16 * h + 16)))
+        ab, dm = C("AB", 16 * h, 16 * h + 16), C("KF", 1264 + 16 * h, 1280 + 16 * h)
+        ts(C("LS" + H, 0, 16), C("AS", 16 * h, 16 * h + 16), 0.5, ALU.is_lt)
+        tt(C("LS" + H, 0, 16), C("LS" + H, 0, 16), dm, ALU.mult)
+        ts(ab, C("AS", 16 * h, 16 * h + 16), -1.0, ALU.add)
+        tt(ab, ab, C("LS" + H, 0, 16), ALU.max)
+        pc_ = lambda a, b: C("pD" + H, a, b)
+        parts = [[(pc_(0, 128), ID, MASK)]]
+        for m in range(8 * h + 8):
+            part = []
+            for k, E in enumerate(("EA", "EB")):
+                sc = C("AS", 16 * (m // 8) + 8 * k + m % 8, 16 * (m // 8) + 8 * k + m % 8 + 1)
+                if m // 8 < h:
+                    e = R(E, m, slice(128 - 16 * m, 256 - 16 * m))
+                    ts(e, row(k, 0), sc, ALU.is_equal)
+                    part.append((pc_(0, 128), BO8, e))
+                else:
+                    a = 16 * (m % 8)
+                    ts(R(E, m, slice(0, 128 - a)), row(k, a), sc, ALU.is_equal)
+                    if a < 112:
+                        part.append((pc_(a + 16, 128), BO8, R(E, m, slice(16, 128 - a))))
+            if m % 2 == 0:
+                parts.append(part)
+            else:
+                parts[-1] += part
+        parts[-1] += [(pc_(0, 128), BOW, R(E, slice(8 * h, 8 * h + 8), slice(0, 16))) for E in ("EA", "EB")]
+        group(parts)
+        scan(R("CS" + H), VRS, pc_(0, 128), ALU.min, ALU.max)
+        ts(C("LS" + H, 16, 32), IN(R("CS" + H), L("c15", 0, 1)), pf(15), ALU.is_ge)
+        tt(C("LS" + H, 32, 48), C("LS" + H, 16, 32), dm, ALU.mult)
+        tt(R("LM", h), C("LS" + H, 32, 48), ab, ALU.max)
+        cpy(C("LW" + r, 16 * h, 16 * h + 16), R("LM", h))
+        send([(cp, C("LA" + r, 8 * h, 8 * h + 8), C("LW" + r, 16 * h, 16 * h + 8)),
+              (cq, C("LB" + r, 8 * h, 8 * h + 8), C("LW" + r, 16 * h + 8, 16 * h + 16))], 100.0)
+        cpy(IN(XO, C("LW" + r, 16 * h, 16 * h + 8)), R("MID" + r, hs))
 
     def merge(rnd):
         r = str(rnd)
-        cpy(R("ABU"), R("AB"))
-        act(C("XA", 0, 256), IN(XOw, C("ABU", 0, 16)))
-        act(C("XA", 256, 512), IN(XPw, C("ABU", 16, 32)))
-        bk = C("pM", 0, 256)
-        mm([(bk, ID, C("XA", 0, 256)), (bk, ID, C("XA", 256, 512))])
-        act(R("MT"), bk, AF.Identity, MAGIC, 0.5 - 2.0 ** -11)
-        act(R("MID" + r), R("MT"), AF.Identity, -MAGIC)
-        send([(cp, R("MIN" + r), R("MID" + r))], 1000.0)
-        cpy(R("ROW"), IN(R("IOT"), R("ABU")))
-        ts(R("AS"), R("AB"), 1.0, ALU.add)
-        for k in range(2):
-            tt(C("AS", 16 * k, 16 * k + 16), C("AS", 16 * k, 16 * k + 16), R("PRP"), ALU.mult)
-        act(C("LS", 0, 16), R("PRP"), AF.Identity, 1.0, -1.0)
-        for m in range(16):
-            for k, E in enumerate(("EA", "EB")):
-                ts(R(E, m, slice(0, 256 - 16 * m)), C("ROW", 256 * k + 16 * m, 256 * k + 256), C("AS", 16 * k + m, 16 * k + m + 1), ALU.is_equal)
-        items = [(C("pC", 0, 256), ID, MASK)]
-        for m in range(15):
-            for E in ("EA", "EB"):
-                items.append((C("pC", 16 * m + 16, 256), BO8, R(E, m, slice(16, 256 - 16 * m))))
-        for E in ("EA", "EB"):
-            items.append((C("pC", 0, 256), BOW, R(E, slice(None), slice(0, 16))))
-        cuts = [0, 5, 11, 19, 27, len(items)]
-        group([items[cuts[j]:cuts[j + 1]] for j in range(5)], C("pC", 0, 256))
-        scan(R("CS"), VRS, C("pC", 0, 256), ALU.min, ALU.max)
-        ts(C("LS", 16, 32), C("CS", 15, 256, 16), pf(15), ALU.is_ge)
-        tt(C("LS", 16, 32), C("LS", 16, 32), C("LS", 0, 16), ALU.max)
-        tt(C("LS", 32, 48), C("LS", 16, 32), DUMC, ALU.mult)
-        for k in range(2):
-            tt(C("LM", 16 * k, 16 * k + 16), C("LS", 32, 48), R("AB", k), ALU.max)
-        cpy(R("LW" + r), R("LM"))
-        send([(cp, R("LA" + r), C("LW" + r, 0, 16)), (cq, R("LB" + r), C("LW" + r, 16, 32))], 600.0)
-        cpy(IN(R("XO"), C("LW" + r, 0, 16)), R("MID" + r))
-        cpy(IN(R("XP"), R("LA" + r)), R("MIN" + r))
-        cpy(IN(R("XP"), C("LW" + r, 16, 32)), C("DK", 256, 512))
-        cpy(IN(R("XO"), R("LB" + r)), C("DK", 0, 256))
+        cpy(IN(XP, C("LA" + r, 0, 8)), C("MIN" + r, 0, 128))
+        for h in range(2):
+            cpy(IN(XP, C("LW" + r, 16 * h + 8, 16 * h + 16)), C("DK", 128, 256))
+        act(R("ZZ"), IN(XPw, R("AP" + r)), AF.Relu, -320.0, 1.25)
+        cpy(IN(XO, C("LB" + r, 0, 8)), C("DK", 0, 128))
+        tt(IN(XP, C("LA" + r, 8, 16)), C("MIN" + r, 128, 256), R("ZZ"), ALU.add)
+        cpy(IN(XO, C("LB" + r, 8, 16)), C("DK", 0, 128))
         if rnd < 2:
-            red(C("CT", 0, 1), C("LS", 16, 32))
-            mm([(C("pM", 256, 257), ONE, C("CT", 0, 1))])
-            ts(C("CTI", 0, 1), C("pM", 256, 257), -1.0, ALU.mult, 2048.0, ALU.add)
+            ts(C("CT", 8, 24), R("LM", slice(None), 0), float(DUM), ALU.is_lt)
+            red(C("CT", 0, 1), C("CT", 8, 24))
+            mm([(C("pE1", 256, 257), ONE, C("CT", 0, 1))])
+            cpy(C("CTI", 0, 1), C("pE1", 256, 257))
             ts(C("CTI", 1, 2), C("CTI", 0, 1), 31, ALU.bitwise_and)
             ts(C("CT", 1, 2), C("CTI", 1, 2), 2.0 ** -13, ALU.mult)
             ts(R("THR"), R("TH"), C("CT", 1, 2), ALU.add)
 
-    def hop(h, j, nv):
+    def hop(h, j):
         H = str(h)
-        cw, xe, xc = (R("CO"), XOw, XPw) if j % 2 == 0 else (R("CP"), XPw, XOw)
-        b0, nb = ((9, 6), (1, 7), (8, 6), (0, 7))[j]
-        act(R("CR" + H), IN(cw, R("EX" + H)))
+        cw, xe, xc = (R("CI"), XOw, XPw) if j % 2 == 0 else (R("CP"), XPw, XOw)
+        b0, nb = ((0, 6), (6, 7), (0, 5), (6, 6))[j]
+        cpy(R("OF" + H), IN(cw, R("EX" + H)))
+        ts(R("C16" + H), R("OF" + H), -2048.0, ALU.add)
         if j == 0:
-            act(R("W1" + H), IN(xe, R("EX" + H)), AF.Relu, 255.0, -1.0)
-            act(R("XE" + H), R("W1" + H), AF.Identity, 255.0, -1.0)
+            ts(R("XE" + H), IN(xe, R("EX" + H)), 255.0, ALU.min)
         else:
             act(R("XE" + H), IN(xe, R("EX" + H)))
-        tr(R("TT" + H), R("CR" + H))
-        cpy(R("OF" + H), IN(R("TT" + H), L("perm", 0, 8)))
-        act(R("CW" + H), IN(R("TT" + H), L("mi", 0, 8)))
-        IC = C("pD" + H, 128, 256)
-        mm([(IC, ID, ICB), (IC, IDF, R("CW" + H))])
-        bc = ("pM", "pC")[h]
-        for k in range(2):
-            mm([(C(bc, 128 * k, 128 * k + 128), IDF, R("CW" + H))])
-        for a, b in (([(9, 12), (12, 15)], [(1, 4), (4, 8)], [(8, 9)], [(0, 1)])[j]):
-            act(C("PP" + H, 128 * a, 128 * b), IN(C("PW" + H, 0, 128 if j < 2 else 144), L("on", 8 * a, 8 * b)))
-        z = 0
-        for p in range(8):
-            src = IN(xc, C("OF" + H, 16 * p, 16 * p + 16))
-            out = R("A" + H, slice(None), slice(4 * (p % 4) + p // 4, 4 * (p % 4) + 4, 2))
-            if (p * nv) % 8 < nv:
-                tt(R("D" + H, p), src, R("XE" + H), ALU.subtract)
-                act(out, R("D" + H, p), AF.Abs)
-            else:
-                act(R("D" + H, p), src)
-                bk = C(("pA", "pB")[z % 2] + H, 0, 256)
-                z += 1
-                mm([(bk, ID, R("D" + H, p)), (bk, NI, R("XE" + H))])
-                act(out, bk, AF.Abs)
-        for k in range(0, nb, 2):
-            e = min(2, nb - k)
-            tt(C("EQ" + H, 128 * k, 128 * (k + e)), C("PP" + H, 128 * (b0 + k), 128 * (b0 + k + e)), C(bc, 0, 128 * e), ALU.is_equal)
-        D = reduce_mm(H, [C("EQ" + H, 128 * k, 128 * k + 128) for k in range(nb)], [slice(0, 8)], [slice(0, 16, 2), slice(1, 16, 2)])
-        scan(R("R" + H), RST, D, ALU.max, ALU.min)
-        tt(R("NN" + H), D, R("R" + H), ALU.not_equal)
-        scan(R("PL" + H, 0), R("NN" + H), IC, ALU.mult, ALU.max)
-        cpy(R("TI" + H, 0), R("PL" + H, 0, slice(15, 128, 16)))
-        ts(R("TI" + H, 1), R("TI" + H, 0), 4095, ALU.bitwise_and)
+        gathers(H, xc, "OF" + H, HB, HV)
+        IC = C("pI" + H, 0, 128)
+        mm([(IC, R("C16" + H), ID)])
+        act(R("CW" + H), IC, AF.Identity, 2048.0)
+        mm([(IC, ID, K2), (IC, R("C16" + H), ID)], True, False)
+        mm([(C("pX" + H, d, 512, 4), ID, R("XE" + H)) for d in range(4)])
+        for a in range(0, nb, 4):
+            e = min(4, nb - a)
+            mm([(C("pE" + H, 0, 128 * e), R("PB" + H), R("EK", slice(b0 + a, b0 + a + e)))])
+            for k in range(e):
+                tt(R("EQ" + H, a + k), R("CW" + H), C("pE" + H, 128 * k, 128 * k + 128), ALU.is_equal)
+        if j > 1:
+            tt(R("EQ" + H, nb), IN(C("PL" + H, 128 * j - 256, 128 * j - 128), L("e16", 0, 8)), R("CW" + H), ALU.is_equal)
+            nb += 1
+        a = 0
+        for m in HB:
+            for q in range(4):
+                tt(C("A" + H, 16 * a + q, 16 * (a + m), 4), C("D" + H, 16 * a + q, 16 * (a + m), 4), C("pX" + H, 4 * a, 4 * (a + m)), ALU.max)
+            a += m
+        D = C("pD" + H, 0, 128)
+        col = lambda i: C("pD" + H, i, 128, 16)
+        group([[(D, ID, ICON)] + [(D, PEN, R("EQ" + H, k)) for k in range(nb)], [(col(i), C("D" + H, i, 2048, 16), SELN) for i in range(16)]] +
+              [[(col(i), C("A" + H, i, 2048, 16), SEL2) for i in range(q, 16, 4)] for q in range(4)])
+        scan(R("R" + H, j), RST, D, ALU.max, ALU.min)
+        tt(R("NN" + H), D, R("R" + H, j), ALU.not_equal)
+        mm([(IC, N4, R("NN" + H))], False, True)
+        pl = C("PL" + H, 128 * j, 128 * j + 128)
+        scan(pl, R("NN" + H), IC, ALU.mult, ALU.max)
         if j < 3:
-            for d in range(2):
-                cpy(C("EX" + H, d, 16, 2), R("TI" + H, 1))
-        c = (136, 128, 152, 144)[j]
-        cpy(C("PW" + H, c, c + 8), R("TI" + H, 1))
-        c = (0, 16, 8, 24)[j]
-        ts(C("FD" + H, c, c + 8), C("R" + H, 15, 128, 16), 0.0625, ALU.is_lt)
+            cpy(R("EX" + H), spread(H, "pI", pl, L("e16", 0, 8), 1))
 
-    def append(h):
+    def append(h, q):
         H = str(h)
         PW = "PW" + H
-        gg = lambda a, b: C("SM" + H, 112 + a, 112 + b)
-        tt(gg(0, 16), C("FD" + H, 0, 16), C("FD" + H, 16, 32), ALU.mult)
-        tt(gg(0, 16), gg(0, 16), C("SM" + H, 80, 96), ALU.mult)
-        tt(gg(8, 16), gg(8, 16), gg(0, 8), ALU.mult)
-        tt(R("IG" + H), gg(0, 16), C("SM" + H, 96, 112), ALU.mult)
-        tt(R("FL" + H), IN(R("IG" + H), L("r8", 0, 16)), CAP, ALU.not_equal)
-        act(R("W3" + H), IN(R(PW), L("val", 0, 16)))
-        bk = C("pA" + H, 0, 256)
-        mm([(bk, IDF, R("W3" + H)), (bk, SI, R("FL" + H))])
-        for k in range(2):
-            tt(C(PW, 0, 128), C(PW, 0, 128), C("pA" + H, 128 * k, 128 * k + 128), ALU.min)
-        tt(gg(16, 24), gg(0, 8), gg(8, 16), ALU.add)
-        tt(R("IX" + H), R("IX" + H), gg(16, 24), ALU.add)
+        sm = lambda k: C("SM" + H, 8 * k, 8 * k + 8)
+        ts(R("FD" + H), R("R" + H, slice(2 * q, 2 * q + 2), slice(15, 128, 16)), 0.125, ALU.is_lt)
+        tt(sm(13), R("FD" + H, 0), sm(10 + q), ALU.mult)
+        tt(sm(14), R("FD" + H, 1), sm(13), ALU.mult)
+        tt(sm(15), sm(14), sm(12), ALU.mult)
+        tt(C("FL" + H, 0, 128), IN(sm(15), L("r16", 0, 8)), C("KF", 960 + 128 * q, 1088 + 128 * q), ALU.not_equal)
+        act(C("W3" + H, 0, 128), IN(C("PL" + H, 256 * q, 256 * q + 256), L("val", 0, 8)))
+        bk = C("pX" + H, 0, 128)
+        mm([(bk, SI, C("FL" + H, 0, 128)), (bk, IDF, C("W3" + H, 0, 128))])
+        tt(C(PW, 0, 128), C(PW, 0, 128), bk, ALU.min)
+        tt(R("IX" + H), R("IX" + H), sm(14), ALU.add)
+        if q == 0:
+            tt(sm(11), sm(11), sm(14), ALU.mult)
 
-    t = 0
     for rnd in range(3):
         for h in range(2):
             cur[0] = BIAS * (1 - h)
             edges(h, rnd)
         cur[0] = 0.0
+        for h in range(2):
+            clash(h, rnd)
         merge(rnd)
         if rnd == 2:
             for k in range(2):
                 c = C("YX", 1856 * k, 1856 * (k + 1))
                 for a in range(1856 * k, 1856 * (k + 1), 464):
-                    ts(C("YX", a, a + 464), C("XO", a, a + 464), 255.0, ALU.min)
+                    ts(C("YX", a, a + 464), C("X", a, a + 464), 255.0, ALU.min)
                 dma("Y", T.yx[:, 1856 * k:1856 * (k + 1)], c["ap"], [], [c], 6000.0)
         for h in range(2):
             cur[0] = BIAS * (1 - h)
             for j in range(4):
-                hop(h, j, NV[(t + h) % len(NV)])
-                t += 1
-            append(h)
+                hop(h, j)
+                if j % 2 == 1:
+                    append(h, j // 2)
     for h in range(2):
         cur[0] = BIAS * (1 - h)
         H = str(h)
+        hs = slice(128 * h, 128 * h + 128)
         ts(C("W2" + H, 0, 128), C("PW" + H, 0, 128), SENT, ALU.is_lt)
-        tt(C("PZ" + H, 0, 128), C("PW" + H, 0, 128), C("W2" + H, 0, 128), ALU.mult)
-        ts(C("PZ" + H, 128, 136), R("IX" + H), 2.0, ALU.mult, 1.0, ALU.add)
-        cpy(R("W1" + H), IN(R("PZ" + H), L("out", 0, 16)))
-        tr(R("TT" + H), R("W1" + H))
-        act(R("YC", 0, slice(128 * h, 128 * h + 128)), IN(R("TT" + H), L("mi", 0, 8)))
-        cpy(R("YC", 1, slice(128 * h, 128 * h + 128)), IN(R("TT" + H), L("sib", 0, 8)))
-        dma("S", T.yw[:, 128 * h:128 * h + 128], T.YC[:, 0, 128 * h:128 * h + 128], [], [R("YC", 0, slice(128 * h, 128 * h + 128))], 2200.0)
-    dma("Y", T.yn[0::2, :], T.YC[16::32, 1, :], [], [R("YC", 1)], 2000.0)
-    dma("Y", T.yn[1::2, :], T.YC[0::32, 1, :], [], [R("YC", 1)], 2000.0)
+        tt(C("W2" + H, 128, 256), C("PW" + H, 0, 128), C("W2" + H, 0, 128), ALU.mult)
+        ts(C("W3" + H, 0, 8), R("IX" + H), 2.0, ALU.mult, 1.0, ALU.add)
+        mm([(C("pI" + H, 0, 128), C("W2" + H, 128, 256), IDF)])
+        mm([(C("pI" + H, 128, 256, p=lo8), C("W3" + H, 0, 8), IDF)])
+        act(R("YC", hs), C("pI" + H, 0, 128))
+        act(R("YN", hs, p=lo8), C("pI" + H, 128, 256, p=lo8))
+        dma("S", T.yw[:, hs], T.YC[:, hs], [], [R("YC", hs)], 2200.0)
+        dma("Y", T.yn[:, hs], T.YN[0:8, hs], [], [R("YN", hs)], 2000.0)
     return ops
-
-
-_sb("LT", [40], U)
 
 
 def order(ops):

@@ -7,11 +7,14 @@ DUM = 3728
 XW = DUM + 256
 DEAD_O, DEAD_P = 3584.0, 1280.0
 MAGIC = 12582912.0
-HB = (48, 48, 32)
+HB = (32, 32, 32, 32)
 HV = ()
-EB = (64, 64)
-EV = ((1,), (), ())
+EB = (32, 32, 32, 32)
+EV = (((0, 2), (0, 2)), ((0, 2), (0, 2)))
+SH = ((32, 32, 32, 32), (32, 32, 32, 32))
 PENAT = 1
+SHAKES, SHAKE, SLACK, SPAN = 1200, 1000.0, 1.0, 2500.0
+BIASE = 2500.0
 BIAS = 2500.0
 LAT = 120.0
 PE = 0.55
@@ -23,6 +26,7 @@ NX, NC = 4, 2
 
 F, B, I, U, H16 = "float32", "bfloat16", "int32", "uint16", "float16"
 SCRATCH = {}
+PLAN = []
 
 
 def _sb(name, shape, dt):
@@ -30,24 +34,24 @@ def _sb(name, shape, dt):
 
 
 for _n, _s, _d in [
-    ("X", [2 * XW], B), ("CI", [V], I), ("CP", [V], F), ("CU", [V], U), ("CN", [V], U),
-    ("IOT", [3840], F), ("YX", [V], B), ("WI", [256], I), ("WF", [256], F), ("ZI", [512], I), ("ZF", [512], F),
-    ("PC", [16], I), ("PF", [24], F), ("XI", [128], F), ("MB", [8, 128], B), ("MF", [2, 128], F), ("SEL", [24], B),
+    ("X", [2 * XW], F), ("XB", [V], B), ("XR", [V], B), ("CI", [V], I), ("CP", [V], F), ("CU", [V], U), ("CN", [V], U),
+    ("IOT", [3840], F), ("WI", [256], I), ("WF", [256], F), ("ZI", [512], I), ("ZF", [512], F),
+    ("PC", [16], I), ("PF", [24], F), ("XI", [128], F), ("MB", [11, 128], B), ("MF", [2, 128], F), ("SEL", [24], B),
     ("KF", [1792], F), ("KB", [768], B), ("EK", [13, 128], B), ("SAB", [256], B),
     ("LI", [128], I), ("LF", [128], F), ("LU", [128], U), ("TM", [80], F),
     ("TH", [16], F), ("THR", [16], F), ("ABU", [32], U), ("AS", [32], F), ("AB", [32], F),
     ("ROW", [512], U), ("EA", [16, 256], B), ("EB", [16, 256], B), ("LM", [2, 2, 8], F),
-    ("DK", [256], B), ("CT", [24], F), ("CTI", [8], I), ("YC", [256], F), ("YN", [256], F), ("ZZ", [128], B),
+    ("DK", [256], F), ("CT", [24], F), ("CTI", [8], I), ("YC", [256], F), ("YN", [256], F), ("ZZ", [128], F), ("NP", [16], B),
 ]:
     _sb(_n, _s, _d)
 for _r in range(3):
-    _sb("MID%d" % _r, [256], B); _sb("MIN%d" % _r, [256], B)
+    _sb("MID%d" % _r, [256], F); _sb("MIN%d" % _r, [256], F)
     _sb("LW%d" % _r, [32], U); _sb("LA%d" % _r, [16], U); _sb("LB%d" % _r, [16], U); _sb("AP%d" % _r, [8], U)
 for _h in range(2):
     for _n, _s, _d in [
-        ("PW", [144], F), ("LP", [128], U), ("PA", [128], H16), ("PB", [128], H16), ("D", [2048], B), ("A", [2048], B),
-        ("R", [4, 128], F), ("PL", [512], F), ("NN", [128], B), ("W1", [256], F), ("W2", [256], F), ("W3", [256], F),
-        ("SM", [176], F), ("IX", [8], F), ("TS", [16], F), ("OH", [48], F), ("PR", [5, 128], F), ("FL", [256], B),
+        ("PW", [144], H16), ("LP", [128], U), ("PA", [128], H16), ("PB", [128], H16), ("D", [2048], B), ("A", [2048], B),
+        ("R", [4, 128], F), ("PL", [512], F), ("NN", [128], B), ("W2", [256], F), ("W3", [256], F),
+        ("SM", [176], F), ("IX", [8], F), ("TS", [16], F), ("OH", [48], B), ("PR", [5, 128], H16), ("FL", [128], B),
         ("EX", [8], U), ("OF", [128], U), ("C16", [128], H16), ("CW", [128], F), ("XE", [128], B), ("WX", [256], F),
         ("EQ", [7, 128], B), ("FD", [2, 8], F), ("XA", [256], B), ("MT", [128], F), ("CS", [128], F), ("LS", [48], F),
     ]:
@@ -138,9 +142,13 @@ def build(g, core, T, topo):
     def ms(out, val):
         return add("V", max(64, out["n"] * (0.5 if out["dt"] == B else 1)), lambda q: q.memset(out["ap"], val), [out], [])
 
-    def act(out, in0, func=AF.Identity, bias=0.0, scale=1.0):
+    def act(out, in0, func=AF.Identity, bias=0.0, scale=1.0, acc=None):
         cost = 80 + 1.56 * in0["n"] if in0["ind"] else 40 + max(64, in0["n"])
-        return add("S", cost, lambda q: q.activation(out["ap"], in0["ap"], func, bias=bias, scale=scale), [out], [in0])
+        if out["ind"]:
+            return add("S", 80 + 3.8 * in0["n"], lambda q: q.activation(out["ap"], in0["ap"], func), [out], [in0])
+        if acc:
+            return add("S", cost, lambda q: q.activation(out["ap"], in0["ap"], func, bias=bias, scale=scale, accum_out=acc["ap"]), [out, acc], [in0])
+        return add("S", cost, lambda q: q.activation(out["ap"], in0["ap"], func, bias=ap(bias), scale=scale), [out], [in0, bias])
 
     def mm(items, first=True, last=True):
         def fn(q):
@@ -201,14 +209,17 @@ def build(g, core, T, topo):
 
     w = V // NX
     for k in range(NX):
-        c = C("X", k * w, (k + 1) * w)
+        c = C("XB", k * w, (k + 1) * w)
         dma("Y", c["ap"], T.pts[:, k * w:(k + 1) * w], [c], [], 2200.0 + 1300 * k)
+        act(C("X", k * w, (k + 1) * w), c)
     lo8 = slice(0, 8)
     dma("S", T.WI[:], T.way[:], [R("WI")], [], 3000.0)
     dma("S", T.ZI[0:8, 0:256], T.cnt[:], [C("ZI", 0, 256)], [], 2500.0)
     dma("S", T.ZI[0:8, 256:512], T.th[:], [C("ZI", 256, 512)], [], 2500.0)
     for k in range(NX):
-        send([(cp, C("X", XW + k * w, XW + (k + 1) * w), C("X", k * w, (k + 1) * w))], 3600.0)
+        send([(cp, C("XR", k * w, (k + 1) * w), C("XB", k * w, (k + 1) * w))], 3600.0)
+        for a, f in ((k * w, act), (k * w + w // 2, cpy)):
+            f(C("X", XW + a, XW + a + w // 2), C("XR", a, a + w // 2))
     w = V // NC
     for k in range(NC):
         c = C("CI", k * w, (k + 1) * w)
@@ -235,13 +246,15 @@ def build(g, core, T, topo):
     tt(pf(9), pf(9), pf(8), ALU.add)
     ts(pf(10), pf(2), -128.0, ALU.mult)
     ts(pf(11), pf(4), 16.0, ALU.mult)
+    ts(pf(12), pf(5), 2048.0, ALU.add)
+    ts(pf(13), pf(7), 2048.0, ALU.add)
     iota(R("XI"), [[1, 128]])
     x128 = R("XI")
-    ID, NI, PEN, SI, BO8, BOW, N4, GEQ = [R("MB", k) for k in range(8)]
+    ID, NI, PEN, SI, BO8, BOW, N4, GEQ, NS, BI = [R("MB", k) for k in range(10)]
     IDF, ONE = R("MF", 0), R("MF", 1)
     ts(IDF, x128, pf(0), ALU.is_equal)
     cpy(ID, IDF)
-    for o, x in ((NI, -1.0), (PEN, 0.125), (SI, SENT), (N4, -4096.0)):
+    for o, x in ((NI, -1.0), (PEN, 0.125), (SI, SENT), (N4, -4096.0), (NS, -SENT), (BI, 131072.0)):
         ts(o, ID, x, ALU.mult)
     ms(ONE, 1.0)
     SEL1, SEL2, SELN = C("SEL", 0, 8), C("SEL", 8, 16), C("SEL", 16, 24)
@@ -268,6 +281,7 @@ def build(g, core, T, topo):
     k128 = C("KF", 0, 128)
     ts(GEQ, C("KB", 640, 768), pf(3), ALU.is_equal)
     ts(BO8, GEQ, 8.0, ALU.mult)
+    ts(R("MB", 10), GEQ, 2.0 ** -15, ALU.mult)
     ts(BOW, GEQ, pf(14), ALU.mult)
     ts(SM8, C("XI", 0, 8), pf(3), ALU.is_equal)
     ts(RST, k128, 0.0, ALU.is_equal, 4.0, ALU.mult)
@@ -283,6 +297,7 @@ def build(g, core, T, topo):
     ms(C("KB", 143, 256, 16), 0.0)
     act(KH1, k128, AF.Identity, 1.0, 0.5)
     ms(C("KF", 1647, 1760, 16), -1.0)
+    ms(C("KF", 975, 1216, 16), -1.0)
     act(MASK, C("KF", 512, 640), AF.Identity, -65536.0, 65536.0)
     ms(K2, 2048.0)
     ts(C("TM", 64, 77), C("TM", 64, 77), pf(1), ALU.is_equal, pf(6), ALU.add)
@@ -321,18 +336,18 @@ def build(g, core, T, topo):
 
     XOw, XPw, XO, XP = C("X", 0, DUM), C("X", XW, XW + DUM), C("X", 0, XW), C("X", XW, 2 * XW)
 
-    cpy(R("WF"), R("WI"))
+    ts(R("WF"), R("WI"), -2048.0, ALU.add)
     cpy(R("ZF", p=lo8), R("ZI", p=lo8))
     for h in range(2):
         H = str(h)
-        ms(C("PW" + H, 128, 144), 0.0)
+        ts(C("PW" + H, 128, 144), C("XI", 0, 16), 0.0, ALU.mult)
         mm([(C("pI" + H, 0, 128), C("WF", 128 * h, 128 * h + 128), IDF)])
         for k in range(2):
             mm([(C("pI" + H, 128 + 8 * k, 136 + 8 * k), C("ZF", 256 * k + 128 * h, 256 * k + 128 * h + 128, p=lo8), R("MF", 0, slice(0, 8), p=lo8))])
         ts(R("IX" + H), C("pI" + H, 128, 136), 0.5, ALU.mult, -0.5, ALU.add)
         ts(C("TH", 8 * h, 8 * h + 8), C("pI" + H, 136, 144), 2.0 ** -16, ALU.mult)
         tt(C("W3" + H, 0, 128), IN(R("IX" + H), L("r16", 0, 8)), KH, ALU.is_lt)
-        ts(C("W3" + H, 0, 128), C("W3" + H, 0, 128), SENT, ALU.mult)
+        act(C("W3" + H, 0, 128), C("W3" + H, 0, 128), AF.Identity, -2048.0, SENT)
         tt(C("PW" + H, 0, 128), C("W3" + H, 0, 128), C("pI" + H, 0, 128), ALU.max)
     for a in range(0, V, 464):
         cpy(C("CP", a, a + 464), C("CN", a, a + 464))
@@ -354,12 +369,12 @@ def build(g, core, T, topo):
         PW = "PW" + H
         sm = lambda k: C("SM" + H, 8 * k, 8 * k + 8)
         R0 = R("R" + H, 0)
-        mm([(C("pI" + H, 0, 128), C(PW, 0, 128), IDF)])
-        ts(R("LP" + H), C("pI" + H, 0, 128), pf(5), ALU.add)
+        mm([(C("pI" + H, 0, 128), C(PW, 0, 128), ID)])
+        ts(R("LP" + H), C("pI" + H, 0, 128), pf(12), ALU.add)
         ts(R("PA" + H), R("LP" + H), pf(9), ALU.add)
         if rnd == 0:
             ts(R("PB" + H), R("LP" + H), pf(8), ALU.add)
-        gathers(H, R("X"), "LP" + H, EB, EV[rnd])
+        gathers(H, R("X"), "LP" + H, EB, EV[rnd > 0][h])
         mm([(C("pI" + H, 128, 384), R("PA" + H), R("SAB"))], True, False)
         D = C("pD" + H, 0, 128)
         parts = [[(D, ID, ICE), (C("pD" + H, 15, 128, 16), IDF, C("TH" if rnd == 0 else "THR", 8 * h, 8 * h + 8))]]
@@ -371,7 +386,7 @@ def build(g, core, T, topo):
             scan(C("W3" + H, 64, 128), KP8, C("W2" + H, 128, 256, 2), ALU.mult, ALU.add)
             No, Ne = C("W3" + H, 7, 64, 8), C("W3" + H, 71, 128, 8)
             tt(sm(1), R("IX" + H), No, ALU.subtract)
-            ts(sm(6), No, 1.0, ALU.add)
+            act(sm(6), No, AF.Identity, 1.0)
             tt(sm(4), sm(1), Ne, ALU.is_gt)
             tt(sm(2), sm(1), Ne, ALU.max)
             tt(C("TS" + H, 0, 8), sm(6), sm(4), ALU.mult)
@@ -397,23 +412,25 @@ def build(g, core, T, topo):
         if rnd > 0:
             act(R("IX" + H), sm(2), AF.Relu, -1.0)
             ts(sm(8), sm(2), 0.5, ALU.is_lt)
-            ts(sm(9), C(PW, 0, 128, 16), float(V - 97), ALU.is_ge, -float(V), ALU.mult)
+            ts(sm(9), C(PW, 0, 128, 16), float(V - 97 - 2048), ALU.is_ge, -float(V), ALU.mult)
             act(sm(9), sm(9), AF.Identity, 97.0)
             tt(sm(9), sm(9), sm(8), ALU.mult)
             tt(R("OH" + H), IN(C("TS" + H, 0, 8), L("oh", 0, 3)), COH, ALU.is_equal)
+            act(C("OH" + H, 40, 48), sm(2), AF.Relu, -1.0)
+            mm([(C("pX" + H, k, 512, 16), ID, C("OH" + H, 0, 32)) for k in range(16)])
+            mm([(C("pE" + H, k, 256, 16), ID, C("OH" + H, 32, 48)) for k in range(16)])
             for t in range(5):
-                tt(R("PR" + H, t), IN(R("OH" + H), L("r16", 8 * t, 8 * t + 8)), C(PW, 2 * t, 2 * t + 128), ALU.mult)
-            tt(C("FL" + H, 0, 128), IN(R("IX" + H), L("r16", 0, 8)), KH, ALU.is_lt)
+                tt(R("PR" + H, t), C(PW, 2 * t, 2 * t + 128), C("pX" + H, 128 * t, 128 * t + 128) if t < 4 else C("pE" + H, 0, 128), ALU.mult)
+            tt(R("FL" + H), KH, C("pE" + H, 128, 256), ALU.is_gt)
             bk = C("pX" + H, 0, 128)
-            mm([(bk, SI, C("FL" + H, 0, 128))] + [(bk, IDF, R("PR" + H, t)) for t in range(5)])
-            ts(C(PW, 0, 128), bk, SENT, ALU.min)
+            mm([(bk, SI, R("FL" + H))] + [(bk, ID, R("PR" + H, t)) for t in range(5)])
+            ts(C(PW, 0, 128), bk, SENT - 2048.0, ALU.min)
             tt(C(PW, 0, 128, 16), C(PW, 0, 128, 16), sm(9), ALU.add)
-            mm([(C("pX" + H, 128, 256), C(PW, 0, 128), IDF)])
-            ts(R("PB" + H), C("pX" + H, 128, 256), pf(7), ALU.add)
-        ts(C("W2" + H, 0, 64), C(PW, 0, 128, 2), SENT, ALU.is_lt, 8192.0, ALU.mult)
-        scan(C("W2" + H, 64, 128), C("W2" + H, 0, 64), C(PW, 0, 128, 2), ALU.max, ALU.min)
-        cpy(R("EX" + H), spread(H, "pX", C("W2" + H, 64, 128), L("e8", 0, 8), 1))
-        ts(sm(10), R("IX" + H), 6.0, ALU.is_le); ts(sm(11), R("IX" + H), 5.0, ALU.is_le)
+            mm([(C("pX" + H, 128, 256), C(PW, 0, 128), ID)])
+            ts(R("PB" + H), C("pX" + H, 128, 256), pf(13), ALU.add)
+        ts(C("W2" + H, 0, 64), C(PW, 0, 128, 2), SENT - 2048.0, ALU.is_lt, 8192.0, ALU.mult)
+        scan(C("W2" + H, 64, 128), C("W2" + H, 0, 64), C(PW, 0, 128, 2), ALU.add, ALU.min)
+        ts(R("EX" + H), spread(H, "pX", C("W2" + H, 64, 128), L("e8", 0, 8), 1), 2048.0, ALU.add)
         act(sm(12), R("IX" + H), AF.Identity, 5.0)
 
     def clash(h, rnd):
@@ -432,12 +449,10 @@ def build(g, core, T, topo):
         row = lambda k, a: C("ROW", 256 * h + 128 * k + a, 256 * h + 128 * k + 128)
         cpy(C("ROW", 256 * h, 256 * h + 256), IN(R("IOT"), C("ABU", 16 * h, 16 * h + 16)))
         ab, dm = C("AB", 16 * h, 16 * h + 16), C("KF", 1264 + 16 * h, 1280 + 16 * h)
-        ts(C("LS" + H, 0, 16), C("AS", 16 * h, 16 * h + 16), 0.5, ALU.is_lt)
-        tt(C("LS" + H, 0, 16), C("LS" + H, 0, 16), dm, ALU.mult)
-        ts(ab, C("AS", 16 * h, 16 * h + 16), -1.0, ALU.add)
-        tt(ab, ab, C("LS" + H, 0, 16), ALU.max)
+        act(ab, C("AS", 16 * h, 16 * h + 16), AF.Identity, -1.0)
+        act(C("NP", 8 * h, 8 * h + 8), C("AS", 16 * h, 16 * h + 8), AF.Relu, 1.0, -1.0)
         pc_ = lambda a, b: C("pD" + H, a, b)
-        parts = [[(pc_(0, 128), ID, MASK)]]
+        parts = [[(pc_(0, 128), ID, MASK), (C("pD" + H, 0, 128, 16), BI, C("NP", 8 * h, 8 * h + 8))]]
         for m in range(8 * h + 8):
             part = []
             for k, E in enumerate(("EA", "EB")):
@@ -464,25 +479,24 @@ def build(g, core, T, topo):
         cpy(C("LW" + r, 16 * h, 16 * h + 16), R("LM", h))
         send([(cp, C("LA" + r, 8 * h, 8 * h + 8), C("LW" + r, 16 * h, 16 * h + 8)),
               (cq, C("LB" + r, 8 * h, 8 * h + 8), C("LW" + r, 16 * h + 8, 16 * h + 16))], 100.0)
-        cpy(IN(XO, C("LW" + r, 16 * h, 16 * h + 8)), R("MID" + r, hs))
 
     def merge(rnd):
         r = str(rnd)
         cpy(IN(XP, C("LA" + r, 0, 8)), C("MIN" + r, 0, 128))
         for h in range(2):
-            cpy(IN(XP, C("LW" + r, 16 * h + 8, 16 * h + 16)), C("DK", 128, 256))
+            cpy(IN(XO, C("LW" + r, 16 * h, 16 * h + 8)), C("MID" + r, 128 * h, 128 * h + 128))
+            act(IN(XP, C("LW" + r, 16 * h + 8, 16 * h + 16)), C("DK", 128, 256), AF.Silu)
         act(R("ZZ"), IN(XPw, R("AP" + r)), AF.Relu, -320.0, 1.25)
-        cpy(IN(XO, C("LB" + r, 0, 8)), C("DK", 0, 128))
-        tt(IN(XP, C("LA" + r, 8, 16)), C("MIN" + r, 128, 256), R("ZZ"), ALU.add)
-        cpy(IN(XO, C("LB" + r, 8, 16)), C("DK", 0, 128))
+        tt(IN(XP, C("LA" + r, 8, 16)), C("MIN" + r, 128, 256), R("ZZ"), ALU.max)
+        for h in range(2):
+            act(IN(XO, C("LB" + r, 8 * h, 8 * h + 8)), C("DK", 0, 128), AF.Silu)
         if rnd < 2:
-            ts(C("CT", 8, 24), R("LM", slice(None), 0), float(DUM), ALU.is_lt)
-            red(C("CT", 0, 1), C("CT", 8, 24))
+            act(C("CT", 8, 24), R("LM", slice(None), 0), AF.Sign, DUM - 0.5, -1.0, C("CT", 0, 1))
             mm([(C("pE1", 256, 257), ONE, C("CT", 0, 1))])
-            cpy(C("CTI", 0, 1), C("pE1", 256, 257))
+            ts(C("CTI", 0, 1), C("pE1", 256, 257), 0.5, ALU.mult, 1024.0, ALU.add)
             ts(C("CTI", 1, 2), C("CTI", 0, 1), 31, ALU.bitwise_and)
             ts(C("CT", 1, 2), C("CTI", 1, 2), 2.0 ** -13, ALU.mult)
-            ts(R("THR"), R("TH"), C("CT", 1, 2), ALU.add)
+            act(R("THR"), R("TH"), AF.Identity, C("CT", 1, 2))
 
     def hop(h, j):
         H = str(h)
@@ -508,14 +522,21 @@ def build(g, core, T, topo):
         if j > 1:
             tt(R("EQ" + H, nb), IN(C("PL" + H, 128 * j - 256, 128 * j - 128), L("e16", 0, 8)), R("CW" + H), ALU.is_equal)
             nb += 1
+        ns = SH[h][j]
+        fix = []
+        if ns:
+            mm([(C("pE" + H, 0, 8 * ns), ID, C("D" + H, 0, 16 * ns, 2))] + [(C("pE" + H, d, 8 * ns, 8), NI, C("XE" + H, 0, ns)) for d in range(8)])
+            act(C("A" + H, 0, 16 * ns, 2), C("pE" + H, 0, 8 * ns), AF.Relu)
+            fix = [(C("pD" + H, 0, 128, 2, p=slice(0, ns)), C("XE" + H, 0, ns), R("MB", 10, slice(0, 128, 2)))]
         a = 0
         for m in HB:
             for q in range(4):
-                tt(C("A" + H, 16 * a + q, 16 * (a + m), 4), C("D" + H, 16 * a + q, 16 * (a + m), 4), C("pX" + H, 4 * a, 4 * (a + m)), ALU.max)
+                if a + m > ns or q % 2:
+                    tt(C("A" + H, 16 * a + q, 16 * (a + m), 4), C("D" + H, 16 * a + q, 16 * (a + m), 4), C("pX" + H, 4 * a, 4 * (a + m)), ALU.max)
             a += m
         D = C("pD" + H, 0, 128)
         col = lambda i: C("pD" + H, i, 128, 16)
-        group([[(D, ID, ICON)] + [(D, PEN, R("EQ" + H, k)) for k in range(nb)], [(col(i), C("D" + H, i, 2048, 16), SELN) for i in range(16)]] +
+        group([[(D, ID, ICON)] + fix + [(D, PEN, R("EQ" + H, k)) for k in range(nb)], [(col(i), C("D" + H, i, 2048, 16), SELN) for i in range(16)]] +
               [[(col(i), C("A" + H, i, 2048, 16), SEL2) for i in range(q, 16, 4)] for q in range(4)])
         scan(R("R" + H, j), RST, D, ALU.max, ALU.min)
         tt(R("NN" + H), D, R("R" + H, j), ALU.not_equal)
@@ -530,21 +551,22 @@ def build(g, core, T, topo):
         PW = "PW" + H
         sm = lambda k: C("SM" + H, 8 * k, 8 * k + 8)
         ts(R("FD" + H), R("R" + H, slice(2 * q, 2 * q + 2), slice(15, 128, 16)), 0.125, ALU.is_lt)
-        tt(sm(13), R("FD" + H, 0), sm(10 + q), ALU.mult)
-        tt(sm(14), R("FD" + H, 1), sm(13), ALU.mult)
-        tt(sm(15), sm(14), sm(12), ALU.mult)
-        tt(C("FL" + H, 0, 128), IN(sm(15), L("r16", 0, 8)), C("KF", 960 + 128 * q, 1088 + 128 * q), ALU.not_equal)
-        act(C("W3" + H, 0, 128), IN(C("PL" + H, 256 * q, 256 * q + 256), L("val", 0, 8)))
+        tt(sm(13 + q), R("FD" + H, 0), R("FD" + H, 1), ALU.mult)
+        if q == 1:
+            tt(sm(14), sm(14), sm(13), ALU.mult)
+        tt(sm(15), sm(13 + q), sm(12), ALU.mult)
+        tt(R("FL" + H), IN(sm(15), L("r16", 0, 8)), C("KF", 960 + 128 * q, 1088 + 128 * q), ALU.not_equal)
+        act(C("W3" + H, 0, 128), IN(C("PL" + H, 256 * q, 256 * q + 256), L("val", 0, 8)), AF.Identity, -2048.0)
         bk = C("pX" + H, 0, 128)
-        mm([(bk, SI, C("FL" + H, 0, 128)), (bk, IDF, C("W3" + H, 0, 128))])
+        mm([(bk, SI, R("FL" + H)), (bk, IDF, C("W3" + H, 0, 128))])
         tt(C(PW, 0, 128), C(PW, 0, 128), bk, ALU.min)
-        tt(R("IX" + H), R("IX" + H), sm(14), ALU.add)
-        if q == 0:
-            tt(sm(11), sm(11), sm(14), ALU.mult)
+        tt(R("IX" + H), R("IX" + H), sm(13 + q), ALU.add)
+        if q == 1:
+            ts(R("IX" + H), R("IX" + H), 7.0, ALU.min)
 
     for rnd in range(3):
         for h in range(2):
-            cur[0] = BIAS * (1 - h)
+            cur[0] = BIASE * (1 - h)
             edges(h, rnd)
         cur[0] = 0.0
         for h in range(2):
@@ -552,9 +574,11 @@ def build(g, core, T, topo):
         merge(rnd)
         if rnd == 2:
             for k in range(2):
-                c = C("YX", 1856 * k, 1856 * (k + 1))
+                c = C("XB", 1856 * k, 1856 * (k + 1))
+                x = C("X", 1856 * k, 1856 * (k + 1))
+                dma("G", c["ap"], x["ap"], [c], [x], 5000.0)
                 for a in range(1856 * k, 1856 * (k + 1), 464):
-                    ts(C("YX", a, a + 464), C("X", a, a + 464), 255.0, ALU.min)
+                    ts(C("XB", a, a + 464), C("XB", a, a + 464), 255.0, ALU.min)
                 dma("Y", T.yx[:, 1856 * k:1856 * (k + 1)], c["ap"], [], [c], 6000.0)
         for h in range(2):
             cur[0] = BIAS * (1 - h)
@@ -566,13 +590,12 @@ def build(g, core, T, topo):
         cur[0] = BIAS * (1 - h)
         H = str(h)
         hs = slice(128 * h, 128 * h + 128)
-        ts(C("W2" + H, 0, 128), C("PW" + H, 0, 128), SENT, ALU.is_lt)
-        tt(C("W2" + H, 128, 256), C("PW" + H, 0, 128), C("W2" + H, 0, 128), ALU.mult)
-        ts(C("W3" + H, 0, 8), R("IX" + H), 2.0, ALU.mult, 1.0, ALU.add)
-        mm([(C("pI" + H, 0, 128), C("W2" + H, 128, 256), IDF)])
-        mm([(C("pI" + H, 128, 256, p=lo8), C("W3" + H, 0, 8), IDF)])
-        act(R("YC", hs), C("pI" + H, 0, 128))
-        act(R("YN", hs, p=lo8), C("pI" + H, 128, 256, p=lo8))
+        ts(R("FL" + H), C("PW" + H, 0, 128), SENT - 2048.0, ALU.is_ge)
+        ts(C("OH" + H, 0, 8), R("IX" + H), 2.0, ALU.mult, 1.0, ALU.add)
+        mm([(C("pI" + H, 0, 128), C("PW" + H, 0, 128), ID), (C("pI" + H, 0, 128), R("FL" + H), NS)])
+        mm([(C("pE" + H, 0, 128, p=lo8), C("OH" + H, 0, 8), ID)])
+        act(R("YC", hs), C("pI" + H, 0, 128), AF.Identity, 2048.0)
+        cpy(R("YN", hs, p=lo8), C("pE" + H, 0, 128, p=lo8))
         dma("S", T.yw[:, hs], T.YC[:, hs], [], [R("YC", hs)], 2200.0)
         dma("Y", T.yn[:, hs], T.YN[0:8, hs], [], [R("YN", hs)], 2000.0)
     return ops
@@ -668,6 +691,19 @@ def order(ops):
             best = (span, end)
         end = place(sorted(range(n), key=lambda k: (-end[k], -k)), True)
         end = place(sorted(range(n), key=lambda k: (-end[k], k)), False)
+    for it in range(SHAKES):
+        key = [0.0] * n
+        x = (x * 1103515245 + 12345) % 2147483648
+        t0 = best[0] * x / 2147483648.0
+        for k in range(n):
+            x = (x * 1103515245 + 12345) % 2147483648
+            near = abs(best[1][k] - t0) < SPAN
+            key[k] = max([best[1][k] + near * SHAKE * x / 2147483648.0] + [key[j] + 0.01 for j in pred[k]])
+        end = place(sorted(range(n), key=lambda k: -key[k]), True)
+        end = place(sorted(range(n), key=lambda k: (-end[k], k)), False)
+        span = max(end[k] + ops[k]["lat"] for k in range(n))
+        if span < best[0] + SLACK:
+            best = (span, end)
     end = best[1]
     seq = sorted(range(n), key=lambda k: (end[k] - max(ops[k]["cost"], 1.0), k))
     return pred, seq, [end[k] + ops[k]["lat"] for k in range(n)]
@@ -677,7 +713,9 @@ def rank_program(g, core, T, topo):
     if T.rank_of(core) is None:
         return
     ops = build(g, core, T, topo)
-    pred, seq, fin = order(ops)
+    if not PLAN:
+        PLAN.append(order(ops))
+    pred, seq, fin = PLAN[0]
     Q = {"V": g.vector, "S": g.scalar, "P": g.tensor, "G": g, "Y": g.sync}
     tok = {}
     know = {}

@@ -7,22 +7,25 @@ DUM = 3728
 XW = DUM + 256
 DEAD_O, DEAD_P = 3584.0, 1280.0
 MAGIC = 12582912.0
-HB = (32, 32, 32, 32)
-HV = ()
+HB = (32, 32, 48, 16)
+HV = (3,)
 EB = (32, 32, 32, 32)
-EV = (((0, 2), (0, 2)), ((0, 2), (0, 2)))
-SH = ((32, 32, 32, 32), (32, 32, 32, 32))
+EV = (((0, 2), (0, 2)), ((0,), (0, 2)))
+SH = ((64, 64, 64, 64), (64, 64, 64, 64))
+CASES = ((-0.35, 1.0, 1.0, 220.0), (0.35, -1.0, 0.9, 100.0), (0.0, 0.0, 1.2, 160.0))
+FAST, XEV = (0, 1), (0,)
 PENAT = 1
-SHAKES, SHAKE, SLACK, SPAN = 1200, 1000.0, 1.0, 2500.0
+SHAKES, SHAKE, SLACK, SPAN = 1600, 1000.0, 1.0, 2500.0
 BIASE = 2500.0
 BIAS = 2500.0
-LAT = 120.0
+LAT = 150.0
 PE = 0.55
 SEED = 36
 NOISE = 300.0
 WIN = 30.0
 PASSES = 8
-NX, NC = 4, 2
+NX, NC = 4, 4
+CORES_ALL = 128
 
 F, B, I, U, H16 = "float32", "bfloat16", "int32", "uint16", "float16"
 SCRATCH = {}
@@ -34,10 +37,10 @@ def _sb(name, shape, dt):
 
 
 for _n, _s, _d in [
-    ("X", [2 * XW], F), ("XB", [V], B), ("XR", [V], B), ("CI", [V], I), ("CP", [V], F), ("CU", [V], U), ("CN", [V], U),
+    ("X", [2 * XW], F), ("XB", [V], B), ("XR", [V], B), ("CI", [V], I), ("CP", [V], F), ("CU", [V], H16), ("CN", [V], H16),
     ("IOT", [3840], F), ("WI", [256], I), ("WF", [256], F), ("ZI", [512], I), ("ZF", [512], F),
     ("PC", [16], I), ("PF", [24], F), ("XI", [128], F), ("MB", [11, 128], B), ("MF", [2, 128], F), ("SEL", [24], B),
-    ("KF", [1792], F), ("KB", [768], B), ("EK", [13, 128], B), ("SAB", [256], B),
+    ("KF", [2016], F), ("KB", [768], B), ("EK", [13, 128], B), ("SAB", [256], B),
     ("LI", [128], I), ("LF", [128], F), ("LU", [128], U), ("TM", [80], F),
     ("TH", [16], F), ("THR", [16], F), ("ABU", [32], U), ("AS", [32], F), ("AB", [32], F),
     ("ROW", [512], U), ("EA", [16, 256], B), ("EB", [16, 256], B), ("LM", [2, 2, 8], F),
@@ -50,7 +53,7 @@ for _r in range(3):
 for _h in range(2):
     for _n, _s, _d in [
         ("PW", [144], H16), ("LP", [128], U), ("PA", [128], H16), ("PB", [128], H16), ("D", [2048], B), ("A", [2048], B),
-        ("R", [4, 128], F), ("PL", [512], F), ("NN", [128], B), ("W2", [256], F), ("W3", [256], F),
+        ("R", [4, 128], F), ("PL", [512], F), ("NN", [128], B), ("W1", [128], F), ("W2", [256], F), ("W3", [256], B),
         ("SM", [176], F), ("IX", [8], F), ("TS", [16], F), ("OH", [48], B), ("PR", [5, 128], H16), ("FL", [128], B),
         ("EX", [8], U), ("OF", [128], U), ("C16", [128], H16), ("CW", [128], F), ("XE", [128], B), ("WX", [256], F),
         ("EQ", [7, 128], B), ("FD", [2, 8], F), ("XA", [256], B), ("MT", [128], F), ("CS", [128], F), ("LS", [48], F),
@@ -59,7 +62,30 @@ for _h in range(2):
     for _n in ("pD", "pX", "pE", "pI"):
         SCRATCH[_n + str(_h)] = ("psum", [128, 512], F)
 
-SEMAPHORES = ["cV", "cS", "cP", "cG"] + ["d%d" % _i for _i in range(20)] + ["l%d" % _i for _i in range(24)] + ["a%d" % _i for _i in range(30)]
+SEMAPHORES = ["cV", "cS", "cP", "cG"] + ["d%d" % _i for _i in range(20)] + ["l%d" % _i for _i in range(30)] + ["a%d" % _i for _i in range(30)] + ["r%d" % _i for _i in range(NC)]
+
+
+def relays(T, topo, rank):
+    core, dst = T.cores[rank], T.cores[(rank - 1) % len(T.cores)]
+    far = [c for c in range(CORES_ALL) if topo.mates(topo.chip(c), topo.chip(dst)) and topo.die(c) == topo.die(core) and topo.may_write(c, dst)][0]
+    near = [c for c in topo.cores_of(core) if c not in T.cores and topo.die(c) == topo.die(core) and topo.may_write(c, far)][0]
+    return near, far
+
+
+def hand_on(g, core, T, topo):
+    n = len(T.cores)
+    w = V // NC
+    for rank in range(n):
+        way = (T.cores[rank],) + relays(T, topo, rank) + (T.cores[(rank - 1) % n],)
+        if core in way[1:3]:
+            at = way.index(core)
+            src, dst = way[at - 1], way[at + 1]
+            nin = len([e for e in topo.engines(src, core) if at == 2 or e not in topo.engines(src, way[3])])
+            rid, pid, _ = topo.addr(dst)
+            for k in range(NC):
+                g.wait_ge(T.sem["r%d" % k], nin)
+                g.remote_dma(T.CN[:, k * w:(k + 1) * w], T.CN[:, k * w:(k + 1) * w], T.sem["r%d" % k], T.sem.l0, pid, rid, topo.mask(core, dst))
+            g.wait_ge(T.sem.l0, NC * len(topo.engines(core, dst)))
 
 
 def build(g, core, T, topo):
@@ -103,6 +129,7 @@ def build(g, core, T, topo):
         for x in outs:
             wr += x["reg"]; rd += x.get("off", [])
         ops.append({"eng": eng, "cost": cost, "fn": fn, "rd": rd, "wr": wr, "lat": lat, "sem": sem, "bias": cur[0], "after": list(after),
+                    "ge": sum(x["n"] for x in ins if isinstance(x, dict) and x.get("ind")), "se": sum(x["n"] for x in outs if x.get("ind")),
                     "ind": any(isinstance(x, dict) and x.get("ind") for x in list(ins) + list(outs))})
         return len(ops) - 1
 
@@ -204,7 +231,8 @@ def build(g, core, T, topo):
                 return q.remote_dma_fused(trs, local_sem=T.sem[sl])
         k0 = add("G", 500, fn, [], [i for d, o, i in parts], lat=1500.0, sem=(sl, ne, False))
         for k, (d, o, i) in enumerate(parts):
-            add("X", lat, None, [o], [], lat=1000.0, sem=(sa[k], nin[k], False), after=[k0])
+            add("X", lat, None, [o], [], lat=2000.0, sem=(sa[k], nin[k], False), after=[k0])
+        ops[k0]["lat"] = 0.0
         return k0
 
     w = V // NX
@@ -221,12 +249,21 @@ def build(g, core, T, topo):
         for a, f in ((k * w, act), (k * w + w // 2, cpy)):
             f(C("X", XW + a, XW + a + w // 2), C("XR", a, a + w // 2))
     w = V // NC
+    h1 = relays(T, topo, rank)[0]
+    up = [e for e in topo.engines(core, h1) if e not in topo.engines(core, cp)]
     for k in range(NC):
         c = C("CI", k * w, (k + 1) * w)
-        dma("Y", c["ap"], T.cand[:, k * w:(k + 1) * w], [c], [], 9000.0 + 4000 * k)
+        dma("Y", c["ap"], T.cand[:, k * w:(k + 1) * w], [c], [], 7500.0 + 2000 * k)
         for a in range(k * w, (k + 1) * w, 464):
-            cpy(C("CU", a, a + 464), C("CI", a, a + 464))
-        send([(cp, C("CN", k * w, (k + 1) * w), C("CU", k * w, (k + 1) * w))], 7000.0)
+            ts(C("CU", a, a + 464), C("CI", a, a + 464), -2048.0, ALU.add)
+        o, i = C("CN", k * w, (k + 1) * w), C("CU", k * w, (k + 1) * w)
+        sl = "l%d" % cnt["l"]; cnt["l"] += 1
+
+        def fn(q, o=o, i=i, sl=sl, k=k):
+            rid, pid, _ = topo.addr(h1)
+            return q.remote_dma(o["ap"], i["ap"], T.sem["r%d" % k], T.sem[sl], pid, rid, sum(1 << e for e in up))
+        k0 = add("G", 500, fn, [], [i], lat=1500.0, sem=(sl, len(up), False))
+        add("Z", 3600.0, None, [o], [], lat=14000.0, sem=("r%d" % k, len(topo.engines(relays(T, topo, (rank + 1) % n)[1], core)), False), after=[k0])
     ms(C("X", V, XW), DEAD_O); ms(C("X", XW + V, 2 * XW), DEAD_P)
     ms(C("DK", 0, 128), DEAD_O); ms(C("DK", 128, 256), DEAD_P)
 
@@ -268,10 +305,9 @@ def build(g, core, T, topo):
     ts(pf(15), pf(14), 4.0, ALU.mult)
     K16, RST, VRS, MW, KH, KP8, CAP, COH, DUMC, SM8 = (C("KF", 0, 256), C("KF", 256, 384), C("KF", 384, 512), C("KF", 512, 768), C("KF", 768, 896),
                                                        C("KF", 896, 960), C("KF", 960, 1216), C("KF", 1216, 1264), C("KF", 1264, 1296), C("KF", 1296, 1304))
-    K8, KAB, KH1 = C("KF", 1312, 1376), C("KF", 1376, 1632), C("KF", 1632, 1760)
+    KAB, KLH, CDN = C("KF", 1376, 1632), C("KF", 1632, 1888), C("KF", 1888, 2016)
     iota(K16, [[0, 16], [1, 16]])
     iota(C("KB", 640, 768), [[1, 8], [0, 16]])
-    iota(K8, [[0, 8], [1, 8]])
     iota(COH, [[1, 6], [0, 8]])
     for q_ in range(2):
         iota(C("KF", 960 + 128 * q_, 1088 + 128 * q_), [[0, 8], [1, 8], [1, 2]], 4 - q_)
@@ -289,14 +325,15 @@ def build(g, core, T, topo):
     act(VRS, k128, AF.Sign)
     act(VRS, VRS, AF.Identity, -1.0e6, 2.0e6)
     act(KH, k128, AF.Identity, 0.0, 0.5)
-    act(KP8, K8, AF.Sign)
     ts(DUMC, DUMC, pf(1), ALU.add)
     ICON, ICE, MASK, K2 = C("KB", 0, 128), C("KB", 128, 256), C("KB", 256, 384), C("KB", 384, 512)
     act(ICON, k128, AF.Identity, 0.0, 2.0 ** -20)
     act(ICE, k128, AF.Identity, 0.0, 2.0 ** -20)
     ms(C("KB", 143, 256, 16), 0.0)
-    act(KH1, k128, AF.Identity, 1.0, 0.5)
-    ms(C("KF", 1647, 1760, 16), -1.0)
+    iota(C("KF", 1632, 1760), [[0, 8], [2, 8], [0, 2]]); iota(C("KF", 1760, 1888), [[0, 8], [-2, 8], [0, 2]], 13)
+    ms(C("KF", 1647, 1888, 16), 99.0)
+    ts(CDN, k128, 0.0, ALU.is_equal, 1001.0, ALU.mult)
+    act(CDN, CDN, AF.Identity, -1.0)
     ms(C("KF", 975, 1216, 16), -1.0)
     act(MASK, C("KF", 512, 640), AF.Identity, -65536.0, 65536.0)
     ms(K2, 2048.0)
@@ -346,11 +383,14 @@ def build(g, core, T, topo):
             mm([(C("pI" + H, 128 + 8 * k, 136 + 8 * k), C("ZF", 256 * k + 128 * h, 256 * k + 128 * h + 128, p=lo8), R("MF", 0, slice(0, 8), p=lo8))])
         ts(R("IX" + H), C("pI" + H, 128, 136), 0.5, ALU.mult, -0.5, ALU.add)
         ts(C("TH", 8 * h, 8 * h + 8), C("pI" + H, 136, 144), 2.0 ** -16, ALU.mult)
-        tt(C("W3" + H, 0, 128), IN(R("IX" + H), L("r16", 0, 8)), KH, ALU.is_lt)
-        act(C("W3" + H, 0, 128), C("W3" + H, 0, 128), AF.Identity, -2048.0, SENT)
-        tt(C("PW" + H, 0, 128), C("W3" + H, 0, 128), C("pI" + H, 0, 128), ALU.max)
-    for a in range(0, V, 464):
-        cpy(C("CP", a, a + 464), C("CN", a, a + 464))
+        tt(R("W1" + H), IN(R("IX" + H), L("r16", 0, 8)), KH, ALU.is_lt)
+        act(R("W1" + H), R("W1" + H), AF.Identity, -2048.0, SENT)
+        tt(C("PW" + H, 0, 128), R("W1" + H), C("pI" + H, 0, 128), ALU.max)
+
+    def widen(k):
+        bk = C("pX" + str(k % 2), 0, 464)
+        mm([(bk, ID, C("CN", 464 * k, 464 * k + 464))])
+        act(C("CP", 464 * k, 464 * k + 464), bk, AF.Identity, 2048.0)
 
     def spread(H, bank, win, off, k):
         tt(C("WX" + H, 0, 128 * k), IN(win, off), C("KF", 512, 512 + 128 * k), ALU.mult)
@@ -369,8 +409,9 @@ def build(g, core, T, topo):
         PW = "PW" + H
         sm = lambda k: C("SM" + H, 8 * k, 8 * k + 8)
         R0 = R("R" + H, 0)
-        mm([(C("pI" + H, 0, 128), C(PW, 0, 128), ID)])
-        ts(R("LP" + H), C("pI" + H, 0, 128), pf(12), ALU.add)
+        if rnd == 0:
+            mm([(C("pX" + H, 0, 128), C(PW, 0, 128), ID)])
+        ts(R("LP" + H), C("pX" + H, 0, 128), pf(12), ALU.add)
         ts(R("PA" + H), R("LP" + H), pf(9), ALU.add)
         if rnd == 0:
             ts(R("PB" + H), R("LP" + H), pf(8), ALU.add)
@@ -380,20 +421,25 @@ def build(g, core, T, topo):
         parts = [[(D, ID, ICE), (C("pD" + H, 15, 128, 16), IDF, C("TH" if rnd == 0 else "THR", 8 * h, 8 * h + 8))]]
         if rnd > 0:
             mm([(C("pD" + H, 128, 256), ID, ICE)] + [(C("pD" + H, 128 + k, 256, 16), C("D" + H, k, 2048, 16), SEL1) for k in range(16)])
-            ts(C("W2" + H, 0, 128), C("pD" + H, 128, 256), 0.125, ALU.is_lt)
-            scan(C("W2" + H, 128, 256), RST, C("W2" + H, 0, 128), ALU.max, ALU.min)
-            scan(C("W3" + H, 0, 64), KP8, C("W2" + H, 129, 256, 2), ALU.mult, ALU.add)
-            scan(C("W3" + H, 64, 128), KP8, C("W2" + H, 128, 256, 2), ALU.mult, ALU.add)
-            No, Ne = C("W3" + H, 7, 64, 8), C("W3" + H, 71, 128, 8)
-            tt(sm(1), R("IX" + H), No, ALU.subtract)
-            act(sm(6), No, AF.Identity, 1.0)
-            tt(sm(4), sm(1), Ne, ALU.is_gt)
-            tt(sm(2), sm(1), Ne, ALU.max)
+            ts(C("W2" + H, 0, 128), C("pD" + H, 128, 256), 0.125, ALU.is_lt, 64.0, ALU.mult)
+            scan(C("W2" + H, 128, 256), CDN, C("W2" + H, 0, 128), ALU.add, ALU.min)
+            J15 = C("W2" + H, 143, 256, 16)
+            act(sm(0), R("IX" + H), AF.Identity, -15.0)
+            ts(sm(3), J15, 16.0, ALU.add)
+            tt(sm(4), J15, sm(0), ALU.is_lt)
+            ts(sm(5), J15, -1.0, ALU.mult, 1.0, ALU.add)
+            tt(sm(7), J15, sm(0), ALU.is_ge)
+            tt(sm(16), sm(4), sm(3), ALU.mult)
+            tt(sm(17), sm(7), sm(5), ALU.mult)
+            tt(C("W3" + H, 0, 256), IN(C("SM" + H, 128, 144), L("r16", 0, 16)), KLH, ALU.is_gt)
+            parts.append([(D, ID, C("W3" + H, 128 * k, 128 * k + 128)) for k in range(2)])
+            act(sm(6), J15, AF.Identity, 8.25, 0.5)
+            ts(sm(6), sm(6), MAGIC, ALU.add, -MAGIC, ALU.add)
+            act(sm(10), R("IX" + H), AF.Identity, 1.0)
+            tt(sm(1), sm(10), sm(6), ALU.subtract)
+            tt(sm(11), sm(3), sm(6), ALU.subtract)
+            tt(sm(2), sm(1), sm(11), ALU.max)
             tt(C("TS" + H, 0, 8), sm(6), sm(4), ALU.mult)
-            tt(C("TS" + H, 8, 16), sm(2), C("TS" + H, 0, 8), ALU.add)
-            tt(R("EQ" + H, 0), IN(R("TS" + H), L("r16", 0, 8)), KH, ALU.is_gt)
-            tt(R("EQ" + H, 1), IN(R("TS" + H), L("r16", 8, 16)), KH1, ALU.is_le)
-            parts.append([(D, ID, R("EQ" + H, k)) for k in range(2)])
         for c in range(4):
             a = 512 * c
             bk = C(("pX", "pE")[c % 2] + H, 0, 511)
@@ -408,7 +454,7 @@ def build(g, core, T, topo):
             scan(C("PL" + H, 128 * k, 128 * k + 128), R("NN" + H), C("pI" + H, 128 + 128 * k, 256 + 128 * k), ALU.mult, ALU.max)
         o = spread(H, "pI", C("PL" + H, 0, 256), L("e16", 0, 16), 2)
         ts(C("ABU", 16 * h, 16 * h + 16), o, -1.0, ALU.add)
-        cpy(C("AS", 16 * h, 16 * h + 16), o)
+        (act if h == 0 else cpy)(C("AS", 16 * h, 16 * h + 16), o)
         if rnd > 0:
             act(R("IX" + H), sm(2), AF.Relu, -1.0)
             ts(sm(8), sm(2), 0.5, ALU.is_lt)
@@ -477,8 +523,13 @@ def build(g, core, T, topo):
         tt(C("LS" + H, 32, 48), C("LS" + H, 16, 32), dm, ALU.mult)
         tt(R("LM", h), C("LS" + H, 32, 48), ab, ALU.max)
         cpy(C("LW" + r, 16 * h, 16 * h + 16), R("LM", h))
-        send([(cp, C("LA" + r, 8 * h, 8 * h + 8), C("LW" + r, 16 * h, 16 * h + 8)),
-              (cq, C("LB" + r, 8 * h, 8 * h + 8), C("LW" + r, 16 * h + 8, 16 * h + 16))], 100.0)
+        ends = [(cp, C("LA" + r, 8 * h, 8 * h + 8), C("LW" + r, 16 * h, 16 * h + 8)),
+                (cq, C("LB" + r, 8 * h, 8 * h + 8), C("LW" + r, 16 * h + 8, 16 * h + 16))]
+        if h == 0:
+            send(ends, 200.0)
+        else:
+            send(ends[:1], 100.0)
+            send(ends[1:], 100.0)
 
     def merge(rnd):
         r = str(rnd)
@@ -504,10 +555,12 @@ def build(g, core, T, topo):
         b0, nb = ((0, 6), (6, 7), (0, 5), (6, 6))[j]
         cpy(R("OF" + H), IN(cw, R("EX" + H)))
         ts(R("C16" + H), R("OF" + H), -2048.0, ALU.add)
-        if j == 0:
+        if j == 0 and h in XEV:
             ts(R("XE" + H), IN(xe, R("EX" + H)), 255.0, ALU.min)
         else:
             act(R("XE" + H), IN(xe, R("EX" + H)))
+            if j == 0:
+                ts(R("XE" + H), R("XE" + H), 255.0, ALU.min)
         gathers(H, xc, "OF" + H, HB, HV)
         IC = C("pI" + H, 0, 128)
         mm([(IC, R("C16" + H), ID)])
@@ -546,29 +599,56 @@ def build(g, core, T, topo):
         if j < 3:
             cpy(R("EX" + H), spread(H, "pI", pl, L("e16", 0, 8), 1))
 
-    def append(h, q):
+    def append(h, q, rnd):
         H = str(h)
-        PW = "PW" + H
+        PW = C("PW" + H, 0, 128)
         sm = lambda k: C("SM" + H, 8 * k, 8 * k + 8)
-        ts(R("FD" + H), R("R" + H, slice(2 * q, 2 * q + 2), slice(15, 128, 16)), 0.125, ALU.is_lt)
-        tt(sm(13 + q), R("FD" + H, 0), R("FD" + H, 1), ALU.mult)
-        if q == 1:
-            tt(sm(14), sm(14), sm(13), ALU.mult)
-        tt(sm(15), sm(13 + q), sm(12), ALU.mult)
-        tt(R("FL" + H), IN(sm(15), L("r16", 0, 8)), C("KF", 960 + 128 * q, 1088 + 128 * q), ALU.not_equal)
-        act(C("W3" + H, 0, 128), IN(C("PL" + H, 256 * q, 256 * q + 256), L("val", 0, 8)), AF.Identity, -2048.0)
+        val = IN(C("PL" + H, 256 * q, 256 * q + 256), L("val", 0, 8))
+        cap = C("KF", 960 + 128 * q, 1088 + 128 * q)
         bk = C("pX" + H, 0, 128)
-        mm([(bk, SI, R("FL" + H)), (bk, IDF, C("W3" + H, 0, 128))])
-        tt(C(PW, 0, 128), C(PW, 0, 128), bk, ALU.min)
-        tt(R("IX" + H), R("IX" + H), sm(13 + q), ALU.add)
-        if q == 1:
-            ts(R("IX" + H), R("IX" + H), 7.0, ALU.min)
+        if q == 0:
+            ts(R("FD" + H), R("R" + H, slice(0, 2), slice(15, 128, 16)), 0.125, ALU.is_lt)
+            tt(sm(13), R("FD" + H, 0), R("FD" + H, 1), ALU.mult)
+            tt(sm(15), sm(13), sm(12), ALU.mult)
+            tt(R("FL" + H), IN(sm(15), L("r16", 0, 8)), cap, ALU.not_equal)
+            act(R("W1" + H), val, AF.Identity, -2048.0)
+            mm([(bk, SI, R("FL" + H)), (bk, IDF, R("W1" + H))])
+            tt(PW, PW, bk, ALU.min)
+            tt(R("IX" + H), R("IX" + H), sm(13), ALU.add)
+            return
+        for k in range(2):
+            ts(R("FD" + H, k), R("R" + H, 2 + k, slice(15, 128, 16)), 0.125, ALU.is_lt)
+        tt(sm(14), R("FD" + H, 0), sm(15), ALU.mult)
+        tt(sm(14), R("FD" + H, 1), sm(14), ALU.mult)
+        if rnd == 2 or h in FAST:
+            tt(R("FL" + H), IN(sm(14), L("r16", 0, 8)), cap, ALU.is_equal)
+            tt(R("W1" + H), val, R("FL" + H), ALU.mult)
+        if rnd < 2 and h not in FAST:
+            tt(R("FL" + H), IN(sm(14), L("r16", 0, 8)), cap, ALU.not_equal)
+            act(R("W1" + H), val, AF.Identity, -2048.0)
+            mm([(bk, SI, R("FL" + H)), (bk, IDF, R("W1" + H))])
+            tt(PW, PW, bk, ALU.min)
+            mm([(bk, PW, ID)])
+        elif rnd < 2:
+            group([[(bk, PW, ID)], [(bk, R("FL" + H), NS)], [(bk, R("W1" + H), IDF)]])
+            pe = C("pE" + H, 0, 128)
+            mm([(pe, ID, PW), (pe, NS, R("FL" + H)), (pe, IDF, R("W1" + H))])
+            cpy(PW, pe)
+        else:
+            ts(C("W3" + H, 0, 128), PW, SENT - 2048.0, ALU.is_ge)
+            group([[(bk, PW, ID), (bk, C("W3" + H, 0, 128), NS)], [(bk, R("W1" + H), IDF)]])
+        ts(sm(14), sm(14), 1.0, ALU.min)
+        tt(R("IX" + H), R("IX" + H), sm(14), ALU.add)
+        ts(R("IX" + H), R("IX" + H), 7.0, ALU.min)
 
     for rnd in range(3):
         for h in range(2):
             cur[0] = BIASE * (1 - h)
             edges(h, rnd)
         cur[0] = 0.0
+        if rnd == 0:
+            for k in range(8):
+                widen(k)
         for h in range(2):
             clash(h, rnd)
         merge(rnd)
@@ -585,16 +665,14 @@ def build(g, core, T, topo):
             for j in range(4):
                 hop(h, j)
                 if j % 2 == 1:
-                    append(h, j // 2)
+                    append(h, j // 2, rnd)
     for h in range(2):
         cur[0] = BIAS * (1 - h)
         H = str(h)
         hs = slice(128 * h, 128 * h + 128)
-        ts(R("FL" + H), C("PW" + H, 0, 128), SENT - 2048.0, ALU.is_ge)
         ts(C("OH" + H, 0, 8), R("IX" + H), 2.0, ALU.mult, 1.0, ALU.add)
-        mm([(C("pI" + H, 0, 128), C("PW" + H, 0, 128), ID), (C("pI" + H, 0, 128), R("FL" + H), NS)])
         mm([(C("pE" + H, 0, 128, p=lo8), C("OH" + H, 0, 8), ID)])
-        act(R("YC", hs), C("pI" + H, 0, 128), AF.Identity, 2048.0)
+        act(R("YC", hs), C("pX" + H, 0, 128), AF.Identity, 2048.0)
         cpy(R("YN", hs, p=lo8), C("pE" + H, 0, 128, p=lo8))
         dma("S", T.yw[:, hs], T.YC[:, hs], [], [R("YC", hs)], 2200.0)
         dma("Y", T.yn[:, hs], T.YN[0:8, hs], [], [R("YN", hs)], 2000.0)
@@ -658,7 +736,7 @@ def order(ops):
                 rdy[j] = max(fin[i] + LAT for i in pred[j])
 
     def gap(j, k):
-        return ops[j]["lat"] + (0.0 if ops[j]["eng"] == "P" and ops[k]["eng"] == "P" else LAT)
+        return 0.0 if ops[j]["eng"] == "P" and ops[k]["eng"] == "P" else ops[j]["lat"] + LAT
 
     def place(lst, back):
         busy = {}
@@ -691,17 +769,37 @@ def order(ops):
             best = (span, end)
         end = place(sorted(range(n), key=lambda k: (-end[k], -k)), True)
         end = place(sorted(range(n), key=lambda k: (-end[k], k)), False)
+    cases = []
+    for dg, ds, pe, lat in CASES:
+        cases.append(([(o["cost"] + dg * o["ge"] + ds * o["se"]) * (pe if o["eng"] == "P" else 1.0) for o in ops],
+                      [[(j, 0.0 if ops[j]["eng"] == "P" and ops[k]["eng"] == "P" else ops[j]["lat"] + lat) for j in pred[k]] for k in range(n)]))
+
+    def judge(end):
+        lst = sorted(range(n), key=lambda k: (end[k] - max(ops[k]["cost"], 1.0), k))
+        total = 0.0
+        for cost, gaps in cases:
+            free, fin = {}, [0.0] * n
+            for k in lst:
+                e = ops[k]["eng"]
+                s = free.get(e, 0.0)
+                for j, d in gaps[k]:
+                    if fin[j] + d > s:
+                        s = fin[j] + d
+                free[e] = fin[k] = s + cost[k]
+            total += max(fin[k] + ops[k]["lat"] for k in range(n))
+        return total / len(cases)
+    best = (judge(best[1]), best[1])
     for it in range(SHAKES):
         key = [0.0] * n
         x = (x * 1103515245 + 12345) % 2147483648
-        t0 = best[0] * x / 2147483648.0
+        t0 = max(best[1]) * x / 2147483648.0
         for k in range(n):
             x = (x * 1103515245 + 12345) % 2147483648
             near = abs(best[1][k] - t0) < SPAN
             key[k] = max([best[1][k] + near * SHAKE * x / 2147483648.0] + [key[j] + 0.01 for j in pred[k]])
         end = place(sorted(range(n), key=lambda k: -key[k]), True)
         end = place(sorted(range(n), key=lambda k: (-end[k], k)), False)
-        span = max(end[k] + ops[k]["lat"] for k in range(n))
+        span = judge(end)
         if span < best[0] + SLACK:
             best = (span, end)
     end = best[1]
@@ -711,6 +809,7 @@ def order(ops):
 
 def rank_program(g, core, T, topo):
     if T.rank_of(core) is None:
+        hand_on(g, core, T, topo)
         return
     ops = build(g, core, T, topo)
     if not PLAN:
@@ -725,7 +824,7 @@ def rank_program(g, core, T, topo):
     for k in seq:
         o = ops[k]
         e = o["eng"]
-        if e == "X":
+        if e in "XZ":
             tok[k] = o["sem"][:2]
             count[tok[k][0]] = tok[k][1]
             continue

@@ -7,24 +7,25 @@ DUM = 3728
 XW = DUM + 256
 DEAD_O, DEAD_P = 3584.0, 1280.0
 MAGIC = 12582912.0
-HB = (32, 32, 48, 16)
-HV = (3,)
+HB = (32, 32, 16, 32, 16)
+HV = (((0, 2), (2,), (2,), (2,)), ((2,), (2,), (2,), (2,)))
 EB = (32, 32, 32, 32)
 EV = (((0, 2), (0, 2)), ((0,), (0, 2)))
 SH = ((64, 64, 64, 64), (64, 64, 64, 64))
-CASES = ((-0.35, 1.0, 1.0, 220.0), (0.35, -1.0, 0.9, 100.0), (0.0, 0.0, 1.2, 160.0))
-FAST, XEV = (0, 1), (0,)
+CASES = ((-0.3, 0.0, 1.0, 230.0), (0.3, 0.0, 1.0, 160.0), (0.0, 0.0, 1.0, 200.0))
+FAST, XEV, CWE, RAWP = (0, 1), (0,), "V", 2
 PENAT = 1
-SHAKES, SHAKE, SLACK, SPAN = 1600, 1000.0, 1.0, 2500.0
+SHAKES, SHAKE, SLACK, SPAN = 3800, 1000.0, 20.0, 2500.0
 BIASE = 2500.0
 BIAS = 2500.0
-LAT = 150.0
+LAT = 220.0
 PE = 0.55
 SEED = 36
 NOISE = 300.0
 WIN = 30.0
 PASSES = 8
-NX, NC = 4, 4
+XPIECES = ((0, 464, 0), (464, 1024, 1), (1024, 1584, 1), (1584, 2416, 0), (2416, 3248, 0), (3248, V, 0))
+NC = 4
 CORES_ALL = 128
 
 F, B, I, U, H16 = "float32", "bfloat16", "int32", "uint16", "float16"
@@ -38,13 +39,13 @@ def _sb(name, shape, dt):
 
 for _n, _s, _d in [
     ("X", [2 * XW], F), ("XB", [V], B), ("XR", [V], B), ("CI", [V], I), ("CP", [V], F), ("CU", [V], H16), ("CN", [V], H16),
-    ("IOT", [3840], F), ("WI", [256], I), ("WF", [256], F), ("ZI", [512], I), ("ZF", [512], F),
-    ("PC", [16], I), ("PF", [24], F), ("XI", [128], F), ("MB", [11, 128], B), ("MF", [2, 128], F), ("SEL", [24], B),
-    ("KF", [2016], F), ("KB", [768], B), ("EK", [13, 128], B), ("SAB", [256], B),
+    ("WB", [256], F), ("WF", [256], F), ("ZI", [768], I), ("ZF", [512], F),
+    ("PC", [16], I), ("PF", [24], F), ("XI", [128], F), ("MB", [11, 128], B), ("MF", [2, 128], F), ("SEL", [32], B),
+    ("KF", [2016], F), ("KB", [896], B), ("EK", [13, 128], B), ("SAB", [256], B),
     ("LI", [128], I), ("LF", [128], F), ("LU", [128], U), ("TM", [80], F),
-    ("TH", [16], F), ("THR", [16], F), ("ABU", [32], U), ("AS", [32], F), ("AB", [32], F),
-    ("ROW", [512], U), ("EA", [16, 256], B), ("EB", [16, 256], B), ("LM", [2, 2, 8], F),
-    ("DK", [256], F), ("CT", [24], F), ("CTI", [8], I), ("YC", [256], F), ("YN", [256], F), ("ZZ", [128], F), ("NP", [16], B),
+    ("TH", [16], F), ("THR", [16], F), ("ABU", [32], U), ("AS", [32], F),
+    ("ROW", [512], U), ("EA", [16, 256], B), ("EB", [16, 256], B), ("LM", [64], F),
+    ("DK", [256], F), ("CT", [40], F), ("CTI", [8], I), ("YC", [256], F), ("YN", [256], F), ("ZZ", [128], F), ("NP", [16], B), ("EXP", [768], B),
 ]:
     _sb(_n, _s, _d)
 for _r in range(3):
@@ -56,13 +57,13 @@ for _h in range(2):
         ("R", [4, 128], F), ("PL", [512], F), ("NN", [128], B), ("W1", [128], F), ("W2", [256], F), ("W3", [256], B),
         ("SM", [176], F), ("IX", [8], F), ("TS", [16], F), ("OH", [48], B), ("PR", [5, 128], H16), ("FL", [128], B),
         ("EX", [8], U), ("OF", [128], U), ("C16", [128], H16), ("CW", [128], F), ("XE", [128], B), ("WX", [256], F),
-        ("EQ", [7, 128], B), ("FD", [2, 8], F), ("XA", [256], B), ("MT", [128], F), ("CS", [128], F), ("LS", [48], F),
+        ("EQ", [7, 128], B), ("FD", [2, 8], F), ("XA", [256], B), ("MT", [128], F), ("CS", [160], F),
     ]:
         _sb(_n + str(_h), _s, _d)
     for _n in ("pD", "pX", "pE", "pI"):
         SCRATCH[_n + str(_h)] = ("psum", [128, 512], F)
 
-SEMAPHORES = ["cV", "cS", "cP", "cG"] + ["d%d" % _i for _i in range(20)] + ["l%d" % _i for _i in range(30)] + ["a%d" % _i for _i in range(30)] + ["r%d" % _i for _i in range(NC)]
+SEMAPHORES = ["cV", "cS", "cP", "cG"] + ["d%d" % _i for _i in range(24)] + ["l%d" % _i for _i in range(32)] + ["a%d" % _i for _i in range(30)] + ["r%d" % _i for _i in range(8)]
 
 
 def relays(T, topo, rank):
@@ -82,10 +83,11 @@ def hand_on(g, core, T, topo):
             src, dst = way[at - 1], way[at + 1]
             nin = len([e for e in topo.engines(src, core) if at == 2 or e not in topo.engines(src, way[3])])
             rid, pid, _ = topo.addr(dst)
-            for k in range(NC):
+            pieces = [T.XR[:, a:b] for a, b, far in XPIECES if far] + [T.CN[:, k * w:(k + 1) * w] for k in range(NC)]
+            for k, x in enumerate(pieces):
                 g.wait_ge(T.sem["r%d" % k], nin)
-                g.remote_dma(T.CN[:, k * w:(k + 1) * w], T.CN[:, k * w:(k + 1) * w], T.sem["r%d" % k], T.sem.l0, pid, rid, topo.mask(core, dst))
-            g.wait_ge(T.sem.l0, NC * len(topo.engines(core, dst)))
+                g.remote_dma(x, x, T.sem["r%d" % k], T.sem.l0, pid, rid, topo.mask(core, dst))
+            g.wait_ge(T.sem.l0, len(pieces) * len(topo.engines(core, dst)))
 
 
 def build(g, core, T, topo):
@@ -94,7 +96,7 @@ def build(g, core, T, topo):
     cp, cq = T.cores[(rank - 1) % n], T.cores[(rank + 1) % n]
     ops = []
     cur = [0.0]
-    cnt = {"d": 0, "l": 0, "a": 0}
+    cnt = {"d": 0, "l": 0, "a": 0, "r": 0}
 
     def R(name, *idx, p=slice(None)):
         shp = SCRATCH[name][1][1:]
@@ -128,7 +130,7 @@ def build(g, core, T, topo):
                 rd += x["reg"] + x.get("off", [])
         for x in outs:
             wr += x["reg"]; rd += x.get("off", [])
-        ops.append({"eng": eng, "cost": cost, "fn": fn, "rd": rd, "wr": wr, "lat": lat, "sem": sem, "bias": cur[0], "after": list(after),
+        ops.append({"eng": eng, "cost": cost, "fn": fn, "rd": rd, "wr": wr, "lat": lat, "sem": sem, "bias": cur[0], "after": list(after), "soft": [],
                     "ge": sum(x["n"] for x in ins if isinstance(x, dict) and x.get("ind")), "se": sum(x["n"] for x in outs if x.get("ind")),
                     "ind": any(isinstance(x, dict) and x.get("ind") for x in list(ins) + list(outs))})
         return len(ops) - 1
@@ -229,41 +231,57 @@ def build(g, core, T, topo):
                     trs.append(RemoteDMATransfer(dst_ids=[DstId(rid=rid, pnc=pid)], dma_engine_mask=sum(1 << e for e in es[k]),
                                                  remote_sem=T.sem[sa[k]], src=i["ap"], dst=o["ap"]))
                 return q.remote_dma_fused(trs, local_sem=T.sem[sl])
-        k0 = add("G", 500, fn, [], [i for d, o, i in parts], lat=1500.0, sem=(sl, ne, False))
+        k0 = add("G", 700, fn, [], [i for d, o, i in parts], lat=1500.0, sem=(sl, ne, False))
         for k, (d, o, i) in enumerate(parts):
             add("X", lat, None, [o], [], lat=2000.0, sem=(sa[k], nin[k], False), after=[k0])
         ops[k0]["lat"] = 0.0
         return k0
 
-    w = V // NX
-    for k in range(NX):
-        c = C("XB", k * w, (k + 1) * w)
-        dma("Y", c["ap"], T.pts[:, k * w:(k + 1) * w], [c], [], 2200.0 + 1300 * k)
-        act(C("X", k * w, (k + 1) * w), c)
-    lo8 = slice(0, 8)
-    dma("S", T.WI[:], T.way[:], [R("WI")], [], 3000.0)
-    dma("S", T.ZI[0:8, 0:256], T.cnt[:], [C("ZI", 0, 256)], [], 2500.0)
-    dma("S", T.ZI[0:8, 256:512], T.th[:], [C("ZI", 256, 512)], [], 2500.0)
-    for k in range(NX):
-        send([(cp, C("XR", k * w, (k + 1) * w), C("XB", k * w, (k + 1) * w))], 3600.0)
-        for a, f in ((k * w, act), (k * w + w // 2, cpy)):
-            f(C("X", XW + a, XW + a + w // 2), C("XR", a, a + w // 2))
-    w = V // NC
     h1 = relays(T, topo, rank)[0]
     up = [e for e in topo.engines(core, h1) if e not in topo.engines(core, cp)]
+    line = {}
+
+    def inline(name, k):
+        ops[k]["soft"] = line.get(name, [])
+        line[name] = [k]
+
+    def load(c, src, ns):
+        k = dma("Y", c["ap"], src, [c], [], 2200.0)
+        ops[k]["cost"] = ns
+        inline("Y", k)
+        return k
+
+    def relay(o, i, lat):
+        sl = "l%d" % cnt["l"]; cnt["l"] += 1
+        sr = "r%d" % cnt["r"]; cnt["r"] += 1
+
+        def fn(q):
+            rid, pid, _ = topo.addr(h1)
+            return q.remote_dma(o["ap"], i["ap"], T.sem[sr], T.sem[sl], pid, rid, sum(1 << e for e in up))
+        k0 = add("G", 500, fn, [], [i], sem=(sl, len(up), False))
+        add("Z", 3.9 * o["n"], None, [o], [], lat=lat, sem=(sr, len(topo.engines(relays(T, topo, (rank + 1) % n)[1], core)), False), after=[k0])
+        return k0
+    lo8 = slice(0, 8)
+    dma("S", T.ZI[:, 512:768], T.way[:], [C("ZI", 512, 768)], [], 3000.0)
+    dma("S", T.ZI[0:8, 0:256], T.cnt[:], [C("ZI", 0, 256)], [], 2500.0)
+    dma("S", T.ZI[0:8, 256:512], T.th[:], [C("ZI", 256, 512)], [], 2500.0)
+    for a, b, far in XPIECES:
+        c, o = C("XB", a, b), C("XR", a, b)
+        load(c, T.pts[:, a:b], 1.2 * (b - a))
+        act(C("X", a, b), c)
+        k0 = relay(o, c, 9000.0) if far else send([(cp, o, c)], 3.9 * (b - a))
+        inline("G", k0)
+        if a == 0:
+            gate = k0 + 1
+        m = (a + b) // 2
+        act(C("X", XW + a, XW + m), C("XR", a, m)); cpy(C("X", XW + m, XW + b), C("XR", m, b))
+    w = V // NC
     for k in range(NC):
         c = C("CI", k * w, (k + 1) * w)
-        dma("Y", c["ap"], T.cand[:, k * w:(k + 1) * w], [c], [], 7500.0 + 2000 * k)
+        ops[load(c, T.cand[:, k * w:(k + 1) * w], 2.4 * w)]["after"].append(gate)
         for a in range(k * w, (k + 1) * w, 464):
             ts(C("CU", a, a + 464), C("CI", a, a + 464), -2048.0, ALU.add)
-        o, i = C("CN", k * w, (k + 1) * w), C("CU", k * w, (k + 1) * w)
-        sl = "l%d" % cnt["l"]; cnt["l"] += 1
-
-        def fn(q, o=o, i=i, sl=sl, k=k):
-            rid, pid, _ = topo.addr(h1)
-            return q.remote_dma(o["ap"], i["ap"], T.sem["r%d" % k], T.sem[sl], pid, rid, sum(1 << e for e in up))
-        k0 = add("G", 500, fn, [], [i], lat=1500.0, sem=(sl, len(up), False))
-        add("Z", 3600.0, None, [o], [], lat=14000.0, sem=("r%d" % k, len(topo.engines(relays(T, topo, (rank + 1) % n)[1], core)), False), after=[k0])
+        inline("G", relay(C("CN", k * w, (k + 1) * w), C("CU", k * w, (k + 1) * w), 10000.0))
     ms(C("X", V, XW), DEAD_O); ms(C("X", XW + V, 2 * XW), DEAD_P)
     ms(C("DK", 0, 128), DEAD_O); ms(C("DK", 128, 256), DEAD_P)
 
@@ -291,20 +309,20 @@ def build(g, core, T, topo):
     IDF, ONE = R("MF", 0), R("MF", 1)
     ts(IDF, x128, pf(0), ALU.is_equal)
     cpy(ID, IDF)
-    for o, x in ((NI, -1.0), (PEN, 0.125), (SI, SENT), (N4, -4096.0), (NS, -SENT), (BI, 131072.0)):
+    for o, x in ((NI, -1.0), (PEN, 0.125), (SI, SENT), (N4, -4096.0), (NS, -SENT), (BI, 2.0 ** 43)):
         ts(o, ID, x, ALU.mult)
     ms(ONE, 1.0)
-    SEL1, SEL2, SELN = C("SEL", 0, 8), C("SEL", 8, 16), C("SEL", 16, 24)
-    for o, x in ((SEL1, 2.0 ** -16), (SEL2, 2.0 ** -15), (SELN, -2.0 ** -16)):
+    SEL1, SEL2, SELN, SEL8 = C("SEL", 0, 8), C("SEL", 8, 16), C("SEL", 16, 24), C("SEL", 24, 32)
+    for o, x in ((SEL1, 2.0 ** -16), (SEL2, 2.0 ** -15), (SELN, -2.0 ** -16), (SEL8, -2.0 ** -8)):
         ts(o, C("XI", 0, 8), pf(3), ALU.is_equal, x, ALU.mult)
     ms(C("TM", 0, 16), 0.5); ms(C("TM", 16, 32), 0.0)
     scan(C("TM", 32, 48), C("TM", 0, 16), C("TM", 16, 32), ALU.mult, ALU.add, 2.0)
     ts(C("TM", 48, 64), C("XI", 0, 16), pf(1), ALU.is_equal)
     tt(C("TM", 48, 64), C("TM", 48, 64), C("TM", 32, 48), ALU.mult)
     red(pf(14), C("TM", 48, 64))
-    ts(pf(15), pf(14), 4.0, ALU.mult)
+    ts(pf(15), pf(14), 2.0 ** 28, ALU.mult)
     K16, RST, VRS, MW, KH, KP8, CAP, COH, DUMC, SM8 = (C("KF", 0, 256), C("KF", 256, 384), C("KF", 384, 512), C("KF", 512, 768), C("KF", 768, 896),
-                                                       C("KF", 896, 960), C("KF", 960, 1216), C("KF", 1216, 1264), C("KF", 1264, 1296), C("KF", 1296, 1304))
+                                                       C("KF", 896, 960), C("KF", 960, 1216), C("KF", 1216, 1264), C("KF", 1312, 1376), C("KF", 1296, 1304))
     KAB, KLH, CDN = C("KF", 1376, 1632), C("KF", 1632, 1888), C("KF", 1888, 2016)
     iota(K16, [[0, 16], [1, 16]])
     iota(C("KB", 640, 768), [[1, 8], [0, 16]])
@@ -312,21 +330,23 @@ def build(g, core, T, topo):
     for q_ in range(2):
         iota(C("KF", 960 + 128 * q_, 1088 + 128 * q_), [[0, 8], [1, 8], [1, 2]], 4 - q_)
         iota(C("KF", 1376 + 128 * q_, 1504 + 128 * q_), [[16, 8], [2, 8], [2 - 2 * q_, 2]], q_)
-    iota(DUMC, [[128, 2], [0, 2], [16, 8]], DUM)
+    for k in range(4):
+        iota(C("KF", 1312 + 16 * k, 1328 + 16 * k), [[16, 8], [0, 2]], DUM - 4096 + 128 * (k // 2))
     iota(C("TM", 64, 70), [[2, 6]], 1); iota(C("TM", 70, 77), [[2, 7]])
     k128 = C("KF", 0, 128)
     ts(GEQ, C("KB", 640, 768), pf(3), ALU.is_equal)
-    ts(BO8, GEQ, 8.0, ALU.mult)
+    ts(BO8, GEQ, 2.0 ** 29, ALU.mult)
     ts(R("MB", 10), GEQ, 2.0 ** -15, ALU.mult)
-    ts(BOW, GEQ, pf(14), ALU.mult)
+    ts(BOW, GEQ, pf(14), ALU.mult, 2.0 ** 26, ALU.mult)
     ts(SM8, C("XI", 0, 8), pf(3), ALU.is_equal)
     ts(RST, k128, 0.0, ALU.is_equal, 4.0, ALU.mult)
     ts(MW, K16, pf(1), ALU.is_equal)
     act(VRS, k128, AF.Sign)
-    act(VRS, VRS, AF.Identity, -1.0e6, 2.0e6)
+    act(VRS, VRS, AF.Identity, -2.0 ** 50, 2.0 ** 51)
     act(KH, k128, AF.Identity, 0.0, 0.5)
     ts(DUMC, DUMC, pf(1), ALU.add)
-    ICON, ICE, MASK, K2 = C("KB", 0, 128), C("KB", 128, 256), C("KB", 256, 384), C("KB", 384, 512)
+    ms(C("KF", 1312, 1376, 2), -2.0 ** 50)
+    ICON, ICE, MASK, K2, LIV = C("KB", 0, 128), C("KB", 128, 256), C("KB", 256, 384), C("KB", 384, 512), C("KB", 768, 896)
     act(ICON, k128, AF.Identity, 0.0, 2.0 ** -20)
     act(ICE, k128, AF.Identity, 0.0, 2.0 ** -20)
     ms(C("KB", 143, 256, 16), 0.0)
@@ -335,8 +355,13 @@ def build(g, core, T, topo):
     ts(CDN, k128, 0.0, ALU.is_equal, 1001.0, ALU.mult)
     act(CDN, CDN, AF.Identity, -1.0)
     ms(C("KF", 975, 1216, 16), -1.0)
-    act(MASK, C("KF", 512, 640), AF.Identity, -65536.0, 65536.0)
+    ts(C("XA0", 0, 128), C("KF", 512, 640), pf(15), ALU.mult)
+    act(C("XA0", 128, 256), C("KF", 512, 640), AF.Identity, -2.0 ** 42, 2.0 ** 42)
+    tt(MASK, C("XA0", 128, 256), C("XA0", 0, 128), ALU.subtract)
+    iota(LIV, [[0, 64], [-144, 2]], 224)
     ms(K2, 2048.0)
+    for k in range(6):
+        ts(C("EXP", 128 * k, 128 * k + 128), C("KB", 640, 768), 8.0 * k, ALU.add, pf(0), ALU.is_equal)
     ts(C("TM", 64, 77), C("TM", 64, 77), pf(1), ALU.is_equal, pf(6), ALU.add)
     for k in range(13):
         ts(R("EK", k), GEQ, C("TM", 64 + k, 65 + k), ALU.mult)
@@ -345,8 +370,6 @@ def build(g, core, T, topo):
     for k in range(2):
         tt(C("SAB", 128 * k, 128 * k + 128), C("SAB", 128 * k, 128 * k + 128), C("KB", 512, 640), ALU.add)
     ms(C("SAB", 15, 256, 16), 0.0)
-    for k in range(8):
-        iota(C("IOT", 480 * k, 480 * k + 480), [[1, 480]], 480 * k + 1)
     lists = {}
     pos = [0]
 
@@ -373,8 +396,8 @@ def build(g, core, T, topo):
 
     XOw, XPw, XO, XP = C("X", 0, DUM), C("X", XW, XW + DUM), C("X", 0, XW), C("X", XW, 2 * XW)
 
-    ts(R("WF"), R("WI"), -2048.0, ALU.add)
-    cpy(R("ZF", p=lo8), R("ZI", p=lo8))
+    ts(R("WF"), C("ZI", 512, 768), -2048.0, ALU.add)
+    cpy(R("ZF", p=lo8), C("ZI", 0, 512, p=lo8))
     for h in range(2):
         H = str(h)
         ts(C("PW" + H, 128, 144), C("XI", 0, 16), 0.0, ALU.mult)
@@ -420,9 +443,8 @@ def build(g, core, T, topo):
         D = C("pD" + H, 0, 128)
         parts = [[(D, ID, ICE), (C("pD" + H, 15, 128, 16), IDF, C("TH" if rnd == 0 else "THR", 8 * h, 8 * h + 8))]]
         if rnd > 0:
-            mm([(C("pD" + H, 128, 256), ID, ICE)] + [(C("pD" + H, 128 + k, 256, 16), C("D" + H, k, 2048, 16), SEL1) for k in range(16)])
-            ts(C("W2" + H, 0, 128), C("pD" + H, 128, 256), 0.125, ALU.is_lt, 64.0, ALU.mult)
-            scan(C("W2" + H, 128, 256), CDN, C("W2" + H, 0, 128), ALU.add, ALU.min)
+            mm([(C("pD" + H, 128, 256), ID, LIV)] + [(C("pD" + H, 128 + k, 256, 16), C("D" + H, k, 2048, 16), SEL8) for k in range(16)])
+            scan(C("W2" + H, 128, 256), CDN, C("pD" + H, 128, 256), ALU.add, ALU.min)
             J15 = C("W2" + H, 143, 256, 16)
             act(sm(0), R("IX" + H), AF.Identity, -15.0)
             ts(sm(3), J15, 16.0, ALU.add)
@@ -453,8 +475,12 @@ def build(g, core, T, topo):
         for k in range(2):
             scan(C("PL" + H, 128 * k, 128 * k + 128), R("NN" + H), C("pI" + H, 128 + 128 * k, 256 + 128 * k), ALU.mult, ALU.max)
         o = spread(H, "pI", C("PL" + H, 0, 256), L("e16", 0, 16), 2)
+        act(R("WB"), IN(C("PL" + H, 0, 256), L("e16", 0, 16)))
+        for k in range(2):
+            mm([(C("pE" + H, 128 * k, 128 * k + 128), C("WB", 128 * k, 128 * k + 128), IDF)])
+        cpy(C("AS", 16 * h, 16 * h + 16), o)
         ts(C("ABU", 16 * h, 16 * h + 16), o, -1.0, ALU.add)
-        (act if h == 0 else cpy)(C("AS", 16 * h, 16 * h + 16), o)
+        cpy(C("ROW", 256 * h, 256 * h + 256), C("pE" + H, 0, 256))
         if rnd > 0:
             act(R("IX" + H), sm(2), AF.Relu, -1.0)
             ts(sm(8), sm(2), 0.5, ALU.is_lt)
@@ -463,8 +489,11 @@ def build(g, core, T, topo):
             tt(sm(9), sm(9), sm(8), ALU.mult)
             tt(R("OH" + H), IN(C("TS" + H, 0, 8), L("oh", 0, 3)), COH, ALU.is_equal)
             act(C("OH" + H, 40, 48), sm(2), AF.Relu, -1.0)
-            mm([(C("pX" + H, k, 512, 16), ID, C("OH" + H, 0, 32)) for k in range(16)])
-            mm([(C("pE" + H, k, 256, 16), ID, C("OH" + H, 32, 48)) for k in range(16)])
+            lo48 = slice(0, 48)
+            mm([(C("pX" + H, 0, 128, p=lo48), R("OH" + H), ID)])
+            act(R("XE" + H, p=lo48), C("pX" + H, 0, 128, p=lo48))
+            mm([(R("pX" + H), R("XE" + H, p=lo48), C("EXP", 0, 512, p=lo48))])
+            mm([(C("pE" + H, 0, 256), R("XE" + H, p=lo48), C("EXP", 512, 768, p=lo48))])
             for t in range(5):
                 tt(R("PR" + H, t), C(PW, 2 * t, 2 * t + 128), C("pX" + H, 128 * t, 128 * t + 128) if t < 4 else C("pE" + H, 0, 128), ALU.mult)
             tt(R("FL" + H), KH, C("pE" + H, 128, 256), ALU.is_gt)
@@ -493,9 +522,8 @@ def build(g, core, T, topo):
         if h == 1:
             send([(cp, R("AP" + r), C("ABU", 16, 24))], 100.0)
         row = lambda k, a: C("ROW", 256 * h + 128 * k + a, 256 * h + 128 * k + 128)
-        cpy(C("ROW", 256 * h, 256 * h + 256), IN(R("IOT"), C("ABU", 16 * h, 16 * h + 16)))
-        ab, dm = C("AB", 16 * h, 16 * h + 16), C("KF", 1264 + 16 * h, 1280 + 16 * h)
-        act(ab, C("AS", 16 * h, 16 * h + 16), AF.Identity, -1.0)
+        dm = C("KF", 1312 + 32 * h, 1344 + 32 * h)
+        act(C("CS" + H, 129, 160, 2), C("AS", 16 * h, 16 * h + 16), AF.Identity, -4097.0)
         act(C("NP", 8 * h, 8 * h + 8), C("AS", 16 * h, 16 * h + 8), AF.Relu, 1.0, -1.0)
         pc_ = lambda a, b: C("pD" + H, a, b)
         parts = [[(pc_(0, 128), ID, MASK), (C("pD" + H, 0, 128, 16), BI, C("NP", 8 * h, 8 * h + 8))]]
@@ -518,11 +546,10 @@ def build(g, core, T, topo):
                 parts[-1] += part
         parts[-1] += [(pc_(0, 128), BOW, R(E, slice(8 * h, 8 * h + 8), slice(0, 16))) for E in ("EA", "EB")]
         group(parts)
-        scan(R("CS" + H), VRS, pc_(0, 128), ALU.min, ALU.max)
-        ts(C("LS" + H, 16, 32), IN(R("CS" + H), L("c15", 0, 1)), pf(15), ALU.is_ge)
-        tt(C("LS" + H, 32, 48), C("LS" + H, 16, 32), dm, ALU.mult)
-        tt(R("LM", h), C("LS" + H, 32, 48), ab, ALU.max)
-        cpy(C("LW" + r, 16 * h, 16 * h + 16), R("LM", h))
+        scan(C("CS" + H, 0, 128), VRS, pc_(0, 128), ALU.min, ALU.max)
+        cpy(C("CS" + H, 128, 160, 2), IN(C("CS" + H, 0, 128), L("c15", 0, 1)))
+        scan(C("LM", 32 * h, 32 * h + 32), dm, C("CS" + H, 128, 160), ALU.min, ALU.max)
+        ts(C("LW" + r, 16 * h, 16 * h + 16), C("LM", 32 * h + 1, 32 * h + 32, 2), 4096.0, ALU.add)
         ends = [(cp, C("LA" + r, 8 * h, 8 * h + 8), C("LW" + r, 16 * h, 16 * h + 8)),
                 (cq, C("LB" + r, 8 * h, 8 * h + 8), C("LW" + r, 16 * h + 8, 16 * h + 16))]
         if h == 0:
@@ -542,9 +569,9 @@ def build(g, core, T, topo):
         for h in range(2):
             act(IN(XO, C("LB" + r, 8 * h, 8 * h + 8)), C("DK", 0, 128), AF.Silu)
         if rnd < 2:
-            act(C("CT", 8, 24), R("LM", slice(None), 0), AF.Sign, DUM - 0.5, -1.0, C("CT", 0, 1))
+            act(C("CT", 8, 40), C("LM", 1, 64, 2), AF.Sign, DUM - 4096.5, -1.0, C("CT", 0, 1))
             mm([(C("pE1", 256, 257), ONE, C("CT", 0, 1))])
-            ts(C("CTI", 0, 1), C("pE1", 256, 257), 0.5, ALU.mult, 1024.0, ALU.add)
+            ts(C("CTI", 0, 1), C("pE1", 256, 257), 0.25, ALU.mult, 1024.0, ALU.add)
             ts(C("CTI", 1, 2), C("CTI", 0, 1), 31, ALU.bitwise_and)
             ts(C("CT", 1, 2), C("CTI", 1, 2), 2.0 ** -13, ALU.mult)
             act(R("THR"), R("TH"), AF.Identity, C("CT", 1, 2))
@@ -552,7 +579,7 @@ def build(g, core, T, topo):
     def hop(h, j):
         H = str(h)
         cw, xe, xc = (R("CI"), XOw, XPw) if j % 2 == 0 else (R("CP"), XPw, XOw)
-        b0, nb = ((0, 6), (6, 7), (0, 5), (6, 6))[j]
+        b0, nb = ((0, 6), (6, 7))[j % 2]
         cpy(R("OF" + H), IN(cw, R("EX" + H)))
         ts(R("C16" + H), R("OF" + H), -2048.0, ALU.add)
         if j == 0 and h in XEV:
@@ -561,20 +588,19 @@ def build(g, core, T, topo):
             act(R("XE" + H), IN(xe, R("EX" + H)))
             if j == 0:
                 ts(R("XE" + H), R("XE" + H), 255.0, ALU.min)
-        gathers(H, xc, "OF" + H, HB, HV)
+        gathers(H, xc, "OF" + H, HB, HV[h][j])
         IC = C("pI" + H, 0, 128)
         mm([(IC, R("C16" + H), ID)])
-        act(R("CW" + H), IC, AF.Identity, 2048.0)
-        mm([(IC, ID, K2), (IC, R("C16" + H), ID)], True, False)
+        if CWE == "S":
+            act(R("CW" + H), IC, AF.Identity, 2048.0)
+        else:
+            ts(R("CW" + H), IC, 2048.0, ALU.add)
         mm([(C("pX" + H, d, 512, 4), ID, R("XE" + H)) for d in range(4)])
-        for a in range(0, nb, 4):
-            e = min(4, nb - a)
-            mm([(C("pE" + H, 0, 128 * e), R("PB" + H), R("EK", slice(b0 + a, b0 + a + e)))])
+        for a, e, bank, c0 in ((0, nb - 3, "pE", 0), (nb - 3, 3, "pI", 128)):
+            mm([(C(bank + H, c0, c0 + 128 * e), R("PB" + H), R("EK", slice(b0 + a, b0 + a + e)))])
             for k in range(e):
-                tt(R("EQ" + H, a + k), R("CW" + H), C("pE" + H, 128 * k, 128 * k + 128), ALU.is_equal)
-        if j > 1:
-            tt(R("EQ" + H, nb), IN(C("PL" + H, 128 * j - 256, 128 * j - 128), L("e16", 0, 8)), R("CW" + H), ALU.is_equal)
-            nb += 1
+                tt(R("EQ" + H, a + k), R("CW" + H), C(bank + H, c0 + 128 * k, c0 + 128 * k + 128), ALU.is_equal)
+        mm([(IC, ID, K2), (IC, R("C16" + H), ID)], True, False)
         ns = SH[h][j]
         fix = []
         if ns:
@@ -589,7 +615,9 @@ def build(g, core, T, topo):
             a += m
         D = C("pD" + H, 0, 128)
         col = lambda i: C("pD" + H, i, 128, 16)
-        group([[(D, ID, ICON)] + fix + [(D, PEN, R("EQ" + H, k)) for k in range(nb)], [(col(i), C("D" + H, i, 2048, 16), SELN) for i in range(16)]] +
+        pen = [(D, PEN, R("EQ" + H, k)) for k in range(nb)]
+        group([[(D, ID, ICON)] + fix + pen[:nb - 3], pen[nb - 3:]] +
+              [[(col(i), C("D" + H, i, 2048, 16), SELN) for i in range(q, 16, RAWP)] for q in range(RAWP)] +
               [[(col(i), C("A" + H, i, 2048, 16), SEL2) for i in range(q, 16, 4)] for q in range(4)])
         scan(R("R" + H, j), RST, D, ALU.max, ALU.min)
         tt(R("NN" + H), D, R("R" + H, j), ALU.not_equal)
@@ -612,8 +640,11 @@ def build(g, core, T, topo):
             tt(sm(15), sm(13), sm(12), ALU.mult)
             tt(R("FL" + H), IN(sm(15), L("r16", 0, 8)), cap, ALU.not_equal)
             act(R("W1" + H), val, AF.Identity, -2048.0)
+            bk = C("pE" + H, 128, 256)
             mm([(bk, SI, R("FL" + H)), (bk, IDF, R("W1" + H))])
             tt(PW, PW, bk, ALU.min)
+            mm([(C("pE" + H, 0, 128), PW, ID)])
+            ts(R("PB" + H), C("pE" + H, 0, 128), pf(13), ALU.add)
             tt(R("IX" + H), R("IX" + H), sm(13), ALU.add)
             return
         for k in range(2):
@@ -685,7 +716,7 @@ def order(ops):
     bank = {}
     pred = []
     for k, o in enumerate(ops):
-        p = set(o["after"])
+        p = set(o["after"] + o["soft"])
         for w, regs in ((False, o["rd"]), (True, o["wr"])):
             for name, bits in regs:
                 if SCRATCH[name][0] == "psum":
@@ -736,31 +767,34 @@ def order(ops):
                 rdy[j] = max(fin[i] + LAT for i in pred[j])
 
     def gap(j, k):
-        return 0.0 if ops[j]["eng"] == "P" and ops[k]["eng"] == "P" else ops[j]["lat"] + LAT
+        return 0.0 if ops[j]["eng"] == "P" and ops[k]["eng"] == "P" or j in ops[k]["soft"] else ops[j]["lat"] + LAT
 
     def place(lst, back):
-        busy = {}
+        busy = {e: ([], []) for e in set(eng)}
         end = [0.0] * n
+        near = after if back else before
         for k in lst:
-            c = max(ops[k]["cost"], 1.0)
-            if back:
-                s = max([end[j] + gap(k, j) for j in succ[k]] + [ops[k]["lat"]])
-            else:
-                s = max([end[j] + gap(j, k) for j in pred[k]] + [0.0])
-            b = busy.setdefault(ops[k]["eng"], [])
-            lo, hi = 0, len(b)
-            while lo < hi:
-                mid = (lo + hi) // 2
-                if b[mid][1] <= s:
-                    lo = mid + 1
-                else:
-                    hi = mid
-            while lo < len(b) and b[lo][0] < s + c:
-                s = max(s, b[lo][1])
+            c = cost0[k]
+            s = ops[k]["lat"] if back else 0.0
+            for j, d in near[k]:
+                if end[j] + d > s:
+                    s = end[j] + d
+            b0, b1 = busy[eng[k]]
+            lo = m = len(b0)
+            while lo and b1[lo - 1] > s:
+                lo -= 1
+            while lo < m and b0[lo] < s + c:
+                if b1[lo] > s:
+                    s = b1[lo]
                 lo += 1
-            b.insert(lo, (s, s + c))
+            b0.insert(lo, s)
+            b1.insert(lo, s + c)
             end[k] = s + c
         return end
+    eng = [o["eng"] for o in ops]
+    cost0 = [max(o["cost"], 1.0) for o in ops]
+    before = [[(j, gap(j, k)) for j in pred[k]] for k in range(n)]
+    after = [[(j, gap(k, j)) for j in succ[k]] for k in range(n)]
     end = place(seq, False)
     best = None
     for _ in range(PASSES):
@@ -772,33 +806,38 @@ def order(ops):
     cases = []
     for dg, ds, pe, lat in CASES:
         cases.append(([(o["cost"] + dg * o["ge"] + ds * o["se"]) * (pe if o["eng"] == "P" else 1.0) for o in ops],
-                      [[(j, 0.0 if ops[j]["eng"] == "P" and ops[k]["eng"] == "P" else ops[j]["lat"] + lat) for j in pred[k]] for k in range(n)]))
+                      [[(j, gap(j, k) and ops[j]["lat"] + lat) for j in pred[k]] for k in range(n)]))
 
     def judge(end):
-        lst = sorted(range(n), key=lambda k: (end[k] - max(ops[k]["cost"], 1.0), k))
+        start = [end[k] - cost0[k] for k in range(n)]
+        lst = sorted(range(n), key=lambda k: start[k])
         total = 0.0
         for cost, gaps in cases:
-            free, fin = {}, [0.0] * n
+            free, fin = dict.fromkeys(eng, 0.0), [0.0] * n
             for k in lst:
-                e = ops[k]["eng"]
-                s = free.get(e, 0.0)
+                s = free[eng[k]]
                 for j, d in gaps[k]:
                     if fin[j] + d > s:
                         s = fin[j] + d
-                free[e] = fin[k] = s + cost[k]
-            total += max(fin[k] + ops[k]["lat"] for k in range(n))
+                free[eng[k]] = fin[k] = s + cost[k]
+            total += max(fin[k] + ops[k]["lat"] for k in last)
         return total / len(cases)
+    last = [k for k in range(n) if not succ[k]]
     best = (judge(best[1]), best[1])
     for it in range(SHAKES):
-        key = [0.0] * n
+        key = list(best[1])
         x = (x * 1103515245 + 12345) % 2147483648
-        t0 = max(best[1]) * x / 2147483648.0
+        t0 = max(key) * x / 2147483648.0
         for k in range(n):
-            x = (x * 1103515245 + 12345) % 2147483648
-            near = abs(best[1][k] - t0) < SPAN
-            key[k] = max([best[1][k] + near * SHAKE * x / 2147483648.0] + [key[j] + 0.01 for j in pred[k]])
+            if t0 - SPAN < key[k] < t0 + SPAN:
+                x = (x * 1103515245 + 12345) % 2147483648
+                key[k] += SHAKE * x / 2147483648.0
+            if t0 - SPAN < key[k] < t0 + SPAN + 3 * SHAKE:
+                for j in pred[k]:
+                    if key[j] >= key[k]:
+                        key[k] = key[j] + 0.01
         end = place(sorted(range(n), key=lambda k: -key[k]), True)
-        end = place(sorted(range(n), key=lambda k: (-end[k], k)), False)
+        end = place(sorted(range(n), key=lambda k: -end[k]), False)
         span = judge(end)
         if span < best[0] + SLACK:
             best = (span, end)
@@ -830,7 +869,7 @@ def rank_program(g, core, T, topo):
             continue
         need = {}
         for j in pred[k]:
-            if e == "P" and ops[j]["eng"] == "P":
+            if e == "P" and ops[j]["eng"] == "P" or j in o["soft"]:
                 continue
             s, v = tok[j]
             if need.get(s, (0, 0))[0] < v:

from concourse.bass import DstId, RemoteDMATransfer
from concourse.mybir import AluOpType as ALU, AxisListType as AX, ActivationFunctionType as AF

V = 3712
SENT = 3712.0
DUM = 3728
XW = DUM + 256
DEAD_O, DEAD_P = 3584.0, 1280.0
MAGIC = 12582912.0
HB = (32, 32, 16, 32, 16)
HV = (((0, 2), (2,), (2,), (2,)), ((2,), (2,), (2,), (2,)))
EB = (32, 32, 32, 32)
EV = (((0, 2), (0, 2)), ((0,), (0, 2)))
SH = ((64, 64, 64, 64), (64, 64, 64, 64))
CASES = ((-0.3, 0.0, 1.0, 230.0), (0.3, 0.0, 1.0, 160.0), (0.0, 0.0, 1.0, 200.0))
FAST, XEV, CWE, RAWP = (0, 1), (0,), "V", 2
PENAT = 1
SHAKES, SHAKE, SLACK, SPAN = 3800, 1000.0, 20.0, 2500.0
BIASE = 2500.0
BIAS = 2500.0
LAT = 220.0
PE = 0.55
SEED = 36
NOISE = 300.0
WIN = 30.0
PASSES = 8
XPIECES = ((0, 464, 0), (464, 1024, 1), (1024, 1584, 1), (1584, 2416, 0), (2416, 3248, 0), (3248, V, 0))
NC = 4
CORES_ALL = 128

F, B, I, U, H16 = "float32", "bfloat16", "int32", "uint16", "float16"
SCRATCH = {}
PLAN = []


def _sb(name, shape, dt):
    SCRATCH[name] = ("sbuf", [128] + shape, dt)


for _n, _s, _d in [
    ("X", [2 * XW], F), ("XB", [V], B), ("XR", [V], B), ("CI", [V], I), ("CP", [V], F), ("CU", [V], H16), ("CN", [V], H16),
    ("WB", [256], F), ("WF", [256], F), ("ZI", [768], I), ("ZF", [512], F),
    ("PC", [16], I), ("PF", [24], F), ("XI", [128], F), ("MB", [11, 128], B), ("MF", [2, 128], F), ("SEL", [32], B),
    ("KF", [2016], F), ("KB", [896], B), ("EK", [13, 128], B), ("SAB", [256], B),
    ("LI", [128], I), ("LF", [128], F), ("LU", [128], U), ("TM", [80], F),
    ("TH", [16], F), ("THR", [16], F), ("ABU", [32], U), ("AS", [32], F),
    ("ROW", [512], U), ("EA", [16, 256], B), ("EB", [16, 256], B), ("LM", [64], F),
    ("DK", [256], F), ("CT", [40], F), ("CTI", [8], I), ("YC", [256], F), ("YN", [256], F), ("ZZ", [128], F), ("NP", [16], B), ("EXP", [768], B),
]:
    _sb(_n, _s, _d)
for _r in range(3):
    _sb("MID%d" % _r, [256], F); _sb("MIN%d" % _r, [256], F)
    _sb("LW%d" % _r, [32], U); _sb("LA%d" % _r, [16], U); _sb("LB%d" % _r, [16], U); _sb("AP%d" % _r, [8], U)
for _h in range(2):
    for _n, _s, _d in [
        ("PW", [144], H16), ("LP", [128], U), ("PA", [128], H16), ("PB", [128], H16), ("D", [2048], B), ("A", [2048], B),
        ("R", [4, 128], F), ("PL", [512], F), ("NN", [128], B), ("W1", [128], F), ("W2", [256], F), ("W3", [256], B),
        ("SM", [176], F), ("IX", [8], F), ("TS", [16], F), ("OH", [48], B), ("PR", [5, 128], H16), ("FL", [128], B),
        ("EX", [8], U), ("OF", [128], U), ("C16", [128], H16), ("CW", [128], F), ("XE", [128], B), ("WX", [256], F),
        ("EQ", [7, 128], B), ("FD", [2, 8], F), ("XA", [256], B), ("MT", [128], F), ("CS", [160], F),
    ]:
        _sb(_n + str(_h), _s, _d)
    for _n in ("pD", "pX", "pE", "pI"):
        SCRATCH[_n + str(_h)] = ("psum", [128, 512], F)

SEMAPHORES = ["cV", "cS", "cP", "cG"] + ["d%d" % _i for _i in range(24)] + ["l%d" % _i for _i in range(32)] + ["a%d" % _i for _i in range(30)] + ["r%d" % _i for _i in range(8)]


def relays(T, topo, rank):
    core, dst = T.cores[rank], T.cores[(rank - 1) % len(T.cores)]
    far = [c for c in range(CORES_ALL) if topo.mates(topo.chip(c), topo.chip(dst)) and topo.die(c) == topo.die(core) and topo.may_write(c, dst)][0]
    near = [c for c in topo.cores_of(core) if c not in T.cores and topo.die(c) == topo.die(core) and topo.may_write(c, far)][0]
    return near, far


def hand_on(g, core, T, topo):
    n = len(T.cores)
    w = V // NC
    for rank in range(n):
        way = (T.cores[rank],) + relays(T, topo, rank) + (T.cores[(rank - 1) % n],)
        if core in way[1:3]:
            at = way.index(core)
            src, dst = way[at - 1], way[at + 1]
            nin = len([e for e in topo.engines(src, core) if at == 2 or e not in topo.engines(src, way[3])])
            rid, pid, _ = topo.addr(dst)
            pieces = [T.XR[:, a:b] for a, b, far in XPIECES if far] + [T.CN[:, k * w:(k + 1) * w] for k in range(NC)]
            for k, x in enumerate(pieces):
                g.wait_ge(T.sem["r%d" % k], nin)
                g.remote_dma(x, x, T.sem["r%d" % k], T.sem.l0, pid, rid, topo.mask(core, dst))
            g.wait_ge(T.sem.l0, len(pieces) * len(topo.engines(core, dst)))


def build(g, core, T, topo):
    rank = T.rank_of(core)
    n = len(T.cores)
    cp, cq = T.cores[(rank - 1) % n], T.cores[(rank + 1) % n]
    ops = []
    cur = [0.0]
    cnt = {"d": 0, "l": 0, "a": 0, "r": 0}

    def R(name, *idx, p=slice(None)):
        shp = SCRATCH[name][1][1:]
        idx = list(idx) + [slice(None)] * (len(shp) - len(idx))
        bits = 1
        num = 1
        st = 1
        for d in range(len(shp) - 1, -1, -1):
            x = idx[d]
            rg = [x] if isinstance(x, int) else range(*x.indices(shp[d]))
            if st == 1 and len(rg) > 1 and rg[1] - rg[0] == 1:
                bits = ((1 << len(rg)) - 1) << rg[0]
            else:
                bits = sum(bits << (y * st) for y in rg)
            num *= len(rg)
            st *= shp[d]
        return {"ap": T[name][tuple([p] + idx)], "reg": [(name, bits)], "n": num, "dt": SCRATCH[name][2],
                "ps": SCRATCH[name][0] == "psum", "ind": False}

    def C(name, a, b, s=1, p=slice(None)):
        return R(name, slice(a, b, s), p=p)

    def IN(win, off):
        return {"ap": win["ap"].indirect(off["ap"]), "reg": win["reg"], "off": off["reg"], "n": 16 * off["n"], "dt": win["dt"],
                "ps": False, "ind": True}

    def add(eng, cost, fn, outs, ins, lat=0.0, sem=None, after=()):
        rd, wr = [], []
        for x in ins:
            if isinstance(x, dict):
                rd += x["reg"] + x.get("off", [])
        for x in outs:
            wr += x["reg"]; rd += x.get("off", [])
        ops.append({"eng": eng, "cost": cost, "fn": fn, "rd": rd, "wr": wr, "lat": lat, "sem": sem, "bias": cur[0], "after": list(after), "soft": [],
                    "ge": sum(x["n"] for x in ins if isinstance(x, dict) and x.get("ind")), "se": sum(x["n"] for x in outs if x.get("ind")),
                    "ind": any(isinstance(x, dict) and x.get("ind") for x in list(ins) + list(outs))})
        return len(ops) - 1

    def ap(x):
        return x["ap"] if isinstance(x, dict) else x

    def vcost(out, in0, base):
        if in0["ind"]:
            return 60 + 1.56 * in0["n"]
        if out["ind"]:
            return 60 + 3.8 * out["n"]
        return max(64, base * out["n"])

    def half(out, in0):
        return 0.5 if out["dt"] in (B, U, H16) and in0["dt"] in (B, U, H16) else 1.0

    def cpy(out, in0):
        return add("V", vcost(out, in0, half(out, in0)), lambda q: q.tensor_copy(out["ap"], in0["ap"]), [out], [in0])

    def ts(out, in0, s1, op0, s2=None, op1=None):
        if op1 is None:
            fn = lambda q: q.tensor_scalar(out["ap"], in0["ap"], ap(s1), None, op0)
        else:
            fn = lambda q: q.tensor_scalar(out["ap"], in0["ap"], ap(s1), ap(s2), op0, op1)
        return add("V", vcost(out, in0, half(out, in0)), fn, [out], [in0, s1, s2])

    def tt(out, in0, in1, op):
        base = 1.0 if in0["ps"] or in1["ps"] else 2.0
        return add("V", vcost(out, in0, base), lambda q: q.tensor_tensor(out["ap"], in0["ap"], in1["ap"], op), [out], [in0, in1])

    def scan(out, d0, d1, op0, op1, init=0.0):
        return add("V", max(64, out["n"]), lambda q: q.tensor_tensor_scan(out["ap"], d0["ap"], d1["ap"], init, op0, op1), [out], [d0, d1])

    def red(out, in0):
        return add("V", max(64, in0["n"]), lambda q: q.tensor_reduce(out["ap"], in0["ap"], AX.X, ALU.add), [out], [in0])

    def ms(out, val):
        return add("V", max(64, out["n"] * (0.5 if out["dt"] == B else 1)), lambda q: q.memset(out["ap"], val), [out], [])

    def act(out, in0, func=AF.Identity, bias=0.0, scale=1.0, acc=None):
        cost = 80 + 1.56 * in0["n"] if in0["ind"] else 40 + max(64, in0["n"])
        if out["ind"]:
            return add("S", 80 + 3.8 * in0["n"], lambda q: q.activation(out["ap"], in0["ap"], func), [out], [in0])
        if acc:
            return add("S", cost, lambda q: q.activation(out["ap"], in0["ap"], func, bias=bias, scale=scale, accum_out=acc["ap"]), [out, acc], [in0])
        return add("S", cost, lambda q: q.activation(out["ap"], in0["ap"], func, bias=ap(bias), scale=scale), [out], [in0, bias])

    def mm(items, first=True, last=True):
        def fn(q):
            ins = None
            for k, (o, l, r) in enumerate(items):
                ins = q.matmul(o["ap"], l["ap"], r["ap"], first and k == 0, last and k == len(items) - 1)
            return ins
        cost = sum(PE * max(min(64, l["n"]), r["n"]) * (4 if r["dt"] == F else 1) for o, l, r in items)
        return add("P", cost, fn, [R(items[0][0]["reg"][0][0])], [x for o, l, r in items for x in (l, r)], lat=60.0)

    def group(parts):
        for j, part in enumerate(parts):
            mm(part, j == 0, j == len(parts) - 1)

    def iota(out, pat, base=0, cm=0):
        if out["dt"] == I:
            fn = lambda q: q.iota(out["ap"], pat, base, cm)
        else:
            fn = lambda q: q.iota(out["ap"], pat, base, cm, allow_small_or_imprecise_dtypes=True)
        return add("G", 160 + 2 * out["n"], fn, [out], [])

    def dma(eng, o, i, outs, ins, lat):
        s = "d%d" % cnt["d"]; cnt["d"] += 1
        return add(eng, 60, lambda q: q.dma_start(o, i), outs, ins, lat=lat, sem=(s, 16, True))

    def send(parts, lat):
        sl = "l%d" % cnt["l"]; cnt["l"] += 1
        sa = []
        for _ in parts:
            sa.append("a%d" % cnt["a"]); cnt["a"] += 1
        if len(parts) == 1:
            dst, o, i = parts[0]
            ne = len(topo.engines(core, dst))
            nin = [len(topo.engines(cq if dst == cp else cp, core))]

            def fn(q):
                rid, pid, _ = topo.addr(dst)
                return q.remote_dma(o["ap"], i["ap"], T.sem[sa[0]], T.sem[sl], pid, rid, topo.mask(core, dst))
        else:
            def share(a, b, c, k):
                e = [x for x in topo.engines(a, b) if x in topo.engines(a, c)]
                return e[:len(e) // 2] if k == 0 else e[len(e) // 2:]
            es = [share(core, cp, cq, 0), share(core, cp, cq, 1)]
            ne = len(es[0]) + len(es[1])
            nin = [len(share(cq, core, T.cores[(rank + 2) % n], 0)), len(share(cp, T.cores[(rank - 2) % n], core, 1))]

            def fn(q):
                trs = []
                for k, (dst, o, i) in enumerate(parts):
                    rid, pid, _ = topo.addr(dst)
                    trs.append(RemoteDMATransfer(dst_ids=[DstId(rid=rid, pnc=pid)], dma_engine_mask=sum(1 << e for e in es[k]),
                                                 remote_sem=T.sem[sa[k]], src=i["ap"], dst=o["ap"]))
                return q.remote_dma_fused(trs, local_sem=T.sem[sl])
        k0 = add("G", 700, fn, [], [i for d, o, i in parts], lat=1500.0, sem=(sl, ne, False))
        for k, (d, o, i) in enumerate(parts):
            add("X", lat, None, [o], [], lat=2000.0, sem=(sa[k], nin[k], False), after=[k0])
        ops[k0]["lat"] = 0.0
        return k0

    h1 = relays(T, topo, rank)[0]
    up = [e for e in topo.engines(core, h1) if e not in topo.engines(core, cp)]
    line = {}

    def inline(name, k):
        ops[k]["soft"] = line.get(name, [])
        line[name] = [k]

    def load(c, src, ns):
        k = dma("Y", c["ap"], src, [c], [], 2200.0)
        ops[k]["cost"] = ns
        inline("Y", k)
        return k

    def relay(o, i, lat):
        sl = "l%d" % cnt["l"]; cnt["l"] += 1
        sr = "r%d" % cnt["r"]; cnt["r"] += 1

        def fn(q):
            rid, pid, _ = topo.addr(h1)
            return q.remote_dma(o["ap"], i["ap"], T.sem[sr], T.sem[sl], pid, rid, sum(1 << e for e in up))
        k0 = add("G", 500, fn, [], [i], sem=(sl, len(up), False))
        add("Z", 3.9 * o["n"], None, [o], [], lat=lat, sem=(sr, len(topo.engines(relays(T, topo, (rank + 1) % n)[1], core)), False), after=[k0])
        return k0
    lo8 = slice(0, 8)
    dma("S", T.ZI[:, 512:768], T.way[:], [C("ZI", 512, 768)], [], 3000.0)
    dma("S", T.ZI[0:8, 0:256], T.cnt[:], [C("ZI", 0, 256)], [], 2500.0)
    dma("S", T.ZI[0:8, 256:512], T.th[:], [C("ZI", 256, 512)], [], 2500.0)
    for a, b, far in XPIECES:
        c, o = C("XB", a, b), C("XR", a, b)
        load(c, T.pts[:, a:b], 1.2 * (b - a))
        act(C("X", a, b), c)
        k0 = relay(o, c, 9000.0) if far else send([(cp, o, c)], 3.9 * (b - a))
        inline("G", k0)
        if a == 0:
            gate = k0 + 1
        m = (a + b) // 2
        act(C("X", XW + a, XW + m), C("XR", a, m)); cpy(C("X", XW + m, XW + b), C("XR", m, b))
    w = V // NC
    for k in range(NC):
        c = C("CI", k * w, (k + 1) * w)
        ops[load(c, T.cand[:, k * w:(k + 1) * w], 2.4 * w)]["after"].append(gate)
        for a in range(k * w, (k + 1) * w, 464):
            ts(C("CU", a, a + 464), C("CI", a, a + 464), -2048.0, ALU.add)
        inline("G", relay(C("CN", k * w, (k + 1) * w), C("CU", k * w, (k + 1) * w), 10000.0))
    ms(C("X", V, XW), DEAD_O); ms(C("X", XW + V, 2 * XW), DEAD_P)
    ms(C("DK", 0, 128), DEAD_O); ms(C("DK", 128, 256), DEAD_P)

    pc = lambda k: C("PC", k, k + 1)
    pf = lambda k: C("PF", k, k + 1)
    iota(pc(0), [[0, 1]], 0, 1)
    ts(pc(1), pc(0), 15, ALU.bitwise_and)
    ts(pc(2), pc(0), 1, ALU.bitwise_and)
    ts(pc(3), pc(0), 4, ALU.logical_shift_right)
    ts(pc(4), pc(0), 7, ALU.bitwise_and)
    cpy(C("PF", 0, 5), C("PC", 0, 5))
    ts(pf(5), pf(2), float(XW), ALU.mult)
    ts(pf(6), pf(1), 15.0, ALU.is_equal)
    ts(pf(7), pf(6), 4096.0 - SENT, ALU.mult, -2048.0, ALU.add)
    tt(pf(8), pf(7), pf(5), ALU.subtract)
    ts(pf(9), pf(6), -1.0, ALU.mult, 1.0, ALU.add)
    tt(pf(9), pf(9), pf(8), ALU.add)
    ts(pf(10), pf(2), -128.0, ALU.mult)
    ts(pf(11), pf(4), 16.0, ALU.mult)
    ts(pf(12), pf(5), 2048.0, ALU.add)
    ts(pf(13), pf(7), 2048.0, ALU.add)
    iota(R("XI"), [[1, 128]])
    x128 = R("XI")
    ID, NI, PEN, SI, BO8, BOW, N4, GEQ, NS, BI = [R("MB", k) for k in range(10)]
    IDF, ONE = R("MF", 0), R("MF", 1)
    ts(IDF, x128, pf(0), ALU.is_equal)
    cpy(ID, IDF)
    for o, x in ((NI, -1.0), (PEN, 0.125), (SI, SENT), (N4, -4096.0), (NS, -SENT), (BI, 2.0 ** 43)):
        ts(o, ID, x, ALU.mult)
    ms(ONE, 1.0)
    SEL1, SEL2, SELN, SEL8 = C("SEL", 0, 8), C("SEL", 8, 16), C("SEL", 16, 24), C("SEL", 24, 32)
    for o, x in ((SEL1, 2.0 ** -16), (SEL2, 2.0 ** -15), (SELN, -2.0 ** -16), (SEL8, -2.0 ** -8)):
        ts(o, C("XI", 0, 8), pf(3), ALU.is_equal, x, ALU.mult)
    ms(C("TM", 0, 16), 0.5); ms(C("TM", 16, 32), 0.0)
    scan(C("TM", 32, 48), C("TM", 0, 16), C("TM", 16, 32), ALU.mult, ALU.add, 2.0)
    ts(C("TM", 48, 64), C("XI", 0, 16), pf(1), ALU.is_equal)
    tt(C("TM", 48, 64), C("TM", 48, 64), C("TM", 32, 48), ALU.mult)
    red(pf(14), C("TM", 48, 64))
    ts(pf(15), pf(14), 2.0 ** 28, ALU.mult)
    K16, RST, VRS, MW, KH, KP8, CAP, COH, DUMC, SM8 = (C("KF", 0, 256), C("KF", 256, 384), C("KF", 384, 512), C("KF", 512, 768), C("KF", 768, 896),
                                                       C("KF", 896, 960), C("KF", 960, 1216), C("KF", 1216, 1264), C("KF", 1312, 1376), C("KF", 1296, 1304))
    KAB, KLH, CDN = C("KF", 1376, 1632), C("KF", 1632, 1888), C("KF", 1888, 2016)
    iota(K16, [[0, 16], [1, 16]])
    iota(C("KB", 640, 768), [[1, 8], [0, 16]])
    iota(COH, [[1, 6], [0, 8]])
    for q_ in range(2):
        iota(C("KF", 960 + 128 * q_, 1088 + 128 * q_), [[0, 8], [1, 8], [1, 2]], 4 - q_)
        iota(C("KF", 1376 + 128 * q_, 1504 + 128 * q_), [[16, 8], [2, 8], [2 - 2 * q_, 2]], q_)
    for k in range(4):
        iota(C("KF", 1312 + 16 * k, 1328 + 16 * k), [[16, 8], [0, 2]], DUM - 4096 + 128 * (k // 2))
    iota(C("TM", 64, 70), [[2, 6]], 1); iota(C("TM", 70, 77), [[2, 7]])
    k128 = C("KF", 0, 128)
    ts(GEQ, C("KB", 640, 768), pf(3), ALU.is_equal)
    ts(BO8, GEQ, 2.0 ** 29, ALU.mult)
    ts(R("MB", 10), GEQ, 2.0 ** -15, ALU.mult)
    ts(BOW, GEQ, pf(14), ALU.mult, 2.0 ** 26, ALU.mult)
    ts(SM8, C("XI", 0, 8), pf(3), ALU.is_equal)
    ts(RST, k128, 0.0, ALU.is_equal, 4.0, ALU.mult)
    ts(MW, K16, pf(1), ALU.is_equal)
    act(VRS, k128, AF.Sign)
    act(VRS, VRS, AF.Identity, -2.0 ** 50, 2.0 ** 51)
    act(KH, k128, AF.Identity, 0.0, 0.5)
    ts(DUMC, DUMC, pf(1), ALU.add)
    ms(C("KF", 1312, 1376, 2), -2.0 ** 50)
    ICON, ICE, MASK, K2, LIV = C("KB", 0, 128), C("KB", 128, 256), C("KB", 256, 384), C("KB", 384, 512), C("KB", 768, 896)
    act(ICON, k128, AF.Identity, 0.0, 2.0 ** -20)
    act(ICE, k128, AF.Identity, 0.0, 2.0 ** -20)
    ms(C("KB", 143, 256, 16), 0.0)
    iota(C("KF", 1632, 1760), [[0, 8], [2, 8], [0, 2]]); iota(C("KF", 1760, 1888), [[0, 8], [-2, 8], [0, 2]], 13)
    ms(C("KF", 1647, 1888, 16), 99.0)
    ts(CDN, k128, 0.0, ALU.is_equal, 1001.0, ALU.mult)
    act(CDN, CDN, AF.Identity, -1.0)
    ms(C("KF", 975, 1216, 16), -1.0)
    ts(C("XA0", 0, 128), C("KF", 512, 640), pf(15), ALU.mult)
    act(C("XA0", 128, 256), C("KF", 512, 640), AF.Identity, -2.0 ** 42, 2.0 ** 42)
    tt(MASK, C("XA0", 128, 256), C("XA0", 0, 128), ALU.subtract)
    iota(LIV, [[0, 64], [-144, 2]], 224)
    ms(K2, 2048.0)
    for k in range(6):
        ts(C("EXP", 128 * k, 128 * k + 128), C("KB", 640, 768), 8.0 * k, ALU.add, pf(0), ALU.is_equal)
    ts(C("TM", 64, 77), C("TM", 64, 77), pf(1), ALU.is_equal, pf(6), ALU.add)
    for k in range(13):
        ts(R("EK", k), GEQ, C("TM", 64 + k, 65 + k), ALU.mult)
    ts(R("SAB"), KAB, pf(0), ALU.is_equal)
    ts(C("KB", 512, 640), GEQ, pf(6), ALU.mult)
    for k in range(2):
        tt(C("SAB", 128 * k, 128 * k + 128), C("SAB", 128 * k, 128 * k + 128), C("KB", 512, 640), ALU.add)
    ms(C("SAB", 15, 256, 16), 0.0)
    lists = {}
    pos = [0]

    def mk(name, pat, base, col):
        m = 1
        for _, c in pat:
            m *= c
        a = pos[0]
        iota(C("LI", a, a + m), pat, base)
        if col is None:
            cpy(C("LF", a, a + m), C("LI", a, a + m))
        else:
            ts(C("LF", a, a + m), C("LI", a, a + m), pf(col), ALU.add)
        pos[0] += m
        lists[name] = a
    mk("r16", [[1, 40]], 0, None)
    mk("e16", [[16, 16]], 15, None)
    mk("e8", [[8, 8]], 7, None)
    mk("val", [[16, 8]], 143, 10)
    mk("oh", [[0, 4]], 0, 4)
    mk("c15", [[0, 2]], 15, 11)
    cpy(C("LU", 0, pos[0]), C("LF", 0, pos[0]))
    L = lambda name, a, b: C("LU", lists[name] + a, lists[name] + b)

    XOw, XPw, XO, XP = C("X", 0, DUM), C("X", XW, XW + DUM), C("X", 0, XW), C("X", XW, 2 * XW)

    ts(R("WF"), C("ZI", 512, 768), -2048.0, ALU.add)
    cpy(R("ZF", p=lo8), C("ZI", 0, 512, p=lo8))
    for h in range(2):
        H = str(h)
        ts(C("PW" + H, 128, 144), C("XI", 0, 16), 0.0, ALU.mult)
        mm([(C("pI" + H, 0, 128), C("WF", 128 * h, 128 * h + 128), IDF)])
        for k in range(2):
            mm([(C("pI" + H, 128 + 8 * k, 136 + 8 * k), C("ZF", 256 * k + 128 * h, 256 * k + 128 * h + 128, p=lo8), R("MF", 0, slice(0, 8), p=lo8))])
        ts(R("IX" + H), C("pI" + H, 128, 136), 0.5, ALU.mult, -0.5, ALU.add)
        ts(C("TH", 8 * h, 8 * h + 8), C("pI" + H, 136, 144), 2.0 ** -16, ALU.mult)
        tt(R("W1" + H), IN(R("IX" + H), L("r16", 0, 8)), KH, ALU.is_lt)
        act(R("W1" + H), R("W1" + H), AF.Identity, -2048.0, SENT)
        tt(C("PW" + H, 0, 128), R("W1" + H), C("pI" + H, 0, 128), ALU.max)

    def widen(k):
        bk = C("pX" + str(k % 2), 0, 464)
        mm([(bk, ID, C("CN", 464 * k, 464 * k + 464))])
        act(C("CP", 464 * k, 464 * k + 464), bk, AF.Identity, 2048.0)

    def spread(H, bank, win, off, k):
        tt(C("WX" + H, 0, 128 * k), IN(win, off), C("KF", 512, 512 + 128 * k), ALU.mult)
        for j in range(k):
            mm([(C(bank + H, 384 + 8 * j, 392 + 8 * j), C("WX" + H, 128 * j, 128 * j + 128), SM8)])
        return C(bank + H, 384, 384 + 8 * k)

    def gathers(H, win, off, blocks, onv):
        a = 0
        for k, m in enumerate(blocks):
            (cpy if k in onv else act)(C("D" + H, 16 * a, 16 * (a + m)), IN(win, C(off, a, a + m)))
            a += m

    def edges(h, rnd):
        H = str(h)
        PW = "PW" + H
        sm = lambda k: C("SM" + H, 8 * k, 8 * k + 8)
        R0 = R("R" + H, 0)
        if rnd == 0:
            mm([(C("pX" + H, 0, 128), C(PW, 0, 128), ID)])
        ts(R("LP" + H), C("pX" + H, 0, 128), pf(12), ALU.add)
        ts(R("PA" + H), R("LP" + H), pf(9), ALU.add)
        if rnd == 0:
            ts(R("PB" + H), R("LP" + H), pf(8), ALU.add)
        gathers(H, R("X"), "LP" + H, EB, EV[rnd > 0][h])
        mm([(C("pI" + H, 128, 384), R("PA" + H), R("SAB"))], True, False)
        D = C("pD" + H, 0, 128)
        parts = [[(D, ID, ICE), (C("pD" + H, 15, 128, 16), IDF, C("TH" if rnd == 0 else "THR", 8 * h, 8 * h + 8))]]
        if rnd > 0:
            mm([(C("pD" + H, 128, 256), ID, LIV)] + [(C("pD" + H, 128 + k, 256, 16), C("D" + H, k, 2048, 16), SEL8) for k in range(16)])
            scan(C("W2" + H, 128, 256), CDN, C("pD" + H, 128, 256), ALU.add, ALU.min)
            J15 = C("W2" + H, 143, 256, 16)
            act(sm(0), R("IX" + H), AF.Identity, -15.0)
            ts(sm(3), J15, 16.0, ALU.add)
            tt(sm(4), J15, sm(0), ALU.is_lt)
            ts(sm(5), J15, -1.0, ALU.mult, 1.0, ALU.add)
            tt(sm(7), J15, sm(0), ALU.is_ge)
            tt(sm(16), sm(4), sm(3), ALU.mult)
            tt(sm(17), sm(7), sm(5), ALU.mult)
            tt(C("W3" + H, 0, 256), IN(C("SM" + H, 128, 144), L("r16", 0, 16)), KLH, ALU.is_gt)
            parts.append([(D, ID, C("W3" + H, 128 * k, 128 * k + 128)) for k in range(2)])
            act(sm(6), J15, AF.Identity, 8.25, 0.5)
            ts(sm(6), sm(6), MAGIC, ALU.add, -MAGIC, ALU.add)
            act(sm(10), R("IX" + H), AF.Identity, 1.0)
            tt(sm(1), sm(10), sm(6), ALU.subtract)
            tt(sm(11), sm(3), sm(6), ALU.subtract)
            tt(sm(2), sm(1), sm(11), ALU.max)
            tt(C("TS" + H, 0, 8), sm(6), sm(4), ALU.mult)
        for c in range(4):
            a = 512 * c
            bk = C(("pX", "pE")[c % 2] + H, 0, 511)
            mm([(bk, ID, C("D" + H, a, a + 511)), (bk, NI, C("D" + H, a + 1, a + 512))])
            act(C("A" + H, a, a + 511), bk, AF.Abs)
        parts.insert(min(PENAT, len(parts)), [(C("pD" + H, k, 128, 16), C("A" + H, k, 2048, 16), SEL1) for k in range(15)])
        group(parts)
        scan(R0, RST, D, ALU.max, ALU.min)
        tt(R("NN" + H), D, R0, ALU.not_equal)
        mm([(C("pI" + H, 128 + 128 * k, 256 + 128 * k), N4, R("NN" + H)) for k in range(2)], False, True)
        for k in range(2):
            scan(C("PL" + H, 128 * k, 128 * k + 128), R("NN" + H), C("pI" + H, 128 + 128 * k, 256 + 128 * k), ALU.mult, ALU.max)
        o = spread(H, "pI", C("PL" + H, 0, 256), L("e16", 0, 16), 2)
        act(R("WB"), IN(C("PL" + H, 0, 256), L("e16", 0, 16)))
        for k in range(2):
            mm([(C("pE" + H, 128 * k, 128 * k + 128), C("WB", 128 * k, 128 * k + 128), IDF)])
        cpy(C("AS", 16 * h, 16 * h + 16), o)
        ts(C("ABU", 16 * h, 16 * h + 16), o, -1.0, ALU.add)
        cpy(C("ROW", 256 * h, 256 * h + 256), C("pE" + H, 0, 256))
        if rnd > 0:
            act(R("IX" + H), sm(2), AF.Relu, -1.0)
            ts(sm(8), sm(2), 0.5, ALU.is_lt)
            ts(sm(9), C(PW, 0, 128, 16), float(V - 97 - 2048), ALU.is_ge, -float(V), ALU.mult)
            act(sm(9), sm(9), AF.Identity, 97.0)
            tt(sm(9), sm(9), sm(8), ALU.mult)
            tt(R("OH" + H), IN(C("TS" + H, 0, 8), L("oh", 0, 3)), COH, ALU.is_equal)
            act(C("OH" + H, 40, 48), sm(2), AF.Relu, -1.0)
            lo48 = slice(0, 48)
            mm([(C("pX" + H, 0, 128, p=lo48), R("OH" + H), ID)])
            act(R("XE" + H, p=lo48), C("pX" + H, 0, 128, p=lo48))
            mm([(R("pX" + H), R("XE" + H, p=lo48), C("EXP", 0, 512, p=lo48))])
            mm([(C("pE" + H, 0, 256), R("XE" + H, p=lo48), C("EXP", 512, 768, p=lo48))])
            for t in range(5):
                tt(R("PR" + H, t), C(PW, 2 * t, 2 * t + 128), C("pX" + H, 128 * t, 128 * t + 128) if t < 4 else C("pE" + H, 0, 128), ALU.mult)
            tt(R("FL" + H), KH, C("pE" + H, 128, 256), ALU.is_gt)
            bk = C("pX" + H, 0, 128)
            mm([(bk, SI, R("FL" + H))] + [(bk, ID, R("PR" + H, t)) for t in range(5)])
            ts(C(PW, 0, 128), bk, SENT - 2048.0, ALU.min)
            tt(C(PW, 0, 128, 16), C(PW, 0, 128, 16), sm(9), ALU.add)
            mm([(C("pX" + H, 128, 256), C(PW, 0, 128), ID)])
            ts(R("PB" + H), C("pX" + H, 128, 256), pf(13), ALU.add)
        ts(C("W2" + H, 0, 64), C(PW, 0, 128, 2), SENT - 2048.0, ALU.is_lt, 8192.0, ALU.mult)
        scan(C("W2" + H, 64, 128), C("W2" + H, 0, 64), C(PW, 0, 128, 2), ALU.add, ALU.min)
        ts(R("EX" + H), spread(H, "pX", C("W2" + H, 64, 128), L("e8", 0, 8), 1), 2048.0, ALU.add)
        act(sm(12), R("IX" + H), AF.Identity, 5.0)

    def clash(h, rnd):
        H = str(h)
        r = str(rnd)
        hs = slice(128 * h, 128 * h + 128)
        act(C("XA" + H, 0, 128), IN(XOw, C("ABU", 16 * h, 16 * h + 8)))
        act(C("XA" + H, 128, 256), IN(XPw, C("ABU", 16 * h + 8, 16 * h + 16)))
        bk = C("pE" + H, 0, 128)
        mm([(bk, ID, C("XA" + H, 0, 128)), (bk, ID, C("XA" + H, 128, 256))])
        act(R("MT" + H), bk, AF.Identity, MAGIC, 0.5 - 2.0 ** -11)
        act(R("MID" + r, hs), R("MT" + H), AF.Identity, -MAGIC)
        send([(cp, R("MIN" + r, hs), R("MID" + r, hs))], 300.0)
        if h == 1:
            send([(cp, R("AP" + r), C("ABU", 16, 24))], 100.0)
        row = lambda k, a: C("ROW", 256 * h + 128 * k + a, 256 * h + 128 * k + 128)
        dm = C("KF", 1312 + 32 * h, 1344 + 32 * h)
        act(C("CS" + H, 129, 160, 2), C("AS", 16 * h, 16 * h + 16), AF.Identity, -4097.0)
        act(C("NP", 8 * h, 8 * h + 8), C("AS", 16 * h, 16 * h + 8), AF.Relu, 1.0, -1.0)
        pc_ = lambda a, b: C("pD" + H, a, b)
        parts = [[(pc_(0, 128), ID, MASK), (C("pD" + H, 0, 128, 16), BI, C("NP", 8 * h, 8 * h + 8))]]
        for m in range(8 * h + 8):
            part = []
            for k, E in enumerate(("EA", "EB")):
                sc = C("AS", 16 * (m // 8) + 8 * k + m % 8, 16 * (m // 8) + 8 * k + m % 8 + 1)
                if m // 8 < h:
                    e = R(E, m, slice(128 - 16 * m, 256 - 16 * m))
                    ts(e, row(k, 0), sc, ALU.is_equal)
                    part.append((pc_(0, 128), BO8, e))
                else:
                    a = 16 * (m % 8)
                    ts(R(E, m, slice(0, 128 - a)), row(k, a), sc, ALU.is_equal)
                    if a < 112:
                        part.append((pc_(a + 16, 128), BO8, R(E, m, slice(16, 128 - a))))
            if m % 2 == 0:
                parts.append(part)
            else:
                parts[-1] += part
        parts[-1] += [(pc_(0, 128), BOW, R(E, slice(8 * h, 8 * h + 8), slice(0, 16))) for E in ("EA", "EB")]
        group(parts)
        scan(C("CS" + H, 0, 128), VRS, pc_(0, 128), ALU.min, ALU.max)
        cpy(C("CS" + H, 128, 160, 2), IN(C("CS" + H, 0, 128), L("c15", 0, 1)))
        scan(C("LM", 32 * h, 32 * h + 32), dm, C("CS" + H, 128, 160), ALU.min, ALU.max)
        ts(C("LW" + r, 16 * h, 16 * h + 16), C("LM", 32 * h + 1, 32 * h + 32, 2), 4096.0, ALU.add)
        ends = [(cp, C("LA" + r, 8 * h, 8 * h + 8), C("LW" + r, 16 * h, 16 * h + 8)),
                (cq, C("LB" + r, 8 * h, 8 * h + 8), C("LW" + r, 16 * h + 8, 16 * h + 16))]
        if h == 0:
            send(ends, 200.0)
        else:
            send(ends[:1], 100.0)
            send(ends[1:], 100.0)

    def merge(rnd):
        r = str(rnd)
        cpy(IN(XP, C("LA" + r, 0, 8)), C("MIN" + r, 0, 128))
        for h in range(2):
            cpy(IN(XO, C("LW" + r, 16 * h, 16 * h + 8)), C("MID" + r, 128 * h, 128 * h + 128))
            act(IN(XP, C("LW" + r, 16 * h + 8, 16 * h + 16)), C("DK", 128, 256), AF.Silu)
        act(R("ZZ"), IN(XPw, R("AP" + r)), AF.Relu, -320.0, 1.25)
        tt(IN(XP, C("LA" + r, 8, 16)), C("MIN" + r, 128, 256), R("ZZ"), ALU.max)
        for h in range(2):
            act(IN(XO, C("LB" + r, 8 * h, 8 * h + 8)), C("DK", 0, 128), AF.Silu)
        if rnd < 2:
            act(C("CT", 8, 40), C("LM", 1, 64, 2), AF.Sign, DUM - 4096.5, -1.0, C("CT", 0, 1))
            mm([(C("pE1", 256, 257), ONE, C("CT", 0, 1))])
            ts(C("CTI", 0, 1), C("pE1", 256, 257), 0.25, ALU.mult, 1024.0, ALU.add)
            ts(C("CTI", 1, 2), C("CTI", 0, 1), 31, ALU.bitwise_and)
            ts(C("CT", 1, 2), C("CTI", 1, 2), 2.0 ** -13, ALU.mult)
            act(R("THR"), R("TH"), AF.Identity, C("CT", 1, 2))

    def hop(h, j):
        H = str(h)
        cw, xe, xc = (R("CI"), XOw, XPw) if j % 2 == 0 else (R("CP"), XPw, XOw)
        b0, nb = ((0, 6), (6, 7))[j % 2]
        cpy(R("OF" + H), IN(cw, R("EX" + H)))
        ts(R("C16" + H), R("OF" + H), -2048.0, ALU.add)
        if j == 0 and h in XEV:
            ts(R("XE" + H), IN(xe, R("EX" + H)), 255.0, ALU.min)
        else:
            act(R("XE" + H), IN(xe, R("EX" + H)))
            if j == 0:
                ts(R("XE" + H), R("XE" + H), 255.0, ALU.min)
        gathers(H, xc, "OF" + H, HB, HV[h][j])
        IC = C("pI" + H, 0, 128)
        mm([(IC, R("C16" + H), ID)])
        if CWE == "S":
            act(R("CW" + H), IC, AF.Identity, 2048.0)
        else:
            ts(R("CW" + H), IC, 2048.0, ALU.add)
        mm([(C("pX" + H, d, 512, 4), ID, R("XE" + H)) for d in range(4)])
        for a, e, bank, c0 in ((0, nb - 3, "pE", 0), (nb - 3, 3, "pI", 128)):
            mm([(C(bank + H, c0, c0 + 128 * e), R("PB" + H), R("EK", slice(b0 + a, b0 + a + e)))])
            for k in range(e):
                tt(R("EQ" + H, a + k), R("CW" + H), C(bank + H, c0 + 128 * k, c0 + 128 * k + 128), ALU.is_equal)
        mm([(IC, ID, K2), (IC, R("C16" + H), ID)], True, False)
        ns = SH[h][j]
        fix = []
        if ns:
            mm([(C("pE" + H, 0, 8 * ns), ID, C("D" + H, 0, 16 * ns, 2))] + [(C("pE" + H, d, 8 * ns, 8), NI, C("XE" + H, 0, ns)) for d in range(8)])
            act(C("A" + H, 0, 16 * ns, 2), C("pE" + H, 0, 8 * ns), AF.Relu)
            fix = [(C("pD" + H, 0, 128, 2, p=slice(0, ns)), C("XE" + H, 0, ns), R("MB", 10, slice(0, 128, 2)))]
        a = 0
        for m in HB:
            for q in range(4):
                if a + m > ns or q % 2:
                    tt(C("A" + H, 16 * a + q, 16 * (a + m), 4), C("D" + H, 16 * a + q, 16 * (a + m), 4), C("pX" + H, 4 * a, 4 * (a + m)), ALU.max)
            a += m
        D = C("pD" + H, 0, 128)
        col = lambda i: C("pD" + H, i, 128, 16)
        pen = [(D, PEN, R("EQ" + H, k)) for k in range(nb)]
        group([[(D, ID, ICON)] + fix + pen[:nb - 3], pen[nb - 3:]] +
              [[(col(i), C("D" + H, i, 2048, 16), SELN) for i in range(q, 16, RAWP)] for q in range(RAWP)] +
              [[(col(i), C("A" + H, i, 2048, 16), SEL2) for i in range(q, 16, 4)] for q in range(4)])
        scan(R("R" + H, j), RST, D, ALU.max, ALU.min)
        tt(R("NN" + H), D, R("R" + H, j), ALU.not_equal)
        mm([(IC, N4, R("NN" + H))], False, True)
        pl = C("PL" + H, 128 * j, 128 * j + 128)
        scan(pl, R("NN" + H), IC, ALU.mult, ALU.max)
        if j < 3:
            cpy(R("EX" + H), spread(H, "pI", pl, L("e16", 0, 8), 1))

    def append(h, q, rnd):
        H = str(h)
        PW = C("PW" + H, 0, 128)
        sm = lambda k: C("SM" + H, 8 * k, 8 * k + 8)
        val = IN(C("PL" + H, 256 * q, 256 * q + 256), L("val", 0, 8))
        cap = C("KF", 960 + 128 * q, 1088 + 128 * q)
        bk = C("pX" + H, 0, 128)
        if q == 0:
            ts(R("FD" + H), R("R" + H, slice(0, 2), slice(15, 128, 16)), 0.125, ALU.is_lt)
            tt(sm(13), R("FD" + H, 0), R("FD" + H, 1), ALU.mult)
            tt(sm(15), sm(13), sm(12), ALU.mult)
            tt(R("FL" + H), IN(sm(15), L("r16", 0, 8)), cap, ALU.not_equal)
            act(R("W1" + H), val, AF.Identity, -2048.0)
            bk = C("pE" + H, 128, 256)
            mm([(bk, SI, R("FL" + H)), (bk, IDF, R("W1" + H))])
            tt(PW, PW, bk, ALU.min)
            mm([(C("pE" + H, 0, 128), PW, ID)])
            ts(R("PB" + H), C("pE" + H, 0, 128), pf(13), ALU.add)
            tt(R("IX" + H), R("IX" + H), sm(13), ALU.add)
            return
        for k in range(2):
            ts(R("FD" + H, k), R("R" + H, 2 + k, slice(15, 128, 16)), 0.125, ALU.is_lt)
        tt(sm(14), R("FD" + H, 0), sm(15), ALU.mult)
        tt(sm(14), R("FD" + H, 1), sm(14), ALU.mult)
        if rnd == 2 or h in FAST:
            tt(R("FL" + H), IN(sm(14), L("r16", 0, 8)), cap, ALU.is_equal)
            tt(R("W1" + H), val, R("FL" + H), ALU.mult)
        if rnd < 2 and h not in FAST:
            tt(R("FL" + H), IN(sm(14), L("r16", 0, 8)), cap, ALU.not_equal)
            act(R("W1" + H), val, AF.Identity, -2048.0)
            mm([(bk, SI, R("FL" + H)), (bk, IDF, R("W1" + H))])
            tt(PW, PW, bk, ALU.min)
            mm([(bk, PW, ID)])
        elif rnd < 2:
            group([[(bk, PW, ID)], [(bk, R("FL" + H), NS)], [(bk, R("W1" + H), IDF)]])
            pe = C("pE" + H, 0, 128)
            mm([(pe, ID, PW), (pe, NS, R("FL" + H)), (pe, IDF, R("W1" + H))])
            cpy(PW, pe)
        else:
            ts(C("W3" + H, 0, 128), PW, SENT - 2048.0, ALU.is_ge)
            group([[(bk, PW, ID), (bk, C("W3" + H, 0, 128), NS)], [(bk, R("W1" + H), IDF)]])
        ts(sm(14), sm(14), 1.0, ALU.min)
        tt(R("IX" + H), R("IX" + H), sm(14), ALU.add)
        ts(R("IX" + H), R("IX" + H), 7.0, ALU.min)

    for rnd in range(3):
        for h in range(2):
            cur[0] = BIASE * (1 - h)
            edges(h, rnd)
        cur[0] = 0.0
        if rnd == 0:
            for k in range(8):
                widen(k)
        for h in range(2):
            clash(h, rnd)
        merge(rnd)
        if rnd == 2:
            for k in range(2):
                c = C("XB", 1856 * k, 1856 * (k + 1))
                x = C("X", 1856 * k, 1856 * (k + 1))
                dma("G", c["ap"], x["ap"], [c], [x], 5000.0)
                for a in range(1856 * k, 1856 * (k + 1), 464):
                    ts(C("XB", a, a + 464), C("XB", a, a + 464), 255.0, ALU.min)
                dma("Y", T.yx[:, 1856 * k:1856 * (k + 1)], c["ap"], [], [c], 6000.0)
        for h in range(2):
            cur[0] = BIAS * (1 - h)
            for j in range(4):
                hop(h, j)
                if j % 2 == 1:
                    append(h, j // 2, rnd)
    for h in range(2):
        cur[0] = BIAS * (1 - h)
        H = str(h)
        hs = slice(128 * h, 128 * h + 128)
        ts(C("OH" + H, 0, 8), R("IX" + H), 2.0, ALU.mult, 1.0, ALU.add)
        mm([(C("pE" + H, 0, 128, p=lo8), C("OH" + H, 0, 8), ID)])
        act(R("YC", hs), C("pX" + H, 0, 128), AF.Identity, 2048.0)
        cpy(R("YN", hs, p=lo8), C("pE" + H, 0, 128, p=lo8))
        dma("S", T.yw[:, hs], T.YC[:, hs], [], [R("YC", hs)], 2200.0)
        dma("Y", T.yn[:, hs], T.YN[0:8, hs], [], [R("YN", hs)], 2000.0)
    return ops


def order(ops):
    n = len(ops)
    hist = {}
    bank = {}
    pred = []
    for k, o in enumerate(ops):
        p = set(o["after"] + o["soft"])
        for w, regs in ((False, o["rd"]), (True, o["wr"])):
            for name, bits in regs:
                if SCRATCH[name][0] == "psum":
                    ph = bank.setdefault(name, [o["eng"], [], []])
                    if ph[0] != o["eng"]:
                        ph[:] = [o["eng"], [], ph[1]]
                        hist[name] = []
                    p.update(ph[2])
                    ph[1].append(k)
                for (j, w2, b2) in hist.get(name, []):
                    if j != k and (w or w2) and bits & b2:
                        p.add(j)
        for w, regs in ((False, o["rd"]), (True, o["wr"])):
            for name, bits in regs:
                hs = hist.setdefault(name, [])
                if w:
                    hs[:] = [x for x in hs if x[2] & ~bits]
                hs.append((k, w, bits))
        pred.append(sorted(p))
    succ = [[] for _ in range(n)]
    for k in range(n):
        for j in pred[k]:
            succ[j].append(k)
    lev = [0.0] * n
    for k in range(n - 1, -1, -1):
        lev[k] = ops[k]["cost"] + ops[k]["lat"] + max([lev[j] + LAT for j in succ[k]] + [0.0])
    x = SEED
    for k in range(n):
        x = (x * 1103515245 + 12345) % 2147483648
        lev[k] += ops[k]["bias"] + NOISE * x / 2147483648.0
    left = [len(p) for p in pred]
    rdy = {k: 0.0 for k in range(n) if left[k] == 0}
    free = {}
    fin = [0.0] * n
    seq = []
    while rdy:
        best = min(rdy, key=lambda k: max(rdy[k], free.get(ops[k]["eng"], 0.0)))
        e = ops[best]["eng"]
        t0 = max(rdy[best], free.get(e, 0.0))
        k = max([j for j in rdy if ops[j]["eng"] == e and rdy[j] <= t0 + WIN], key=lambda j: lev[j])
        s = max(rdy.pop(k), free.get(e, 0.0))
        free[e] = s + ops[k]["cost"]
        fin[k] = free[e] + ops[k]["lat"]
        seq.append(k)
        for j in succ[k]:
            left[j] -= 1
            if left[j] == 0:
                rdy[j] = max(fin[i] + LAT for i in pred[j])

    def gap(j, k):
        return 0.0 if ops[j]["eng"] == "P" and ops[k]["eng"] == "P" or j in ops[k]["soft"] else ops[j]["lat"] + LAT

    def place(lst, back):
        busy = {e: ([], []) for e in set(eng)}
        end = [0.0] * n
        near = after if back else before
        for k in lst:
            c = cost0[k]
            s = ops[k]["lat"] if back else 0.0
            for j, d in near[k]:
                if end[j] + d > s:
                    s = end[j] + d
            b0, b1 = busy[eng[k]]
            lo = m = len(b0)
            while lo and b1[lo - 1] > s:
                lo -= 1
            while lo < m and b0[lo] < s + c:
                if b1[lo] > s:
                    s = b1[lo]
                lo += 1
            b0.insert(lo, s)
            b1.insert(lo, s + c)
            end[k] = s + c
        return end
    eng = [o["eng"] for o in ops]
    cost0 = [max(o["cost"], 1.0) for o in ops]
    before = [[(j, gap(j, k)) for j in pred[k]] for k in range(n)]
    after = [[(j, gap(k, j)) for j in succ[k]] for k in range(n)]
    end = place(seq, False)
    best = None
    for _ in range(PASSES):
        span = max(end[k] + ops[k]["lat"] for k in range(n))
        if best is None or span < best[0]:
            best = (span, end)
        end = place(sorted(range(n), key=lambda k: (-end[k], -k)), True)
        end = place(sorted(range(n), key=lambda k: (-end[k], k)), False)
    cases = []
    for dg, ds, pe, lat in CASES:
        cases.append(([(o["cost"] + dg * o["ge"] + ds * o["se"]) * (pe if o["eng"] == "P" else 1.0) for o in ops],
                      [[(j, gap(j, k) and ops[j]["lat"] + lat) for j in pred[k]] for k in range(n)]))

    def judge(end):
        start = [end[k] - cost0[k] for k in range(n)]
        lst = sorted(range(n), key=lambda k: start[k])
        total = 0.0
        for cost, gaps in cases:
            free, fin = dict.fromkeys(eng, 0.0), [0.0] * n
            for k in lst:
                s = free[eng[k]]
                for j, d in gaps[k]:
                    if fin[j] + d > s:
                        s = fin[j] + d
                free[eng[k]] = fin[k] = s + cost[k]
            total += max(fin[k] + ops[k]["lat"] for k in last)
        return total / len(cases)
    last = [k for k in range(n) if not succ[k]]
    best = (judge(best[1]), best[1])
    for it in range(SHAKES):
        key = list(best[1])
        x = (x * 1103515245 + 12345) % 2147483648
        t0 = max(key) * x / 2147483648.0
        for k in range(n):
            if t0 - SPAN < key[k] < t0 + SPAN:
                x = (x * 1103515245 + 12345) % 2147483648
                key[k] += SHAKE * x / 2147483648.0
            if t0 - SPAN < key[k] < t0 + SPAN + 3 * SHAKE:
                for j in pred[k]:
                    if key[j] >= key[k]:
                        key[k] = key[j] + 0.01
        end = place(sorted(range(n), key=lambda k: -key[k]), True)
        end = place(sorted(range(n), key=lambda k: -end[k]), False)
        span = judge(end)
        if span < best[0] + SLACK:
            best = (span, end)
    end = best[1]
    seq = sorted(range(n), key=lambda k: (end[k] - max(ops[k]["cost"], 1.0), k))
    return pred, seq, [end[k] + ops[k]["lat"] for k in range(n)]


def rank_program(g, core, T, topo):
    if T.rank_of(core) is None:
        hand_on(g, core, T, topo)
        return
    ops = build(g, core, T, topo)
    if not PLAN:
        PLAN.append(order(ops))
    pred, seq, fin = PLAN[0]
    Q = {"V": g.vector, "S": g.scalar, "P": g.tensor, "G": g, "Y": g.sync}
    tok = {}
    know = {}
    at = {k: i for i, k in enumerate(seq)}
    count = {}
    seen = {e: {} for e in Q}
    for k in seq:
        o = ops[k]
        e = o["eng"]
        if e in "XZ":
            tok[k] = o["sem"][:2]
            count[tok[k][0]] = tok[k][1]
            continue
        need = {}
        for j in pred[k]:
            if e == "P" and ops[j]["eng"] == "P" or j in o["soft"]:
                continue
            s, v = tok[j]
            if need.get(s, (0, 0))[0] < v:
                need[s] = (v, j)
        for s, (v, j) in sorted(need.items(), key=lambda y: -at[y[1][1]]):
            if seen[e].get(s, 0) < v:
                Q[e].wait_ge(T.sem[s], v)
                seen[e][s] = v
                for s2, v2 in know.get(j, {}).items():
                    if seen[e].get(s2, 0) < v2:
                        seen[e][s2] = v2
        know[k] = dict(seen[e])
        ins = o["fn"](Q[e])
        if o["sem"] is None:
            s = "c" + e
            count[s] = count.get(s, 0) + 1
            ins.then_inc(T.sem[s], 1)
            tok[k] = (s, count[s])
        else:
            tok[k] = o["sem"][:2]
            count[tok[k][0]] = tok[k][1]
            if o["sem"][2]:
                ins.then_inc(T.sem[tok[k][0]], 16)
    for s, v in count.items():
        if seen["G"].get(s, 0) < v:
            g.wait_ge(T.sem[s], v)
